import numpy as np, ml_dtypes
CORES = [48,51,52,55]
N = 4
BF = ml_dtypes.bfloat16
def gentries(a):
    return np.ascontiguousarray(a.reshape(8, 16, -1).transpose(0, 2, 1)).reshape(8, -1)
def gtable(e):
    e = np.asarray(e); return np.ascontiguousarray(e.reshape(8, -1, 16).transpose(0, 2, 1)).reshape(128, -1).astype(np.int32)
W, L, M, B, TS, CAP = 8192, 256, 4, 4, 4, 128
R = M * B
KAPPA = (3, 29, 71, 113)
def run(x, z, v):
    tr = []
    for b in range(B):
        u = np.add.reduce(z, axis=2)
        c = np.concatenate([((u * u >> 4) + k * u + v) & (W - 1) for k in KAPPA], axis=2)
        y = np.take_along_axis(x, c[:, :, None, :], 3).reshape(N, 8, 16, M, L)
        z = np.abs(np.maximum.reduce(y, axis=3) - z)
        tr.append(c)
    return z, np.concatenate(tr, axis=2)
def starts(z, h, fr):
    halt = (~fr) & (np.add.reduce((z >= h[..., None]).astype(np.int64), axis=2) >= 9)
    slot = np.add.accumulate(halt.astype(np.int64), axis=2) - halt
    return halt & (slot < CAP)
def parts(rng):
    return rng.integers(0, 256, (N, 8, 16, W)), rng.integers(0, 256, (N, 8, 16, L)), rng.integers(0, W, (N, 8, L))
def levels(rng, x, s, v, share):
    j = rng.integers(-24, 25, (N, 8, 16, TS)); z = run(x, s, v)[0]; th = np.zeros((N, 8, 16, TS), np.int64)
    for t in range(TS):
        k = np.sort(np.sort(z - j[..., t:t + 1], axis=2)[:, :, 7], axis=2)
        n = np.minimum(np.maximum((share[..., t] * L).astype(np.int64), 1), L)
        th[..., t] = np.take_along_axis(k, (L - n)[..., None], 2) + j[..., t]
    return np.minimum(np.maximum(th, 0), 255)
def pack(x, s, v, th):
    return {"x": x.reshape(N, 128, W).astype(np.float32).astype(BF), "sd": s.reshape(N, 128, L).astype(np.float32).astype(BF),
            "v0": np.stack([gtable(a) for a in v]), "th": np.ascontiguousarray(th.reshape(N, 128, TS)).astype(np.int32)}
def shares(rng):
    return rng.choice(np.array([0.1, 0.25, 0.4, 0.6]), (N, 8, TS))
def setup_inputs(rng):
    x, s, v = parts(rng)
    return pack(x, s, v, levels(rng, x, s, v, shares(rng)))
def setup_inputs_claims(rng):
    x, s, v = parts(rng); share = rng.choice(np.array([0.2, 0.35, 0.45]), (N, 8, TS)); th = levels(rng, x, s, v, share)
    z, c = run(x, s, v); go = starts(z, th[..., 0], np.zeros((N, 8, L), bool))
    for r in range(0, N, 2):
        for g in range(8):
            j = np.nonzero(go[r + 1, g])[0]
            if len(j) == 0: j = np.arange(L)
            e = rng.choice(np.array([0, R - 1, -1]), L); e = np.where(e < 0, rng.integers(0, R, L), e)
            v[r, g] = np.where(rng.random(L) < 0.6, c[r + 1, g, e * L + rng.choice(j, L)], v[r, g])
    th[0::2] = levels(rng, x, s, v, share)[0::2]
    th[1, :, :, 1] = 255; th[:, 5, :, 2] = 255; th[2, :, :, TS - 1] = 255
    return pack(x, s, v, th)
def setup_inputs_corners(rng):
    x, s, v = parts(rng); v = np.ascontiguousarray(np.argsort(rng.random((N, 8, W)), axis=-1)[..., :L])
    pm = np.ones((N, 8), bool); pm[2:, 6:] = False
    x = np.where(pm[:, :, None, None], 255, x)
    n = rng.choice(np.array([0, 1, CAP - 1, CAP, CAP + 1, L]), (N, 8)); n[0] = 0
    n[1] = np.array([CAP, CAP + 1, L, CAP, L, CAP + 1, CAP, L]); n[2] = np.array([CAP, CAP + 1, L, CAP - 1, 1, 0, CAP, CAP])
    hot = np.argsort(np.argsort(rng.random((N, 8, L)), axis=2), axis=2) < n[:, :, None]
    k = np.where(hot, np.where(rng.random((N, 8, L)) < 0.5, 9, rng.integers(9, 17, (N, 8, L))), np.where(rng.random((N, 8, L)) < 0.5, 8, rng.integers(0, 9, (N, 8, L))))
    up = np.argsort(np.argsort(rng.random((N, 8, 16, L)), axis=2), axis=2) < k[:, :, None, :]
    tb = rng.integers(1, 256, (N, 8, 16)); tb[:, 1] = 1; tb[:, 3] = 255; tb[:, 5] = rng.choice(np.array([1, 255]), (N, 16))
    b = tb[..., None]; near = rng.random(s.shape) < 0.5
    hi = np.where(near, b, b + ((256 - b) * rng.random(s.shape)).astype(np.int64)); lo = np.where(near, b - 1, (b * rng.random(s.shape)).astype(np.int64))
    s = np.where(pm[:, :, None, None], np.where(up, hi, lo), s)
    th = levels(rng, x, s, v, shares(rng)); th[..., 0] = np.where(pm[:, :, None], tb, th[..., 0])
    return pack(x, s, v, th)
def setup_inputs_ends(rng):
    x, s, v = parts(rng); one = 1.0
    for i in range(M.bit_length() - 1): one = one * 0.5
    a = rng.random((N, 8, 1, W)); x = np.where(a < 0.4 * one, 255, np.where(a < 1.2 * one, 255 * rng.integers(0, 2, x.shape), 0))
    a = rng.random((N, 8, 1, L)); s = np.where(a < 0.35, 255, np.where(a < 0.6, 0, 255 * rng.integers(0, 2, s.shape)))
    v = np.where(rng.random(v.shape) < 0.72, (W - 1) * rng.integers(0, 2, v.shape), v)
    x[:, 1::2, :, W - 1] = 255; x[:, 0::2, :, W - 1] = 0; x[:, :, :, 0] = 255 - x[:, :, :, W - 1]
    s[:, 1::2, :, L - 1] = 255; s[:, 0::2, :, L - 1] = 0; s[:, :, :, 0] = 255 - s[:, :, :, L - 1]; s[:, 1::2, :, 5] = 255; s[:, 1::2, :, L - 4] = 255
    v[:, :, L - 1] = W - 1; v[:, :, L - 4] = W - 1; v[:, :, 5] = W - 1; v[:, :, 0] = 0
    k = rng.choice(np.array([16, 16, 12, 10, 9, 8, 8, 7, 0]), (N, 8, 1, TS)); k[:, 7, :, 0] = 12; k[:, 6, :, 0] = 0; k[:, 0, :, TS - 1] = 9; k[:, 7, :, TS - 1] = 16
    th = np.where(np.argsort(np.argsort(rng.random((N, 8, 16, TS)), axis=2), axis=2) < k, 255, 0)
    return pack(x, s, v, th)
def setup_inputs_spread(rng):
    x, s, v = parts(rng)
    x = np.minimum((np.exp2(1 + 7 * rng.random((N, 8, 1, W))) * rng.random(x.shape)).astype(np.int64), 255)
    s = np.minimum((np.exp2(1 + 7 * rng.random((N, 8, 1, L))) * rng.random(s.shape)).astype(np.int64), 255)
    v = np.minimum((W * rng.random(v.shape) ** 3).astype(np.int64), W - 1)
    return pack(x, s, v, levels(rng, x, s, v, shares(rng)))
def setup_inputs_ties(rng):
    x, s, v = parts(rng); pool = rng.integers(0, W, (8, 12)); pool[:, 0] = 0; pool[:, 1] = W - 1; h = L // 2; q = L // 4
    v = np.stack([pool[g][rng.integers(0, 12, (N, L))] for g in range(8)], axis=1)
    s[..., h:] = s[..., :h]; v[..., h:] = np.where(rng.random((N, 8, h)) < 0.5, v[..., :h], v[..., h:])
    pl = [2, 4, 7]; x[:, 2] = 255; x[:, 4] = 0; x[:, 7] = 0
    s[:, pl] = rng.integers(0, 100, (N, 3, 16, L))
    for a in range(0, N, 2):
        b = a + 1
        k = int(rng.integers(1, 4)); p = int(v[b, 2, 0])
        s[b, 2, :, k * q:(k + 1) * q] = 255; v[b, 2, k * q:(k + 1) * q] = p
        s[a, 2, :, (k - 1) * q:k * q] = rng.integers(201, 256, (16, q))
        v[a, 2, (k - 1) * q:k * q] = np.where(rng.random(q) < 0.8, p, v[a, 2, (k - 1) * q:k * q]); v[a, 2, (k - 1) * q] = p
        ln = np.append(q + rng.permutation(3 * q - 1)[:3], L - 1); e = rng.integers(201, 252, 4); pv = 16 * rng.permutation(W // 16)[:4] + 1; u = 16 * e
        s[b, 4][:, ln] = e; v[b, 4][ln] = pv
        wr = rng.permutation(q)[:4 * M]; s[a, 4][:, wr] = rng.integers(201, 252, 4 * M); s[a, 4][5, wr] += 4
        v[a, 4][wr] = np.concatenate([((u * u >> 4) + m * u + pv) & (W - 1) for m in KAPPA])
        p = W - 2 if a == 0 else int(rng.integers(W // 2, W - 1))
        for l, c in ((0, p + 1), (h, p)):
            s[b, 7, :, l] = rng.integers(201, 256, 16); u = int(np.sum(s[b, 7, :, l])); v[b, 7, l] = (c - (u * u >> 4) - KAPPA[0] * u) & (W - 1)
        for l, c in ((3, p + 1), (L - 1, p)):
            s[a, 7, :, l] = rng.integers(201, 256, 16); v[a, 7, l] = c
    th = levels(rng, x, s, v, shares(rng)); th[..., 0][:, pl] = rng.integers(100, 201, (N, 3, 16))
    return pack(x, s, v, th)
def check_inputs(d):
    bad = []
    for k, lo, hi in (("x", 0, 255), ("sd", 0, 255), ("v0", 0, W - 1), ("th", 0, 255)):
        a = np.asarray(d[k]).astype(np.float64)
        if not (np.min(a) >= lo and np.max(a) <= hi): bad.append("range of " + k)
        elif np.any(np.floor(a) != a): bad.append("whole numbers in " + k)
    return bad
def reference(x, sd, v0, th):
    X = x.astype(np.float32).astype(np.int64).reshape(N, 8, 16, W); S = sd.astype(np.float32).astype(np.int64).reshape(N, 8, 16, L)
    H = th.astype(np.int64).reshape(N, 8, 16, TS); v = np.stack([gentries(a) for a in v0]).astype(np.int64)
    fr = np.zeros((N, 8, L), bool); tr = np.zeros((N, 8, R * L), np.int64); cl = np.arange(L) * 4 // L
    for t in range(TS):
        z, c = run(X, S, v)
        tr = np.where(np.tile(fr, (1, 1, R)), tr, c)
        go = starts(z, H[..., t], fr); fr = fr | go
        back = np.zeros((N, 8, L), bool); hurt = np.zeros((N, 8, L), bool); done = np.zeros((N, 1, 1), np.int64)
        for q in range(N):
            p = q ^ (1 + t % (N - 1))
            for g in range(8):
                ln = np.nonzero(go[p, g])[0]; w = v[p, g, ln]
                mark = np.full(W, 9); np.minimum.at(mark, tr[q, g], np.where(np.tile(fr[q, g], R), np.tile(cl, R), 9))
                ok = np.nonzero(mark[w] > cl[ln])[0]
                win = np.zeros(len(ln), bool); win[ok[np.unique(w[ok], return_index=True)[1]]] = True
                back[p, g, ln[~win]] = True; done[q, 0, 0] += np.count_nonzero(win)
                if t < TS - 1: X[q, g][:, w[win]] = z[p, g][:, ln[win]]
                hit = np.zeros(W, bool); hit[w[win]] = True
                hurt[q, g] = fr[q, g] & np.any(hit[tr[q, g]].reshape(R, L), axis=0)
        fr = fr & (~back) & (~hurt)
        v = np.where(fr, v, (((v & 4095) ** 2 >> 3) + 37 * v + done) & (W - 1))
    ys = np.concatenate([v, fr.astype(np.int64)], axis=2)
    return {"yt": np.stack([gtable(a) for a in tr]).astype(np.float32), "ys": np.stack([gtable(a) for a in ys]).astype(np.float32)}

@@ -1,0 +1,595 @@
+from concourse.mybir import AluOpType as Op, AxisListType, ActivationFunctionType as AF
+
+W, L, D = 8192, 256, 8448
+KAPPA = (3, 29, 71, 113)
+TS, CAP = 4, 128
+FL = "GO THR DS L1 L2 LF IW LD E1 E2 FR FS VF BA S4 S5 S6".split()
+IL = "VN VC S1 S2 S3 S7".split()
+CM = "ID NI N5 BO TG ON BK TK".split()
+
+SCRATCH = {
+    "X": ("sbuf", [128, 8448], "bfloat16"),
+    "QA": ("sbuf", [128, 8464], "bfloat16"), "QB": ("sbuf", [128, 8464], "bfloat16"), "HT": ("sbuf", [128, 8464], "bfloat16"),
+    "OW": ("sbuf", [128, 1024], "bfloat16"),
+    "IO": ("sbuf", [128, 8192], "float32"),
+    "SD": ("sbuf", [128, 256], "bfloat16"), "V0": ("sbuf", [128, 16], "int32"), "TI": ("sbuf", [128, 4], "int32"), "TF": ("sbuf", [128, 4], "float32"),
+    "PI": ("sbuf", [128, 4], "int32"), "PF": ("sbuf", [128, 4], "float32"),
+    "RM": ("sbuf", [128, 256], "float32"), "RD": ("sbuf", [128, 256], "float32"), "RP": ("sbuf", [128, 128], "float32"), "RG": ("sbuf", [128, 128], "float32"),
+    "K1": ("sbuf", [128, 256], "float32"), "K2": ("sbuf", [128, 256], "float32"), "K3": ("sbuf", [128, 256], "float32"), "K4": ("sbuf", [128, 256], "float32"),
+    "CM": ("sbuf", [128, 128 * len(CM)], "bfloat16"), "FL": ("sbuf", [128, 16 * len(FL)], "float32"), "IL": ("sbuf", [128, 16 * len(IL)], "int32"),
+    "KA": ("sbuf", [128, 256], "float32"), "KC": ("sbuf", [128, 256], "float32"), "NK": ("sbuf", [128, 256], "bfloat16"),
+    "NM": ("sbuf", [128, 256], "bfloat16"), "CO": ("sbuf", [128, 256], "bfloat16"), "D0": ("sbuf", [128, 256], "float32"),
+    "TH": ("sbuf", [128, 128], "float32"), "WH": ("sbuf", [128, 2], "float32"), "DM": ("sbuf", [128, 16], "float32"),
+    "OB": ("sbuf", [128, 256], "bfloat16"), "ZB": ("sbuf", [128, 529], "bfloat16"),
+    "TN": ("sbuf", [128, 256], "int32"), "TR": ("sbuf", [128, 256], "float32"), "P1": ("sbuf", [128, 256], "float32"),
+    "P2": ("sbuf", [128, 256], "float32"), "M1": ("sbuf", [128, 256], "float32"), "M2": ("sbuf", [128, 256], "float32"),
+    "OM": ("sbuf", [128, 256], "uint16"), "NG": ("sbuf", [128, 256], "bfloat16"), "NF": ("sbuf", [128, 256], "bfloat16"), "FO": ("sbuf", [128, 256], "bfloat16"),
+    "OV": ("sbuf", [128, 16], "uint16"), "DV": ("sbuf", [128, 256], "uint16"), "OD": ("sbuf", [128, 16], "uint16"),
+    "HA": ("sbuf", [128, 16], "bfloat16"), "SC": ("sbuf", [128, 18], "bfloat16"),
+    "EB": ("sbuf", [128, 16, 256], "bfloat16"), "DUL": ("sbuf", [128, 256], "float32"), "HUL": ("sbuf", [128, 256], "float32"),
+    "MC": ("sbuf", [128, 128], "bfloat16"), "MD": ("sbuf", [128, 64], "bfloat16"), "ME": ("sbuf", [128, 32], "bfloat16"), "MF": ("sbuf", [128, 16], "bfloat16"),
+    "AA": ("sbuf", [128, 1], "float32"), "YT": ("sbuf", [128, 16, 16], "float32"), "YS": ("sbuf", [128, 32], "float32"),
+    "GB": ("sbuf", [128, 4096], "bfloat16"), "HB": ("sbuf", [128, 2048], "bfloat16"), "LA": ("sbuf", [128, 2048], "bfloat16"), "LB": ("sbuf", [128, 2048], "bfloat16"),
+    "pU0": ("psum", [128, 512], "float32"), "pU1": ("psum", [128, 512], "float32"), "pD0": ("psum", [128, 512], "float32"), "pD1": ("psum", [128, 512], "float32"),
+    "pT0": ("psum", [128, 1024], "bfloat16"), "pT1": ("psum", [128, 1024], "bfloat16"), "pC": ("psum", [128, 512], "float32"), "pH": ("psum", [128, 512], "float32"),
+}
+SCRATCH.update({"Z": ("sbuf", [128, 256], "bfloat16"), "Y": ("sbuf", [128, 1024], "bfloat16"), "F": ("sbuf", [128, 256], "bfloat16"),
+                "UL": ("sbuf", [128, 256], "float32"), "SQ": ("sbuf", [128, 64], "float32"), "SZ": ("sbuf", [128, 64], "float32"), "XQ": ("sbuf", [128, 32], "float32"),
+                "XI": ("sbuf", [128, 64], "int32"), "OF": ("sbuf", [128, 64], "uint16"), "VK": ("sbuf", [128, 64], "float32")})
+for _t in range(TS):
+    SCRATCH.update({"ZF%d" % _t: ("sbuf", [128, 256], "bfloat16"), "ZP%d" % _t: ("sbuf", [128, 256], "bfloat16"), "LQ%d" % _t: ("sbuf", [128, 16], "uint16"),
+                    "RL%d" % _t: ("sbuf", [128, 16], "uint16"), "DO%d" % _t: ("sbuf", [128, 16], "bfloat16"), "DR%d" % _t: ("sbuf", [128, 16], "bfloat16")})
+SEMAPHORES = ["cV", "cS", "cP", "cG", "dx", "dv", "ds", "dt", "dy", "dz", "loc"] + ["r%s%d" % (k, t) for k in "LZD" for t in range(TS)]
+CYC, WAKE, SFIX, LOOK, PUT, REMOTE = 0.00083, 0.15, 0.15, 1.3, 3.0, 3.0
+MARGIN, AHEAD = 2, 0.0
+STIR, SEED = 0.0, 0
+ORDER = []
+SFIRST = (1,)
+GAP = {"S": 0.3, "V": 0.9}
+POS = (0, 256, 128, 384)
+HITS_ON_VECTOR = (4, 9, 14)
+
+
+def rank_program(g, core, T, topo):
+    rank = T.rank_of(core)
+    if rank is None:
+        return
+    eng = {"V": g.vector, "S": g.scalar, "P": g.tensor, "G": g, "Y": g.sync}
+    ops = []
+    boost = [0.0]
+    chain = [None]
+
+    def op(q, reads, writes, cost, f, kind="c", sem=None, n=0, lat=0.0):
+        ops.append({"chain": chain[0], "first": boost[0], "q": q, "r": reads.split(), "w": writes.split(), "cost": cost, "f": f, "kind": kind, "sem": sem, "n": n, "lat": lat})
+
+    def dma(q, sem, total, out, in_, reads, writes):
+        op(q, reads, writes, 0.1, lambda e: e.dma_start(out, in_).then_inc(T.sem[sem], 16), "d", sem, total, 7.0 if sem == "dx" else 2.5)
+
+    def part(k, a, b):
+        for group, buf, w in ((FL, "FL", 16), (IL, "IL", 16), (CM, "CM", 128)):
+            if k in group:
+                o = w * group.index(k)
+                return T[buf][:, o + a:o + b]
+        return T[k][:, a:b]
+
+    def lst(k):
+        return part(k, 0, 16)
+
+    def mat(k):
+        return part(k, 0, 128)
+
+    def vc(n):
+        return 0.02 + max(n, 64) * CYC
+
+    def ts(reads, writes, n, out, in0, s1, o1, s2=None, o2=None):
+        if o2 is None:
+            op("V", reads, writes, vc(n), lambda e: e.tensor_scalar(out, in0, s1, None, o1))
+        else:
+            op("V", reads, writes, vc(n), lambda e: e.tensor_scalar(out, in0, s1, s2, o1, o2))
+
+    def tt(reads, writes, n, out, in0, in1, o):
+        op("V", reads, writes, vc(n), lambda e: e.tensor_tensor(out, in0, in1, o))
+
+    def cp(reads, writes, n, out, in_):
+        op("V", reads, writes, vc(n), lambda e: e.tensor_copy(out, in_))
+
+    def act(reads, writes, n, out, in_, fn, bias=0.0, scale=1.0):
+        op("S", reads, writes, SFIX + n * CYC, lambda e: e.activation(out, in_, fn, bias=bias, scale=scale))
+
+    def mm(reads, writes, n, out, lhsT, rhs, a, z):
+        op("P", reads, writes, vc(n), lambda e: e.matmul(out, lhsT, rhs, a, z))
+
+    def scan(reads, writes, n, out, d0, d1, init, o0, o1):
+        op("V", reads, writes, vc(n), lambda e: e.tensor_tensor_scan(out, d0, d1, init, o0, o1))
+
+    def fill(key, n, ap, c):
+        op("V", "", key, vc(n), lambda e: e.memset(ap, c))
+
+    def iota(key, n, out, pat, base, cm):
+        op("G", "", key, 0.13 + 2 * n * CYC, lambda e: e.iota(out, pat, base, cm, allow_small_or_imprecise_dtypes=True))
+
+    def looks(n):
+        return LOOK * n + 60
+
+    def puts(n):
+        return PUT * n + 60
+    sent = [0]
+
+    def send(t, kind, dst, src, keys):
+        to = T.cores[rank ^ (1 + t % (len(T.cores) - 1))]
+        rid, pid = topo.addr(to)[:2]
+        m = topo.mask(core, to)
+        n = bin(m).count("1")
+        sem = "r%s%d" % (kind, t)
+        sent[0] += n
+        op("G", keys, "recv%s%d" % (kind, t), 0.3, lambda e: e.remote_dma(dst, src, T.sem[sem], T.sem.loc, pid, rid, m), "r", sem, n, REMOTE)
+
+    XK = "Xa Xb"
+    dma("S", "dv", 16, T.V0[:], T.v0[:], "", "V0")
+    dma("S", "ds", 16, T.SD[:], T.sd[:], "", "SD")
+    dma("S", "dt", 16, T.TI[:], T.th[:], "", "TI")
+    dma("Y", "dx", 32, T.X[0:64, 0:W], T.x[0:64, :], "", "Xa")
+    dma("Y", "dx", 32, T.X[64:128, 0:W], T.x[64:128, :], "", "Xb")
+
+    iota("PI0", 1, T.PI[:, 0:1], [[0, 1]], 0, 1)
+    iota("RM", 256, T.RM[:], [[0, 16], [1, 16]], 0, 0)
+    iota("RP", 128, T.RP[:], [[1, 128]], 0, 0)
+    iota("RG", 128, T.RG[:], [[1, 8], [0, 16]], 0, 0)
+    iota("RD", 256, T.RD[:], [[1, 16], [0, 16]], 0, 0)
+    iota("DMI", 16, T.DM[:], [[16, 16]], W, 0)
+    for j in range(8):
+        iota("IO%d" % j, 512, T.IO[:, 512 * j:512 * j + 512], [[1, 512]], 512 * j, 0)
+        act("IO%d" % j, "IO%d" % (j + 8), 512, T.IO[:, 512 * j + 4096:512 * j + 4608], T.IO[:, 512 * j:512 * j + 512], AF.Identity, bias=4096.0)
+    IOK = " ".join("IO%d" % j for j in range(16))
+    ts("PI0", "PI1", 1, T.PI[:, 1:2], T.PI[:, 0:1], 15, Op.bitwise_and)
+    ts("PI0", "PI2", 1, T.PI[:, 2:3], T.PI[:, 0:1], 4, Op.arith_shift_right)
+    cp("PI0 PI1 PI2", "PF", 3, T.PF[:, 0:3], T.PI[:, 0:3])
+    p, pi, pg = T.PF[:, 0:1], T.PF[:, 1:2], T.PF[:, 2:3]
+    ts("RM PF", "NM", 256, T.NM[:], T.RM[:], pi, Op.not_equal, -8192.0, Op.mult)
+    ts("RG PF", "BO", 128, mat("BO"), T.RG[:], pg, Op.is_equal)
+    ts("RM", "K4", 256, T.K4[:], T.RM[:], 0.0, Op.is_equal, -65536.0, Op.mult)
+    ts("K4", "D0", 256, T.D0[:], T.K4[:], 32768.0, Op.add)
+    ts("RP PF", "ID", 128, mat("ID"), T.RP[:], p, Op.is_equal)
+    ts("RP PF", "NI", 128, mat("NI"), T.RP[:], p, Op.is_equal, -1.0, Op.mult)
+    ts("RP PF", "N5", 128, mat("N5"), T.RP[:], p, Op.is_equal, -512.0, Op.mult)
+    ts("RM PF", "K1", 256, T.K1[:], T.RM[:], pi, Op.is_equal)
+    ts("RM PF", "K2", 128, T.K2[:, 0:128], T.RM[:, 0:128], pi, Op.is_gt)
+    tt("K2 BO", "TG", 256, mat("TG"), T.K2[:, 0:128], mat("BO"), Op.mult)
+    ts("BO", "BK", 128, mat("BK"), mat("BO"), 32768.0, Op.mult)
+    ts("ID", "KA", 128, T.KA[:, 0:128], mat("ID"), -16384.0, Op.mult)
+    ts("TG", "KB", 128, T.KA[:, 128:256], mat("TG"), 32768.0, Op.mult)
+    tt("KA KB", "TK", 256, mat("TK"), T.KA[:, 0:128], T.KA[:, 128:256], Op.add)
+    ts("RM PF", "KC", 256, T.KC[:], T.RM[:], pi, Op.not_equal, -float(2 ** 24 + 2 ** 14), Op.mult)
+    ts("KC", "NK", 256, T.NK[:], T.KC[:], 16384.0, Op.add)
+    ts("DMI PF", "DM", 16, T.DM[:], T.DM[:], pi, Op.add)
+    ts("DM", "DS", 16, lst("DS"), T.DM[:], 1.0 / 16384, Op.mult)
+    fill("OB", 128, T.OB[:], 1.0)
+    for t in range(TS):
+        fill("OW%d" % t, 128, T.OW[:, 256 * t:256 * t + 256], 32.0 ** (t + 1 - TS))
+    fill("ZB", 265, T.ZB[:], 0.0)
+    fill("ON", 64, mat("ON"), 1.0)
+    fill("SC0", 1, T.SC[:, 0:1], 0.0)
+    fill("THR", 16, lst("THR"), 9.0)
+    fill("FR", 16, lst("FR"), 0.0)
+    cp("TI", "TF", 4, T.TF[:], T.TI[:])
+    ts("RD PF", "K2", 256, T.K2[:], T.RD[:], pi, Op.is_equal, 2.0, Op.mult)
+    tt("K1 K2", "K3", 512, T.K3[:], T.K1[:], T.K2[:], Op.mult)
+    ts("K3", "K3", 256, T.K3[:], T.K3[:], 4194304.0, Op.mult)
+    tt("K1 K3", "K3", 512, T.K3[:], T.K3[:], T.K1[:], Op.add)
+    tt("K2 K3", "CO", 512, T.CO[:], T.K3[:], T.K2[:], Op.add)
+    fill("TH0", 16, T.TH[:, 0:4], 0.75 * 2.0 ** 33)
+    for k in range(1, 4):
+        fill("TH%d" % k, 16, T.TH[:, 4 * k:4 * k + 4], 0.75 * 2.0 ** (11 * (3 - k)))
+    cp("TH0 TH1 TH2 TH3", "TH4", 16, T.TH[:, 16:32], T.TH[:, 0:16])
+    cp("TH0 TH1 TH2 TH3 TH4", "TH5", 32, T.TH[:, 32:64], T.TH[:, 0:32])
+    cp("TH0 TH1 TH2 TH3 TH4 TH5", "TH", 64, T.TH[:, 64:128], T.TH[:, 0:64])
+    ts("K1", "K4", 128, T.K4[:, 0:128], T.K1[:, 0:128], 2.0 ** 46, Op.mult, 1.0, Op.max)
+    tt("K4 TH TH5", "TH", 256, T.TH[:], T.TH[:], T.K4[:, 0:128], Op.mult)
+    ts("BO", "K3", 128, T.K3[:, 0:128], mat("BO"), 0.0, Op.is_equal, 1.0e29, Op.mult)
+    tt("K3 TH", "TH", 256, T.TH[:], T.TH[:], T.K3[:, 0:128], Op.max)
+    for h in range(2):
+        for a in range(2):
+            fill("WH%d%d" % (h, a), 1, T.WH[64 * a:64 * a + 64, h:h + 1], 2.0 ** (11 * (3 - 2 * h - a)))
+    pieces = []
+    for j in range(0, 8464, 1058):
+        fill("QA" + str(j), 529, T.QA[:, j:j + 1058], 0.0)
+        for i in range(j, j + 1058, 264):
+            pieces.append((str(j), i, min(264, j + 1058 - i)))
+
+    for key, i, n in pieces:
+        act("ZB", "HT" + key, n, T.HT[:, i:i + n], T.ZB[:, 0:n], AF.Copy)
+
+    def wipe(Q, a, b, behind):
+        for key, i, n in pieces[a:b]:
+            op("G", behind, Q + key, 0.13 + 2 * n * CYC, lambda e, i=i, n=n: e.iota(T[Q][:, i:i + n], [[0, n]], 0, 0, allow_small_or_imprecise_dtypes=True))
+    tabs = {buf: " ".join(buf + str(j) for j in range(0, 8464, 1058)) for buf in ("QA", "QB", "HT")}
+
+    def hs(h):
+        return slice(128 * h, 128 * h + 128)
+
+    def rowsum(src, key0, key1):
+        for h, key in ((0, key0), (1, key1)):
+            u = "pU%d" % h
+            mm("ID NM", u, 128, T[u][:, 0:128], mat("ID"), T.NM[:, 0:128], True, False)
+            mm("BO " + key, u, 128, T[u][:, 0:128], mat("BO"), src[:, hs(h)], False, True)
+            scan("D0 " + u, "UL%d" % h, 128, T.UL[:, hs(h)], T.D0[:, 0:128], T[u][:, 0:128], -8192.0, Op.min, Op.max)
+
+    SQK = "SQ.0 SQ.1 SQ.2"
+
+    def squares(dst):
+        for m in range(2):
+            act("UL0 UL1", "%s.%d" % (dst, m), 16, T[dst][:, 16 * m:16 * m + 16], T.UL[:, 15::16], AF.Square, bias=2.0 * KAPPA[m], scale=0.25)
+        for m in (2, 3):
+            ts("UL0 UL1", "XQ%d" % m, 16, T.XQ[:, 16 * m - 32:16 * m - 16], T.UL[:, 15::16], 0.25, Op.mult, 2.0 * KAPPA[m], Op.add)
+        tt("XQ2 XQ3", "%s.2" % dst, 64, T[dst][:, 32:64], T.XQ[:], T.XQ[:], Op.mult)
+
+    def vk():
+        for m in range(4):
+            ts("VN", "VK%d" % m, 16, T.VK[:, 16 * m:16 * m + 16], lst("VN"), -4.0 * KAPPA[m] ** 2 - 0.25, Op.add)
+
+    def step(t, b):
+        if b:
+            rowsum(T.Z, "Z0", "Z1")
+            squares("SQ")
+        for h in range(2):
+            src, zk = (T.SD[:, hs(h)], "SD") if b == 0 else (T.Z[:, hs(h)], "Z%d" % h)
+            mm("NI " + zk, "pD%d" % h, 128, T["pD%d" % h][:, 0:128], mat("NI"), src, True, False)
+        tn = "TN%d" % b
+        if b:
+            tt(SQK + " VK0 VK1 VK2 VK3", "XI0 XI1 XI2 XI3", 128, T.XI[:], T.SQ[:], T.VK[:], Op.add)
+        else:
+            for m in range(4):
+                tt("SY%d VN" % m, "XI%d" % m, 32, T.XI[:, 16 * m:16 * m + 16], T.SZ[:, 16 * m:16 * m + 16], lst("VN"), Op.add)
+        ts("XI0 XI1 XI2 XI3", tn, 64, T.TN[:, 64 * b:64 * b + 64], T.XI[:], W - 1, Op.bitwise_and)
+        cp(tn, "OF", 64, T.OF[:], T.TN[:, 64 * b:64 * b + 64])
+        for h in range(2):
+            boost[0] = AHEAD * (1 - h)
+            look = [T.X[:, 0:W].indirect(T.OF[:, 16 * m + 8 * h:16 * m + 8 * h + 8]) for m in range(4)]
+            y, d = "Y%d." % h, "pD%d" % h
+            ys = [T.Y[:, 256 * m + 128 * h:256 * m + 128 * h + 128] for m in range(4)]
+            if h in SFIRST:
+                act(XK + " OF", y + "0", looks(128), ys[0], look[0], AF.Copy)
+            else:
+                cp(XK + " OF", y + "0", looks(128), ys[0], look[0])
+            for m in range(1, 4):
+                tt("%s OF %s%d" % (XK, y, m - 1), "%s%d" % (y, m), looks(128), ys[m], look[m], ys[m - 1], Op.max)
+            mm("ID %s3" % y, d, 128, T[d][:, 0:128], mat("ID"), ys[3], False, True)
+            if b < 3:
+                act(d, "Z%d" % h, 128, T.Z[:, hs(h)], T[d][:, 0:128], AF.Abs)
+            else:
+                act(d, "ZF%d.%d" % (t, h), 128, T["ZF%d" % t][:, hs(h)], T[d][:, 0:128], AF.Abs)
+        boost[0] = 0.0
+
+    def spread(key, out, src):
+        act(src, key, 16, out[:, 0:16], lst(src), AF.Identity, bias=float(D), scale=-float(D))
+        for n in (16, 32, 64, 128):
+            act(key, key, n, out[:, n:2 * n], out[:, 0:n], AF.Copy)
+
+    def halts(t):
+        for h in range(2):
+            ts("ZF%d.%d TF" % (t, h), "F%d" % h, 64, T.F[:, hs(h)], T["ZF%d" % t][:, hs(h)], T.TF[:, t:t + 1], Op.is_ge)
+        rowsum(T.F, "F0", "F1")
+        tt("UL0 UL1 THR", "HA", 32, T.HA[:], T.UL[:, 15::16], lst("THR"), Op.is_ge)
+        mm("TG HA", "pC", 16, T.pC[:, 0:16], mat("TG"), T.HA[:], True, False)
+        mm("N5 HA", "pC", 16, T.pC[:, 0:16], mat("N5"), T.HA[:], False, False)
+        scan("OB HA", "SC1", 16, T.SC[:, 1:17], T.OB[:, 0:16], T.HA[:], 0.0, Op.mult, Op.add)
+        mm("BO SC0 SC1", "pC", 16, T.pC[:, 0:16], mat("BO"), T.SC[:, 0:16], False, True)
+        ts("pC", "GO", 16, lst("GO"), T.pC[:, 0:16], float(CAP - 512), Op.is_lt)
+
+    def shadows():
+        for c in range(16):
+            ts("DV VF GO", "EB%d" % c, (L - 16 * c) // 2, T.EB[:, c, 0:L - 16 * c], T.DV[:, 16 * c:L], part("VF", c, c + 1), Op.is_equal, part("GO", c, c + 1), Op.mult)
+            if c < 15:
+                mm("BK EB%d" % c, "pH", L - 16 - 16 * c, T.pH[:, 272 + 16 * c:512], mat("BK"), T.EB[:, c, 16:L - 16 * c], False, False)
+        mm("TK " + " ".join("EB%d" % c for c in range(16)), "pH", 256, T.pH[:, 256:512], mat("TK"), T.EB[:, :, 0:16], False, True)
+
+    def places():
+        cp("VN", "OV", 16, T.OV[:], lst("VN"))
+        cp("VN", "VF", 16, lst("VF"), lst("VN"))
+        cp("OV " + IOK, "DV", looks(256), T.DV[:], T.IO[:].indirect(T.OV[:]))
+
+    def base():
+        ts("VC", "S1", 16, lst("S1"), lst("VC"), 4095, Op.bitwise_and)
+        tt("S1", "S2", 32, lst("S2"), lst("S1"), lst("S1"), Op.mult)
+        ts("S2", "S3", 16, lst("S3"), lst("S2"), 3, Op.arith_shift_right)
+        ts("VC", "S4", 16, lst("S4"), lst("VC"), 37.0, Op.mult)
+        tt("S3 S4", "BA", 32, lst("BA"), lst("S4"), lst("S3"), Op.add)
+
+    def hits(t, onv):
+        mark = 32.0 ** (t + 1 - TS)
+        cp("OD OW%d " % t + tabs["HT"], tabs["HT"], puts(256), T.HT[:, 0:8448].indirect(T.OD[:]), T.OW[:, 256 * t:256 * t + 256])
+        for k in range(16):
+            hb, b0 = "HB%d" % (k % 8), 256 * (k % 8)
+            src, key = T.HT[:].indirect(T.OM[:, 16 * k:16 * k + 16]), "%s OM" % tabs["HT"]
+            chain[0] = "V" if k in onv else "S"
+            if k in onv:
+                cp(key, hb, looks(256), T.HB[:, b0:b0 + 256], src)
+            else:
+                act(key, hb, looks(256), T.HB[:, b0:b0 + 256], src, AF.Copy)
+            chain[0] = None
+            if k == 0:
+                mm("ID NM", "pH", 256, T.pH[:, 0:256], mat("ID"), T.NM[:], True, False)
+            mm("ID " + hb, "pH", 256, T.pH[:, 0:256], mat("ID"), T.HB[:, b0:b0 + 256], False, k == 15)
+        scan("D0 pH", "HUL", 256, T.HUL[:], T.D0[:], T.pH[:, 0:256], -8192.0, Op.min, Op.max)
+        tt("FR recvD%d" % t, "FS", 32, lst("FS"), T["DR%d" % t][:], lst("FR"), Op.add)
+        if mark != 1.0:
+            ts("FS", "FS", 16, lst("FS"), lst("FS"), mark, Op.mult)
+        fr, v = (T.YS[:, 16:32], T.YS[:, 0:16]) if t == TS - 1 else (lst("FR"), lst("VC"))
+        tt("VC VN", "S5", 32, lst("S5"), lst("VC"), lst("VN"), Op.subtract)
+        tt("HUL FS", "FR", 32, fr, T.HUL[:, 15::16], lst("FS"), Op.is_lt)
+        tt("S5 FR", "S6", 32, lst("S6"), lst("S5"), fr, Op.mult)
+        tt("S6 VN", "VC", 32, v, lst("S6"), lst("VN"), Op.add)
+
+    def keep():
+        ts("FR", "THR", 16, lst("THR"), lst("FR"), 1000.0, Op.mult, 9.0, Op.add)
+        base()
+        spread("NF", T.NF, "FR")
+        ts("NF", "FO", 128, T.FO[:], T.NF[:], -1.0, Op.mult, float(D), Op.add)
+        tt("TR NF", "P1", 512, T.P1[:], T.TR[:], T.NF[:], Op.max)
+
+    cp("V0", "VN", 16, lst("VN"), T.V0[:])
+    cp("V0", "VC", 16, lst("VC"), T.V0[:])
+    rowsum(T.SD, "SD", "SD")
+    squares("SZ")
+    for m in range(4):
+        ts("SZ.%d" % min(m, 2), "SY%d" % m, 16, T.SZ[:, 16 * m:16 * m + 16], T.SZ[:, 16 * m:16 * m + 16], -4.0 * KAPPA[m] ** 2 - 0.25, Op.add)
+    base()
+
+    for t in range(TS):
+        last = t == TS - 1
+        Q = "QA" if t % 2 == 0 else "QB"
+        zf = "ZF%d" % t
+        vk()
+        places()
+        for b in range(4):
+            step(t, b)
+        mm("ID NK", "pH", 256, T.pH[:, 256:512], mat("ID"), T.NK[:], True, False)
+        halts(t)
+        shadows()
+        if not last:
+            send(t, "Z", T["ZP%d" % t][:], T[zf][:], zf + ".0 " + zf + ".1")
+        scan("D0 pH", "DUL", 256, T.DUL[:], T.D0[:], T.pH[:, 256:512], -8192.0, Op.min, Op.max)
+        tt("DUL VF", "L1", 32, lst("L1"), T.DUL[:, 15::16], lst("VF"), Op.max)
+        tt("L1 DM", "L2", 32, lst("L2"), lst("L1"), T.DM[:], Op.min)
+        lq = "LQ%d" % t
+        cp("L2", lq, 16, T[lq][:], lst("L2"))
+        send(t, "L", T["RL%d" % t][:], T[lq][:], lq)
+        if t < 3:
+            wipe("QA" if t == 1 else "QB", 0, 16, lq)
+        tn = "TN0 TN1 TN2 TN3"
+        spread("NG", T.NG, "GO")
+        tt(tn + " NG", "M1", 512, T.M1[:], T.TN[:], T.NG[:], Op.max)
+        if t == 0:
+            cp("M1", "OM", 256, T.OM[:], T.M1[:])
+        else:
+            tt("M1 P1", "M2", 512, T.M2[:], T.M1[:], T.P1[:], Op.min)
+            cp("M2", "OM", 256, T.OM[:], T.M2[:])
+        rl = T["RL%d" % t]
+        rk = "recvL%d" % t
+        cp("%s CO %s" % (rk, tabs[Q]), tabs[Q], puts(256), T[Q][:, 0:8448].indirect(rl[:]), T.CO[:])
+        cp(rk, "LF", 16, lst("LF"), rl[:])
+        ts("LF", "IW", 16, lst("IW"), lst("LF"), float(W), Op.is_lt)
+        ts("LF", "LD", 16, lst("LD"), lst("LF"), 1.0 / 16384, Op.mult)
+        if t == 0:
+            cp(tn, "TR", 256, T.TR[:], T.TN[:])
+        else:
+            tt(tn + " FO", "P2", 512, T.P2[:], T.TN[:], T.FO[:], Op.max)
+            tt("P1 P2", "TR", 512, T.TR[:], T.P2[:], T.P1[:], Op.min)
+        if last:
+            dma("Y", "dy", 32, T.yt[:], T.TR[:], "TR", "yt")
+
+        def turn(k):
+            b0, pt, a0 = 512 * k, "pT%d" % (k % 2), 512 * (k % 4)
+            for j in range(4):
+                op("P", "ID GB%d%s" % (k, "aabb"[j]), pt, 128 * CYC, lambda e, j=j: e.transpose(T[pt][:, POS[j]:POS[j] + 128], T.GB[:, b0 + 128 * j:b0 + 128 * j + 128], mat("ID")))
+            for h in range(2):
+                a1 = 256 * h
+                ts("%s WH%d0 WH%d1" % (pt, h, h), "LA%d" % (k % 4), 128, T.LA[:, a0 + a1:a0 + a1 + 256], T[pt][:, a1:a1 + 256], T.WH[:, h:h + 1], Op.mult)
+            ts(pt, "LB%d" % (k % 4), 256, T.LB[:, a0:a0 + 512], T[pt][:, 0:512], -1.0, Op.add, 0.0, Op.max)
+
+        def cells(k):
+            for j in range(4):
+                a0 = 512 * (k % 4) + 128 * j
+                mm("LA%d LB%d" % (k % 4, k % 4), "pC", 128, T.pC[:, 128:256], T.LA[:, a0:a0 + 128], T.LB[:, a0:a0 + 128], k == 0 and j == 0, k == 7 and j == 3)
+        for k in range(8):
+            key = "%s OM" % tabs[Q]
+            if k == 0:
+                cp(key, "GB0a", looks(256), T.GB[:, 0:256], T[Q][:].indirect(T.OM[:, 0:16]))
+                act(key, "GB0b", looks(256), T.GB[:, 256:512], T[Q][:].indirect(T.OM[:, 16:32]), AF.Copy)
+            else:
+                act(key, "GB%da GB%db" % (k, k), looks(512), T.GB[:, 512 * k:512 * k + 512], T[Q][:].indirect(T.OM[:, 32 * k:32 * k + 32]), AF.Copy)
+        for k in range(8):
+            turn(k)
+            cells(k)
+        tt("pC TH", "MC", 128, T.MC[:], T.pC[:, 128:256], T.TH[:], Op.is_ge)
+        tt("MC", "MD", 128, T.MD[:], T.MC[:, 0:64], T.MC[:, 64:128], Op.add)
+        tt("MD", "ME", 64, T.ME[:], T.MD[:, 0:32], T.MD[:, 32:64], Op.add)
+        tt("ME", "MF", 32, T.MF[:], T.ME[:, 0:16], T.ME[:, 16:32], Op.add)
+        do = "DO%d" % t
+        tt("MF IW", do, 32, T[do][:], T.MF[:], lst("IW"), Op.is_lt)
+        mm("ON " + do, "pC", 16, T.pC[:, 0:16], mat("ON"), T[do][:], True, True)
+        send(t, "D", T["DR%d" % t][:], T[do][:], do)
+        tt("LD MF", "E1", 32, lst("E1"), T.MF[:], lst("LD"), Op.max)
+        tt("E1 DS", "E2", 32, lst("E2"), lst("E1"), lst("DS"), Op.min)
+        ts("E2", "OD", 16, T.OD[:], lst("E2"), 16384.0, Op.mult)
+        op("V", "pC", "AA", vc(16), lambda e: e.tensor_reduce(T.AA[:], T.pC[:, 0:16], AxisListType.X, Op.add))
+        if not last:
+            cp("OD recvZ%d" % t, XK, puts(256), T.X[:].indirect(T.OD[:]), T["ZP%d" % t][:])
+        ts("BA AA", "S7", 16, lst("S7"), lst("BA"), T.AA[:], Op.add)
+        ts("S7", "VN", 16, lst("VN"), lst("S7"), W - 1, Op.bitwise_and)
+        if t == 0:
+            wipe("QB", 16, 40, "DO0")
+        if 0 < t < 3:
+            wipe("QA" if t == 1 else "QB", 16, 40, do)
+        hits(t, (1, 3, 5, 7, 9, 11, 13, 15) if last else HITS_ON_VECTOR)
+        if not last:
+            keep()
+    dma("Y", "dy", 32, T.ys[:], T.YS[:], "FR VC", "ys")
+
+    N = len(ops)
+    preds = [dict() for _ in ops]
+    last_w, readers, banks = {}, {}, {}
+    ends = {}
+    for i, o in enumerate(ops):
+        def after(j, wake):
+            if j != i:
+                preds[i][j] = max(preds[i].get(j, 0.0), wake)
+        if o["chain"]:
+            if o["chain"] in ends:
+                after(ends[o["chain"]], 0.0)
+            ends[o["chain"]] = i
+        for k in o["r"] + o["w"]:
+            if k[0] == "p":
+                for q, j in banks.get(k, {}).items():
+                    after(j, WAKE if q != o["q"] else 0.0)
+        for k in o["r"]:
+            if k[0] != "p" and k in last_w:
+                after(last_w[k], WAKE)
+        for k in o["w"]:
+            if k[0] != "p":
+                if k in last_w:
+                    after(last_w[k], WAKE)
+                for j in readers.get(k, []):
+                    after(j, WAKE)
+        for k in o["r"] + o["w"]:
+            if k[0] == "p":
+                banks.setdefault(k, {})[o["q"]] = i
+        for k in o["r"]:
+            if k[0] != "p":
+                readers.setdefault(k, []).append(i)
+        for k in o["w"]:
+            if k[0] != "p":
+                last_w[k] = i
+                readers[k] = []
+    succs = [[] for _ in ops]
+    for i in range(N):
+        for j, wake in preds[i].items():
+            succs[j].append((i, wake))
+    prio = [0.0] * N
+    for i in range(N - 1, -1, -1):
+        best = 0.0
+        for j, wake in succs[i]:
+            gap = GAP[ops[i]["chain"]] if ops[i]["chain"] and ops[i]["chain"] == ops[j]["chain"] else 0.0
+            best = max(best, wake + ops[i]["lat"] + gap + prio[j])
+        prio[i] = best + ops[i]["cost"] + ops[i]["first"]
+        if STIR:
+            prio[i] += STIR * ((i * 7919 + SEED * 104729) * 2654435761 % 4294967296) / 4294967296
+    left = [len(preds[i]) for i in range(N)]
+    ready = [0.0] * N
+    free = {q: 0.0 for q in eng}
+    avail = {q: [] for q in eng}
+    for i in range(N):
+        if left[i] == 0:
+            avail[ops[i]["q"]].append(i)
+    order = []
+    over = [False] * N
+    came = [0.0] * N
+    line = {q: sorted((i for i in range(N) if ops[i]["q"] == q), key=lambda i: -prio[i]) for q in eng}
+
+    def soonest(i, memo):
+        if left[i] == 0:
+            return ready[i]
+        if i not in memo:
+            best = 0.0
+            for j, wake in preds[i].items():
+                if over[j]:
+                    best = max(best, came[j] + ops[j]["lat"] + wake)
+                else:
+                    best = max(best, max(soonest(j, memo), free[ops[j]["q"]]) + ops[j]["cost"] + ops[j]["lat"] + wake)
+            memo[i] = best
+        return memo[i]
+
+    order += ORDER
+    while len(order) < N:
+        pick = None
+        for q in "VSPGY":
+            if avail[q]:
+                t0 = max(free[q], min(ready[i] for i in avail[q]))
+                if pick is None or t0 < pick[0]:
+                    pick = (t0, q)
+        t0, q = pick
+        line[q] = [i for i in line[q] if not over[i]]
+        memo, i, wait = {}, None, None
+        for c in sorted((c for c in avail[q] if ready[c] <= t0), key=lambda c: -prio[c]):
+            cost = ops[c]["cost"]
+            block = None
+            for j in line[q][:8]:
+                if j == c or prio[j] < prio[c] + MARGIN * cost:
+                    break
+                e = soonest(j, memo)
+                if t0 < e < t0 + cost - 0.02:
+                    block = e if block is None else min(block, e)
+            if block is None:
+                i = c
+                break
+            wait = block if wait is None else min(wait, block)
+        if i is None:
+            free[q] = wait
+            continue
+        avail[q].remove(i)
+        done = t0 + ops[i]["cost"]
+        free[q] = came[i] = done
+        over[i] = True
+        order.append(i)
+        for j, wake in succs[i]:
+            ready[j] = max(ready[j], done + ops[i]["lat"] + wake)
+            left[j] -= 1
+            if left[j] == 0:
+                avail[ops[j]["q"]].append(j)
+
+    if not ORDER:
+        ORDER.extend(order)
+
+    count = {q: 0 for q in eng}
+    clock = {q: {} for q in eng}
+    wr, rd, bank = {}, {}, {}
+
+    def need(q, tok):
+        s, n, known = tok
+        if clock[q].get(s, 0) < n:
+            eng[q].wait_ge(T.sem[s], n)
+            clock[q][s] = n
+            for k, m in known.items():
+                clock[q][k] = max(clock[q].get(k, 0), m)
+
+    for i in order:
+        o = ops[i]
+        q, keys = o["q"], o["r"] + o["w"]
+        toks = []
+        for k in keys:
+            if k[0] == "p":
+                toks += [tok for q2, tok in bank.get(k, {}).items() if q2 != q]
+            elif k in wr:
+                toks.append(wr[k])
+        for k in o["w"]:
+            if k[0] != "p":
+                toks += rd.get(k, {}).values()
+        best = {}
+        for tok in toks:
+            if tok[0] not in best or best[tok[0]][1] < tok[1]:
+                best[tok[0]] = tok
+        for s in sorted(best, key=lambda s: -len(best[s][2])):
+            need(q, best[s])
+        ins = o["f"](eng[q])
+        if o["kind"] == "c":
+            ins.then_inc(T.sem["c" + q], 1)
+            count[q] += 1
+            tok = ("c" + q, count[q], dict(clock[q]))
+        elif o["kind"] == "d":
+            tok = (o["sem"], o["n"], dict(clock[q]))
+        else:
+            tok = (o["sem"], o["n"], {})
+        for k in keys:
+            if k[0] == "p":
+                bank.setdefault(k, {})[q] = tok
+        for k in o["r"]:
+            if k[0] != "p" and o["kind"] != "r":
+                rd.setdefault(k, {})[q] = tok
+        for k in o["w"]:
+            if k[0] != "p":
+                wr[k] = tok
+                rd[k] = {}
+    g.sync.wait_ge(T.sem.dy, 32)
+    g.wait_ge(T.sem.loc, sent[0])
+    for q in "VSPG":
+        g.wait_ge(T.sem["c" + q], count[q])

@@ -3,51 +3,57 @@ from concourse.mybir import AluOpType as Op, AxisListType, ActivationFunctionTyp
 W, L, D = 8192, 256, 8448
 KAPPA = (3, 29, 71, 113)
 TS, CAP = 4, 128
-FL = "GO THR DS L1 L2 LF IW LD E1 E2 FR FS VF BA S4 S5 S6".split()
-IL = "VN VC S1 S2 S3 S7".split()
-CM = "ID NI N5 BO TG ON BK TK".split()
+FL = "L1 L2 R1 R2 LF IW E1 E2 FR FS VF BA BM S4 S5 S6 DM".split()
+IL = "VN VC S1 S2 S3 S7 S8 S9".split()
+QL = "THR THG NF FO NG VK BK4 SB SQ".split()
+CM = "ID NI N5 NX BO TG ON BK TK T4 O4 B0 B1 B2 B3 C0 C1 C2 C3 U0 U1 U2 U3".split()
 
 SCRATCH = {
     "X": ("sbuf", [128, 8448], "bfloat16"),
-    "QA": ("sbuf", [128, 8464], "bfloat16"), "QB": ("sbuf", [128, 8464], "bfloat16"), "HT": ("sbuf", [128, 8464], "bfloat16"),
+    "Q": ("sbuf", [128, 8464], "bfloat16"), "HT": ("sbuf", [128, 8464], "bfloat16"),
     "OW": ("sbuf", [128, 1024], "bfloat16"),
     "IO": ("sbuf", [128, 8192], "float32"),
     "SD": ("sbuf", [128, 256], "bfloat16"), "V0": ("sbuf", [128, 16], "int32"), "TI": ("sbuf", [128, 4], "int32"), "TF": ("sbuf", [128, 4], "float32"),
-    "PI": ("sbuf", [128, 4], "int32"), "PF": ("sbuf", [128, 4], "float32"),
+    "PI": ("sbuf", [128, 8], "int32"), "PF": ("sbuf", [128, 8], "float32"), "KP": ("sbuf", [128, 16], "float32"),
     "RM": ("sbuf", [128, 256], "float32"), "RD": ("sbuf", [128, 256], "float32"), "RP": ("sbuf", [128, 128], "float32"), "RG": ("sbuf", [128, 128], "float32"),
+    "J0": ("sbuf", [128, 128], "float32"), "J1": ("sbuf", [128, 128], "float32"), "J2": ("sbuf", [128, 128], "float32"), "J3": ("sbuf", [128, 128], "float32"),
+    "J4": ("sbuf", [128, 512], "bfloat16"), "MK": ("sbuf", [128, 512], "bfloat16"),
     "K1": ("sbuf", [128, 256], "float32"), "K2": ("sbuf", [128, 256], "float32"), "K3": ("sbuf", [128, 256], "float32"), "K4": ("sbuf", [128, 256], "float32"),
     "CM": ("sbuf", [128, 128 * len(CM)], "bfloat16"), "FL": ("sbuf", [128, 16 * len(FL)], "float32"), "IL": ("sbuf", [128, 16 * len(IL)], "int32"),
+    "QL": ("sbuf", [128, 64 * len(QL)], "float32"), "UF": ("sbuf", [128, 512], "float32"), "YM": ("sbuf", [128, 2048], "float32"),
     "KA": ("sbuf", [128, 256], "float32"), "KC": ("sbuf", [128, 256], "float32"), "NK": ("sbuf", [128, 256], "bfloat16"),
-    "NM": ("sbuf", [128, 256], "bfloat16"), "CO": ("sbuf", [128, 256], "bfloat16"), "D0": ("sbuf", [128, 256], "float32"),
-    "TH": ("sbuf", [128, 128], "float32"), "WH": ("sbuf", [128, 2], "float32"), "DM": ("sbuf", [128, 16], "float32"),
-    "OB": ("sbuf", [128, 256], "bfloat16"), "ZB": ("sbuf", [128, 529], "bfloat16"),
+    "NM": ("sbuf", [128, 256], "bfloat16"), "CO": ("sbuf", [128, 1024], "bfloat16"), "D0": ("sbuf", [128, 256], "float32"),
+    "WH": ("sbuf", [128, 10], "float32"), "OB": ("sbuf", [128, 64], "bfloat16"),
     "TN": ("sbuf", [128, 256], "int32"), "TR": ("sbuf", [128, 256], "float32"), "P1": ("sbuf", [128, 256], "float32"),
-    "P2": ("sbuf", [128, 256], "float32"), "M1": ("sbuf", [128, 256], "float32"), "M2": ("sbuf", [128, 256], "float32"),
-    "OM": ("sbuf", [128, 256], "uint16"), "NG": ("sbuf", [128, 256], "bfloat16"), "NF": ("sbuf", [128, 256], "bfloat16"), "FO": ("sbuf", [128, 256], "bfloat16"),
-    "OV": ("sbuf", [128, 16], "uint16"), "DV": ("sbuf", [128, 256], "uint16"), "OD": ("sbuf", [128, 16], "uint16"),
-    "HA": ("sbuf", [128, 16], "bfloat16"), "SC": ("sbuf", [128, 18], "bfloat16"),
+    "P2": ("sbuf", [128, 256], "float32"), "M1": ("sbuf", [128, 256], "float32"), "OM": ("sbuf", [128, 256], "uint16"),
+    "DV": ("sbuf", [128, 256], "uint16"), "OD": ("sbuf", [128, 16], "uint16"), "BL": ("sbuf", [128, 16], "uint16"),
+    "HA": ("sbuf", [128, 64], "bfloat16"), "SC": ("sbuf", [128, 66], "bfloat16"), "GO": ("sbuf", [128, 64], "bfloat16"),
+    "FB": ("sbuf", [128, 64], "bfloat16"), "F6": ("sbuf", [128, 16], "bfloat16"), "SY": ("sbuf", [128, 64], "int32"),
     "EB": ("sbuf", [128, 16, 256], "bfloat16"), "DUL": ("sbuf", [128, 256], "float32"), "HUL": ("sbuf", [128, 256], "float32"),
-    "MC": ("sbuf", [128, 128], "bfloat16"), "MD": ("sbuf", [128, 64], "bfloat16"), "ME": ("sbuf", [128, 32], "bfloat16"), "MF": ("sbuf", [128, 16], "bfloat16"),
-    "AA": ("sbuf", [128, 1], "float32"), "YT": ("sbuf", [128, 16, 16], "float32"), "YS": ("sbuf", [128, 32], "float32"),
+    "RUL": ("sbuf", [128, 256], "float32"), "BUL": ("sbuf", [128, 256], "float32"), "MUL": ("sbuf", [128, 256], "float32"),
+    "GQ": ("sbuf", [128, 256], "bfloat16"), "A1": ("sbuf", [128, 256], "bfloat16"), "A2": ("sbuf", [128, 256], "bfloat16"), "A3": ("sbuf", [128, 256], "bfloat16"),
+    "TH": ("sbuf", [128, 256], "bfloat16"), "BB": ("sbuf", [128, 256], "bfloat16"), "BD": ("sbuf", [128, 256], "bfloat16"), "CW": ("sbuf", [128, 128], "float32"),
+    "AA": ("sbuf", [128, 1], "float32"), "YT": ("sbuf", [128, 4, 4, 16], "float32"), "YS": ("sbuf", [128, 32], "float32"),
     "GB": ("sbuf", [128, 4096], "bfloat16"), "HB": ("sbuf", [128, 2048], "bfloat16"), "LA": ("sbuf", [128, 2048], "bfloat16"), "LB": ("sbuf", [128, 2048], "bfloat16"),
-    "pU0": ("psum", [128, 512], "float32"), "pU1": ("psum", [128, 512], "float32"), "pD0": ("psum", [128, 512], "float32"), "pD1": ("psum", [128, 512], "float32"),
+    "Z": ("sbuf", [128, 256], "bfloat16"), "GR": ("sbuf", [128, 1024], "bfloat16"), "H": ("sbuf", [128, 1024], "bfloat16"), "F": ("sbuf", [128, 256], "bfloat16"),
+    "XI": ("sbuf", [128, 64], "int32"), "OF": ("sbuf", [128, 64], "uint16"),
+    "pS0": ("psum", [128, 512], "float32"), "pS1": ("psum", [128, 512], "float32"), "pD0": ("psum", [128, 512], "float32"), "pD1": ("psum", [128, 512], "float32"),
     "pT0": ("psum", [128, 1024], "bfloat16"), "pT1": ("psum", [128, 1024], "bfloat16"), "pC": ("psum", [128, 512], "float32"), "pH": ("psum", [128, 512], "float32"),
 }
-SCRATCH.update({"Z": ("sbuf", [128, 256], "bfloat16"), "Y": ("sbuf", [128, 1024], "bfloat16"), "F": ("sbuf", [128, 256], "bfloat16"),
-                "UL": ("sbuf", [128, 256], "float32"), "SQ": ("sbuf", [128, 64], "float32"), "SZ": ("sbuf", [128, 64], "float32"), "XQ": ("sbuf", [128, 32], "float32"),
-                "XI": ("sbuf", [128, 64], "int32"), "OF": ("sbuf", [128, 64], "uint16"), "VK": ("sbuf", [128, 64], "float32")})
 for _t in range(TS):
     SCRATCH.update({"ZF%d" % _t: ("sbuf", [128, 256], "bfloat16"), "ZP%d" % _t: ("sbuf", [128, 256], "bfloat16"), "LQ%d" % _t: ("sbuf", [128, 16], "uint16"),
-                    "RL%d" % _t: ("sbuf", [128, 16], "uint16"), "DO%d" % _t: ("sbuf", [128, 16], "bfloat16"), "DR%d" % _t: ("sbuf", [128, 16], "bfloat16")})
-SEMAPHORES = ["cV", "cS", "cP", "cG", "dx", "dv", "ds", "dt", "dy", "dz", "loc"] + ["r%s%d" % (k, t) for k in "LZD" for t in range(TS)]
-CYC, WAKE, SFIX, LOOK, PUT, REMOTE = 0.00083, 0.15, 0.15, 1.3, 3.0, 3.0
-MARGIN, AHEAD = 2, 0.0
-STIR, SEED = 0.0, 0
+                    "RL%d" % _t: ("sbuf", [128, 16], "uint16"), "DO%d" % _t: ("sbuf", [128, 16], "bfloat16"), "DR%d" % _t: ("sbuf", [128, 16], "bfloat16"),
+                    "MS%d" % _t: ("sbuf", [128, 32], "uint16"), "MR%d" % _t: ("sbuf", [128, 32], "uint16")})
+SEMAPHORES = ["cV", "cS", "cP", "cG", "dx", "dv", "ds", "dt", "dy", "loc"] + ["r%s%d" % (k, t) for k in "MLZD" for t in range(TS)]
+CYC, WAKE, SFIX, LOOK, PUT, REMOTE = 0.00083, 0.15, 0.15, 1.56, 3.8, 3.0
+MARGIN = 2
 ORDER = []
-SFIRST = (1,)
+RUN_S = (16, 16)
+CLAIM_V = ((0, 16), (3, 32))
+HITS_V = (4, 9, 14)
+LAST_V = (1, 3, 5, 7, 9, 11, 13, 15)
 GAP = {"S": 0.3, "V": 0.9}
-POS = (0, 256, 128, 384)
-HITS_ON_VECTOR = (4, 9, 14)
+AHEAD = 0.0
 
 
 def rank_program(g, core, T, topo):
@@ -65,15 +71,18 @@ def rank_program(g, core, T, topo):
     def dma(q, sem, total, out, in_, reads, writes):
         op(q, reads, writes, 0.1, lambda e: e.dma_start(out, in_).then_inc(T.sem[sem], 16), "d", sem, total, 7.0 if sem == "dx" else 2.5)
 
-    def part(k, a, b):
-        for group, buf, w in ((FL, "FL", 16), (IL, "IL", 16), (CM, "CM", 128)):
+    def part(k, a, b, step=1):
+        for group, buf, w in ((FL, "FL", 16), (IL, "IL", 16), (QL, "QL", 64), (CM, "CM", 128)):
             if k in group:
                 o = w * group.index(k)
-                return T[buf][:, o + a:o + b]
-        return T[k][:, a:b]
+                return T[buf][:, o + a:o + b:step]
+        return T[k][:, a:b:step]
 
     def lst(k):
         return part(k, 0, 16)
+
+    def quad(k, h=None):
+        return part(k, 0, 64) if h is None else part(k, 32 * h, 32 * h + 32)
 
     def mat(k):
         return part(k, 0, 128)
@@ -96,8 +105,14 @@ def rank_program(g, core, T, topo):
     def act(reads, writes, n, out, in_, fn, bias=0.0, scale=1.0):
         op("S", reads, writes, SFIX + n * CYC, lambda e: e.activation(out, in_, fn, bias=bias, scale=scale))
 
+    def look(q, reads, writes, n, out, src):
+        if q == "V":
+            op("V", reads, writes, 0.05 + LOOK * n * CYC, lambda e: e.tensor_copy(out, src))
+        else:
+            op("S", reads, writes, 0.065 + LOOK * n * CYC, lambda e: e.activation(out, src, AF.Copy))
+
     def mm(reads, writes, n, out, lhsT, rhs, a, z):
-        op("P", reads, writes, vc(n), lambda e: e.matmul(out, lhsT, rhs, a, z))
+        op("P", reads, writes, max(n, 64) * CYC, lambda e: e.matmul(out, lhsT, rhs, a, z))
 
     def scan(reads, writes, n, out, d0, d1, init, o0, o1):
         op("V", reads, writes, vc(n), lambda e: e.tensor_tensor_scan(out, d0, d1, init, o0, o1))
@@ -109,10 +124,10 @@ def rank_program(g, core, T, topo):
         op("G", "", key, 0.13 + 2 * n * CYC, lambda e: e.iota(out, pat, base, cm, allow_small_or_imprecise_dtypes=True))
 
     def looks(n):
-        return LOOK * n + 60
+        return LOOK * n + 36
 
     def puts(n):
-        return PUT * n + 60
+        return PUT * n + 36
     sent = [0]
 
     def send(t, kind, dst, src, keys):
@@ -125,191 +140,234 @@ def rank_program(g, core, T, topo):
         op("G", keys, "recv%s%d" % (kind, t), 0.3, lambda e: e.remote_dma(dst, src, T.sem[sem], T.sem.loc, pid, rid, m), "r", sem, n, REMOTE)
 
     XK = "Xa Xb"
+    dma("Y", "dx", 32, T.X[0:64, 0:W], T.x[0:64, :], "", "Xa")
+    dma("Y", "dx", 32, T.X[64:128, 0:W], T.x[64:128, :], "", "Xb")
     dma("S", "dv", 16, T.V0[:], T.v0[:], "", "V0")
     dma("S", "ds", 16, T.SD[:], T.sd[:], "", "SD")
     dma("S", "dt", 16, T.TI[:], T.th[:], "", "TI")
-    dma("Y", "dx", 32, T.X[0:64, 0:W], T.x[0:64, :], "", "Xa")
-    dma("Y", "dx", 32, T.X[64:128, 0:W], T.x[64:128, :], "", "Xb")
 
     iota("PI0", 1, T.PI[:, 0:1], [[0, 1]], 0, 1)
     iota("RM", 256, T.RM[:], [[0, 16], [1, 16]], 0, 0)
     iota("RP", 128, T.RP[:], [[1, 128]], 0, 0)
     iota("RG", 128, T.RG[:], [[1, 8], [0, 16]], 0, 0)
     iota("RD", 256, T.RD[:], [[1, 16], [0, 16]], 0, 0)
-    iota("DMI", 16, T.DM[:], [[16, 16]], W, 0)
-    for j in range(8):
+    iota("DMI", 16, lst("DM"), [[16, 16]], W, 0)
+    iota("J0", 128, T.J0[:], [[16, 8], [1000, 4], [4, 4]], 0, 0)
+    iota("J1", 128, T.J1[:], [[16, 8], [1, 4], [0, 4]], 0, 0)
+    iota("J2", 128, T.J2[:], [[1, 8], [1000, 4], [0, 4]], 0, 0)
+    iota("J3", 128, T.J3[:], [[0, 8], [1, 4], [0, 4]], 0, 0)
+    iota("J4", 512, T.J4[:], [[0, 128], [1, 4]], 0, 0)
+    iota("KI", 4, T.KP[:, 0:4], [[1, 4]], 0, 0)
+    for j in range(4):
         iota("IO%d" % j, 512, T.IO[:, 512 * j:512 * j + 512], [[1, 512]], 512 * j, 0)
-        act("IO%d" % j, "IO%d" % (j + 8), 512, T.IO[:, 512 * j + 4096:512 * j + 4608], T.IO[:, 512 * j:512 * j + 512], AF.Identity, bias=4096.0)
+        for a in range(1, 4):
+            act("IO%d" % j, "IO%d" % (j + 4 * a), 512, T.IO[:, 512 * j + 2048 * a:512 * j + 2048 * a + 512], T.IO[:, 512 * j:512 * j + 512], AF.Identity, bias=2048.0 * a)
     IOK = " ".join("IO%d" % j for j in range(16))
     ts("PI0", "PI1", 1, T.PI[:, 1:2], T.PI[:, 0:1], 15, Op.bitwise_and)
     ts("PI0", "PI2", 1, T.PI[:, 2:3], T.PI[:, 0:1], 4, Op.arith_shift_right)
-    cp("PI0 PI1 PI2", "PF", 3, T.PF[:, 0:3], T.PI[:, 0:3])
-    p, pi, pg = T.PF[:, 0:1], T.PF[:, 1:2], T.PF[:, 2:3]
-    ts("RM PF", "NM", 256, T.NM[:], T.RM[:], pi, Op.not_equal, -8192.0, Op.mult)
+    ts("PI0", "PI3", 1, T.PI[:, 3:4], T.PI[:, 0:1], 2, Op.arith_shift_right, 3, Op.bitwise_and)
+    ts("PI0", "PI4", 1, T.PI[:, 4:5], T.PI[:, 0:1], 3, Op.bitwise_and)
+    cp("PI0 PI1 PI2 PI3 PI4", "PF", 5, T.PF[:, 0:5], T.PI[:, 0:5])
+    p, pi, pg, pr, pm = [T.PF[:, j:j + 1] for j in range(5)]
+    for m in range(4):
+        fill("KV%d" % m, 1, T.KP[:, 4 + m:5 + m], 2.0 * KAPPA[m])
+    ts("KI PF", "KE", 4, T.KP[:, 8:12], T.KP[:, 0:4], pm, Op.is_equal)
+    tt("KE KV0 KV1 KV2 KV3", "KF", 8, T.KP[:, 8:12], T.KP[:, 8:12], T.KP[:, 4:8], Op.mult)
+    op("V", "KF", "K2K", vc(4), lambda e: e.tensor_reduce(T.KP[:, 12:13], T.KP[:, 8:12], AxisListType.X, Op.add))
+    ts("K2K", "KSQ", 1, T.KP[:, 13:14], T.KP[:, 12:13], T.KP[:, 12:13], Op.mult, -1.0, Op.mult)
+    ts("KSQ", "KOF", 1, T.KP[:, 14:15], T.KP[:, 13:14], -0.25, Op.add)
+    k2k, kof = T.KP[:, 12:13], T.KP[:, 14:15]
+    ts("RM PF", "NM", 256, T.NM[:], T.RM[:], pi, Op.not_equal, -float(2 ** 24), Op.mult)
     ts("RG PF", "BO", 128, mat("BO"), T.RG[:], pg, Op.is_equal)
     ts("RM", "K4", 256, T.K4[:], T.RM[:], 0.0, Op.is_equal, -65536.0, Op.mult)
     ts("K4", "D0", 256, T.D0[:], T.K4[:], 32768.0, Op.add)
     ts("RP PF", "ID", 128, mat("ID"), T.RP[:], p, Op.is_equal)
-    ts("RP PF", "NI", 128, mat("NI"), T.RP[:], p, Op.is_equal, -1.0, Op.mult)
-    ts("RP PF", "N5", 128, mat("N5"), T.RP[:], p, Op.is_equal, -512.0, Op.mult)
+    ts("ID", "NI", 64, mat("NI"), mat("ID"), -1.0, Op.mult)
+    ts("ID", "N5", 64, mat("N5"), mat("ID"), -512.0, Op.mult)
+    ts("ID", "NX", 64, mat("NX"), mat("ID"), -1024.0, Op.mult)
     ts("RM PF", "K1", 256, T.K1[:], T.RM[:], pi, Op.is_equal)
     ts("RM PF", "K2", 128, T.K2[:, 0:128], T.RM[:, 0:128], pi, Op.is_gt)
     tt("K2 BO", "TG", 256, mat("TG"), T.K2[:, 0:128], mat("BO"), Op.mult)
-    ts("BO", "BK", 128, mat("BK"), mat("BO"), 32768.0, Op.mult)
+    ts("J4", "MK", 256, T.MK[:], T.J4[:], 1.0, Op.min)
+    for r in range(4):
+        ts("J2 PF", "B%d" % r, 128, mat("B%d" % r), T.J2[:], pg, Op.subtract, 1000.0 * r, Op.is_equal)
+        ts("J0 PF", "C%d" % r, 128, mat("C%d" % r), T.J0[:], p, Op.subtract, 1000.0 * r, Op.is_equal)
+        ts("J1 PF", "UF%d" % r, 128, T.UF[:, 128 * r:128 * r + 128], T.J1[:], p, Op.subtract, -4.0 * r, Op.is_equal)
+        cp("UF%d" % r, "U%d" % r, 128, mat("U%d" % r), T.UF[:, 128 * r:128 * r + 128])
+        for m in range(4):
+            ts("J0 PF", "YM%d%d" % (m, r), 128, T.YM[:, 512 * m + 128 * r:512 * m + 128 * r + 128], T.J0[:], p, Op.subtract, 1000.0 * r - m, Op.is_equal)
+    ts("J3 PF", "J3", 128, T.J3[:], T.J3[:], pr, Op.is_gt, 0.25, Op.mult)
+    tt("J3 BO", "T4", 256, mat("T4"), T.J3[:], mat("BO"), Op.mult)
+    ts("BO", "O4", 64, mat("O4"), mat("BO"), 0.25, Op.mult)
+    ts("BO", "BK", 64, mat("BK"), mat("BO"), 32768.0, Op.mult)
     ts("ID", "KA", 128, T.KA[:, 0:128], mat("ID"), -16384.0, Op.mult)
     ts("TG", "KB", 128, T.KA[:, 128:256], mat("TG"), 32768.0, Op.mult)
     tt("KA KB", "TK", 256, mat("TK"), T.KA[:, 0:128], T.KA[:, 128:256], Op.add)
     ts("RM PF", "KC", 256, T.KC[:], T.RM[:], pi, Op.not_equal, -float(2 ** 24 + 2 ** 14), Op.mult)
     ts("KC", "NK", 256, T.NK[:], T.KC[:], 16384.0, Op.add)
-    ts("DMI PF", "DM", 16, T.DM[:], T.DM[:], pi, Op.add)
-    ts("DM", "DS", 16, lst("DS"), T.DM[:], 1.0 / 16384, Op.mult)
-    fill("OB", 128, T.OB[:], 1.0)
+    ts("DMI PF", "DM", 16, lst("DM"), lst("DM"), pi, Op.add)
+    fill("OB", 32, T.OB[:], 1.0)
     for t in range(TS):
         fill("OW%d" % t, 128, T.OW[:, 256 * t:256 * t + 256], 32.0 ** (t + 1 - TS))
-    fill("ZB", 265, T.ZB[:], 0.0)
     fill("ON", 64, mat("ON"), 1.0)
     fill("SC0", 1, T.SC[:, 0:1], 0.0)
-    fill("THR", 16, lst("THR"), 9.0)
+    fill("THR", 64, quad("THR"), 9.0)
+    fill("THG", 64, quad("THG"), float(CAP - 512))
     fill("FR", 16, lst("FR"), 0.0)
+    fill("AA", 1, T.AA[:], 0.0)
     cp("TI", "TF", 4, T.TF[:], T.TI[:])
     ts("RD PF", "K2", 256, T.K2[:], T.RD[:], pi, Op.is_equal, 2.0, Op.mult)
     tt("K1 K2", "K3", 512, T.K3[:], T.K1[:], T.K2[:], Op.mult)
     ts("K3", "K3", 256, T.K3[:], T.K3[:], 4194304.0, Op.mult)
     tt("K1 K3", "K3", 512, T.K3[:], T.K3[:], T.K1[:], Op.add)
-    tt("K2 K3", "CO", 512, T.CO[:], T.K3[:], T.K2[:], Op.add)
-    fill("TH0", 16, T.TH[:, 0:4], 0.75 * 2.0 ** 33)
-    for k in range(1, 4):
-        fill("TH%d" % k, 16, T.TH[:, 4 * k:4 * k + 4], 0.75 * 2.0 ** (11 * (3 - k)))
-    cp("TH0 TH1 TH2 TH3", "TH4", 16, T.TH[:, 16:32], T.TH[:, 0:16])
-    cp("TH0 TH1 TH2 TH3 TH4", "TH5", 32, T.TH[:, 32:64], T.TH[:, 0:32])
-    cp("TH0 TH1 TH2 TH3 TH4 TH5", "TH", 64, T.TH[:, 64:128], T.TH[:, 0:64])
-    ts("K1", "K4", 128, T.K4[:, 0:128], T.K1[:, 0:128], 2.0 ** 46, Op.mult, 1.0, Op.max)
-    tt("K4 TH TH5", "TH", 256, T.TH[:], T.TH[:], T.K4[:, 0:128], Op.mult)
-    ts("BO", "K3", 128, T.K3[:, 0:128], mat("BO"), 0.0, Op.is_equal, 1.0e29, Op.mult)
-    tt("K3 TH", "TH", 256, T.TH[:], T.TH[:], T.K3[:, 0:128], Op.max)
+    tt("K2 K3", "K3", 512, T.K3[:], T.K3[:], T.K2[:], Op.add)
+    size = [2.0 ** (24 * t - 24) for t in range(TS)]
     for h in range(2):
         for a in range(2):
-            fill("WH%d%d" % (h, a), 1, T.WH[64 * a:64 * a + 64, h:h + 1], 2.0 ** (11 * (3 - 2 * h - a)))
-    pieces = []
-    for j in range(0, 8464, 1058):
-        fill("QA" + str(j), 529, T.QA[:, j:j + 1058], 0.0)
-        for i in range(j, j + 1058, 264):
-            pieces.append((str(j), i, min(264, j + 1058 - i)))
-
-    for key, i, n in pieces:
-        act("ZB", "HT" + key, n, T.HT[:, i:i + n], T.ZB[:, 0:n], AF.Copy)
-
-    def wipe(Q, a, b, behind):
-        for key, i, n in pieces[a:b]:
-            op("G", behind, Q + key, 0.13 + 2 * n * CYC, lambda e, i=i, n=n: e.iota(T[Q][:, i:i + n], [[0, n]], 0, 0, allow_small_or_imprecise_dtypes=True))
-    tabs = {buf: " ".join(buf + str(j) for j in range(0, 8464, 1058)) for buf in ("QA", "QB", "HT")}
+            fill("WH%d%d" % (h, a), 1, T.WH[64 * a:64 * a + 64, 8 + h:9 + h], 2.0 ** (11 * (3 - 2 * h - a)))
+    for t in range(TS):
+        ts("K3", "CO%d" % t, 256, T.CO[:, 256 * t:256 * t + 256], T.K3[:], size[t], Op.mult)
+        ts("WH00 WH01 WH10 WH11", "WT%d" % t, 2, T.WH[:, 2 * t:2 * t + 2], T.WH[:, 8:10], size[t] ** -2, Op.mult)
+    for j in range(0, 8464, 529):
+        fill("Q" + str(j), 265, T.Q[:, j:j + 529], 0.0)
+        iota("HT" + str(j), 529, T.HT[:, j:j + 529], [[0, 529]], 0, 0)
+    tabs = {buf: " ".join(buf + str(j) for j in range(0, 8464, 529)) for buf in ("Q", "HT")}
 
     def hs(h):
         return slice(128 * h, 128 * h + 128)
 
-    def rowsum(src, key0, key1):
-        for h, key in ((0, key0), (1, key1)):
-            u = "pU%d" % h
-            mm("ID NM", u, 128, T[u][:, 0:128], mat("ID"), T.NM[:, 0:128], True, False)
-            mm("BO " + key, u, 128, T[u][:, 0:128], mat("BO"), src[:, hs(h)], False, True)
-            scan("D0 " + u, "UL%d" % h, 128, T.UL[:, hs(h)], T.D0[:, 0:128], T[u][:, 0:128], -8192.0, Op.min, Op.max)
+    def sums(src, key, h):
+        for r in range(4):
+            mm("B%d %s" % (r, key), "pS%d" % h, 32, T["pS%d" % h][:, 0:32], mat("B%d" % r), src[:, 128 * h + r:128 * h + 128:4], r == 0, r == 3)
 
-    SQK = "SQ.0 SQ.1 SQ.2"
-
-    def squares(dst):
-        for m in range(2):
-            act("UL0 UL1", "%s.%d" % (dst, m), 16, T[dst][:, 16 * m:16 * m + 16], T.UL[:, 15::16], AF.Square, bias=2.0 * KAPPA[m], scale=0.25)
-        for m in (2, 3):
-            ts("UL0 UL1", "XQ%d" % m, 16, T.XQ[:, 16 * m - 32:16 * m - 16], T.UL[:, 15::16], 0.25, Op.mult, 2.0 * KAPPA[m], Op.add)
-        tt("XQ2 XQ3", "%s.2" % dst, 64, T[dst][:, 32:64], T.XQ[:], T.XQ[:], Op.mult)
-
-    def vk():
-        for m in range(4):
-            ts("VN", "VK%d" % m, 16, T.VK[:, 16 * m:16 * m + 16], lst("VN"), -4.0 * KAPPA[m] ** 2 - 0.25, Op.add)
+    def pick(bank, a, lhs, key, src, out):
+        mm("ID NM", bank, 256, T[bank][:, a:a + 256], mat("ID"), T.NM[:], True, False)
+        mm(lhs + " " + key, bank, 256, T[bank][:, a:a + 256], mat(lhs), src, False, True)
+        scan("D0 " + bank, out, 256, T[out][:], T.D0[:], T[bank][:, a:a + 256], -8192.0, Op.min, Op.max)
 
     def step(t, b):
-        if b:
-            rowsum(T.Z, "Z0", "Z1")
-            squares("SQ")
-        for h in range(2):
-            src, zk = (T.SD[:, hs(h)], "SD") if b == 0 else (T.Z[:, hs(h)], "Z%d" % h)
-            mm("NI " + zk, "pD%d" % h, 128, T["pD%d" % h][:, 0:128], mat("NI"), src, True, False)
-        tn = "TN%d" % b
-        if b:
-            tt(SQK + " VK0 VK1 VK2 VK3", "XI0 XI1 XI2 XI3", 128, T.XI[:], T.SQ[:], T.VK[:], Op.add)
-        else:
-            for m in range(4):
-                tt("SY%d VN" % m, "XI%d" % m, 32, T.XI[:, 16 * m:16 * m + 16], T.SZ[:, 16 * m:16 * m + 16], lst("VN"), Op.add)
-        ts("XI0 XI1 XI2 XI3", tn, 64, T.TN[:, 64 * b:64 * b + 64], T.XI[:], W - 1, Op.bitwise_and)
-        cp(tn, "OF", 64, T.OF[:], T.TN[:, 64 * b:64 * b + 64])
         for h in range(2):
             boost[0] = AHEAD * (1 - h)
-            look = [T.X[:, 0:W].indirect(T.OF[:, 16 * m + 8 * h:16 * m + 8 * h + 8]) for m in range(4)]
-            y, d = "Y%d." % h, "pD%d" % h
-            ys = [T.Y[:, 256 * m + 128 * h:256 * m + 128 * h + 128] for m in range(4)]
-            if h in SFIRST:
-                act(XK + " OF", y + "0", looks(128), ys[0], look[0], AF.Copy)
-            else:
-                cp(XK + " OF", y + "0", looks(128), ys[0], look[0])
-            for m in range(1, 4):
-                tt("%s OF %s%d" % (XK, y, m - 1), "%s%d" % (y, m), looks(128), ys[m], look[m], ys[m - 1], Op.max)
-            mm("ID %s3" % y, d, 128, T[d][:, 0:128], mat("ID"), ys[3], False, True)
+            s, d, cols = "pS%d" % h, "pD%d" % h, slice(32 * h, 32 * h + 32)
+            src, zk = (T.SD, "SD") if b == 0 else (T.Z, "Z%d" % h)
+            xi, tn, of = "XI%d" % h, "TN%d%d" % (b, h), "OF%d" % h
+            if b:
+                sums(src, zk, h)
+                act(s + " K2K", "SQ%d" % h, 32, quad("SQ", h), T[s][:, 0:32], AF.Square, bias=k2k, scale=0.25)
+                tt("SQ%d VK" % h, xi, 64, T.XI[:, cols], quad("SQ", h), quad("VK", h), Op.add)
+            mm("NI " + zk, d, 128, T[d][:, 0:128], mat("NI"), src[:, hs(h)], True, False)
+            a = 64 * b + 32 * h
+            ts(xi, tn, 32, T.TN[:, a:a + 32], T.XI[:, cols], W - 1, Op.bitwise_and)
+            cp(tn, of, 32, T.OF[:, cols], T.TN[:, a:a + 32])
+            n = 32 - RUN_S[h]
+            keys = []
+            for q, c0, c1 in (("V", 0, n), ("S", n, 32)):
+                if c1 > c0:
+                    keys.append("GR%d%s" % (h, q))
+                    c0, c1 = c0 + 32 * h, c1 + 32 * h
+                    look(q, XK + " " + of, keys[-1], 16 * (c1 - c0), T.GR[:, 16 * c0:16 * c1], T.X[:, 0:W].indirect(T.OF[:, c0:c1]))
+            scan("MK " + " ".join(keys), "H%d" % h, 256, T.H[:, 512 * h:512 * h + 512], T.MK[:], T.GR[:, 512 * h:512 * h + 512], 0.0, Op.mult, Op.max)
+            mm("ID H%d" % h, d, 128, T[d][:, 0:128], mat("ID"), T.H[:, 512 * h + 3:512 * h + 512:4], False, True)
             if b < 3:
                 act(d, "Z%d" % h, 128, T.Z[:, hs(h)], T[d][:, 0:128], AF.Abs)
             else:
                 act(d, "ZF%d.%d" % (t, h), 128, T["ZF%d" % t][:, hs(h)], T[d][:, 0:128], AF.Abs)
         boost[0] = 0.0
-
-    def spread(key, out, src):
-        act(src, key, 16, out[:, 0:16], lst(src), AF.Identity, bias=float(D), scale=-float(D))
-        for n in (16, 32, 64, 128):
-            act(key, key, n, out[:, n:2 * n], out[:, 0:n], AF.Copy)
+        cols, tn = slice(64 * b, 64 * b + 64), "TN%d0 TN%d1" % (b, b)
+        if t == 0:
+            cp(tn, "TR%d" % b, 64, T.TR[:, cols], T.TN[:, cols])
+        else:
+            tt("TR%d NF" % b, "P1%d" % b, 128, T.P1[:, cols], T.TR[:, cols], quad("NF"), Op.max)
+            tt(tn + " FO", "P2%d" % b, 128, T.P2[:, cols], T.TN[:, cols], quad("FO"), Op.max)
+            tt("P1%d P2%d" % (b, b), "TR%d" % b, 128, T.TR[:, cols], T.P2[:, cols], T.P1[:, cols], Op.min)
 
     def halts(t):
         for h in range(2):
             ts("ZF%d.%d TF" % (t, h), "F%d" % h, 64, T.F[:, hs(h)], T["ZF%d" % t][:, hs(h)], T.TF[:, t:t + 1], Op.is_ge)
-        rowsum(T.F, "F0", "F1")
-        tt("UL0 UL1 THR", "HA", 32, T.HA[:], T.UL[:, 15::16], lst("THR"), Op.is_ge)
-        mm("TG HA", "pC", 16, T.pC[:, 0:16], mat("TG"), T.HA[:], True, False)
-        mm("N5 HA", "pC", 16, T.pC[:, 0:16], mat("N5"), T.HA[:], False, False)
-        scan("OB HA", "SC1", 16, T.SC[:, 1:17], T.OB[:, 0:16], T.HA[:], 0.0, Op.mult, Op.add)
-        mm("BO SC0 SC1", "pC", 16, T.pC[:, 0:16], mat("BO"), T.SC[:, 0:16], False, True)
-        ts("pC", "GO", 16, lst("GO"), T.pC[:, 0:16], float(CAP - 512), Op.is_lt)
+            sums(T.F, "F%d" % h, h)
+            tt("pS%d THR" % h, "HA%d" % h, 32, T.HA[:, 32 * h:32 * h + 32], T["pS%d" % h][:, 0:32], quad("THR", h), Op.is_ge)
+        if t:
+            mm("NX FB", "pC", 64, T.pC[:, 0:64], mat("NX"), T.FB[:], True, False)
+        mm("T4 HA0 HA1", "pC", 64, T.pC[:, 0:64], mat("T4"), T.HA[:], t == 0, False)
+        mm("N5 HA0 HA1", "pC", 64, T.pC[:, 0:64], mat("N5"), T.HA[:], False, False)
+        scan("OB HA0 HA1", "SC1", 32, T.SC[:, 1:65], T.OB[:], T.HA[:], 0.0, Op.mult, Op.add)
+        mm("O4 SC0 SC1", "pC", 64, T.pC[:, 0:64], mat("O4"), T.SC[:, 0:64], False, True)
+        ts("pC", "NG", 64, quad("NG"), T.pC[:, 0:64], float(CAP - 512), Op.is_ge, float(D), Op.mult)
+        tt("pC THG", "GO", 64, T.GO[:], T.pC[:, 0:64], quad("THG"), Op.is_lt)
+        for q in range(4):
+            mm("C%d GO" % q, "pS1", 16, T.pS1[:, 64:80], mat("C%d" % q), T.GO[:, q:64:4], q == 0, q == 3)
 
-    def shadows():
+    def shadows(bank, late, sums_, a, b, out, key):
+        mm("ID NK", bank, 256, T[bank][:, 256:512], mat("ID"), T.NK[:], True, False)
         for c in range(16):
-            ts("DV VF GO", "EB%d" % c, (L - 16 * c) // 2, T.EB[:, c, 0:L - 16 * c], T.DV[:, 16 * c:L], part("VF", c, c + 1), Op.is_equal, part("GO", c, c + 1), Op.mult)
+            e, n = T.EB[:, c, 0:L - 16 * c], (L - 16 * c) // 2
+            if late:
+                ts("DV VF pS1", "EB%d" % c, n, e, T.DV[:, 16 * c:L], part("VF", c, c + 1), Op.is_equal, T.pS1[:, 64 + c:65 + c], Op.mult)
+            else:
+                ts("DV VF", "EB%d" % c, n, e, T.DV[:, 16 * c:L], part("VF", c, c + 1), Op.is_equal)
             if c < 15:
-                mm("BK EB%d" % c, "pH", L - 16 - 16 * c, T.pH[:, 272 + 16 * c:512], mat("BK"), T.EB[:, c, 16:L - 16 * c], False, False)
-        mm("TK " + " ".join("EB%d" % c for c in range(16)), "pH", 256, T.pH[:, 256:512], mat("TK"), T.EB[:, :, 0:16], False, True)
+                mm("BK EB%d" % c, bank, L - 16 - 16 * c, T[bank][:, 272 + 16 * c:512], mat("BK"), T.EB[:, c, 16:L - 16 * c], False, False)
+        mm("TK " + " ".join("EB%d" % c for c in range(16)), bank, 256, T[bank][:, 256:512], mat("TK"), T.EB[:, :, 0:16], False, True)
+        scan("D0 " + bank, sums_, 256, T[sums_][:], T.D0[:], T[bank][:, 256:512], -8192.0, Op.min, Op.max)
+        tt(sums_ + " VF", a, 32, lst(a), T[sums_][:, 15::16], lst("VF"), Op.max)
+        tt(a + " DM", b, 32, lst(b), lst(a), lst("DM"), Op.min)
+        cp(b, key, 16, out, lst(b))
 
-    def places():
-        cp("VN", "OV", 16, T.OV[:], lst("VN"))
+    def advance(more):
+        ts("S8 AA", "S7", 16, lst("S7"), lst("S8"), T.AA[:], Op.add)
+        ts("S7", "VN", 16, lst("VN"), lst("S7"), W - 1, Op.bitwise_and)
+        if more:
+            for h in range(2):
+                ts("SB AA", "XI%d" % h, 32, T.XI[:, 32 * h:32 * h + 32], quad("SB", h), T.AA[:], Op.add)
+            ts("BK4 AA", "VK", 64, quad("VK"), quad("BK4"), T.AA[:], Op.add)
+
+    def announce(t):
+        ms = "MS%d" % t
+        cp("VN", ms + "v", 16, T[ms][:, 16:32], lst("VN"))
         cp("VN", "VF", 16, lst("VF"), lst("VN"))
-        cp("OV " + IOK, "DV", looks(256), T.DV[:], T.IO[:].indirect(T.OV[:]))
+        cp(ms + "v " + IOK, "DV", looks(256), T.DV[:], T.IO[:].indirect(T[ms][:, 16:32]))
+        shadows("pC", False, "RUL", "R1", "R2", T[ms][:, 0:16], ms + "r")
+        send(t, "M", T["MR%d" % t][:], T[ms][:], ms + "v " + ms + "r")
+
+    def prepare(t):
+        mr, rk, s = T["MR%d" % t], "recvM%d" % t, size[t]
+        cp("%s CO%d %s" % (rk, t, tabs["Q"]), tabs["Q"], puts(256), T.Q[:, 0:8448].indirect(mr[:, 0:16]), T.CO[:, 256 * t:256 * t + 256])
+        look("S", rk + " " + tabs["Q"], "GQ", 256, T.GQ[:], T.Q[:].indirect(mr[:, 16:32]))
+        ts("GQ PF", "BB", 128, T.BB[:], T.GQ[:], 1.5 * s, Op.is_ge, p, Op.mult)
+        pick("pC", 0, "BO", "BB", T.BB[:], "BUL")
+        cp("BUL", "BL", 16, T.BL[:], T.BUL[:, 15::16])
+        ts("GQ", "A1", 128, T.A1[:], T.GQ[:], s, Op.not_equal, 2.0 ** 46, Op.mult)
+        ts("GQ", "A2", 128, T.A2[:], T.GQ[:], 2 * s, Op.is_equal, 2.0 ** 90, Op.mult)
+        tt("A1 A2", "A3", 512, T.A3[:], T.A1[:], T.A2[:], Op.max)
+        for k in range(4):
+            ts("A3", "TH%d" % k, 32, T.TH[:, 64 * k:64 * k + 64], T.A3[:, 64 * k:64 * k + 64], 1.0, Op.max, 0.75 * 2.0 ** (11 * (3 - k)), Op.mult)
+
+    def widen():
+        ts("S8", "S9", 16, lst("S9"), lst("S8"), W - 1, Op.bitwise_and)
+        cp("S9", "BM", 16, lst("BM"), lst("S9"))
+        for q in range(4):
+            mm("UF%d BM" % q, "pH", 256, T.pH[:, 320 + q:384:4], T.UF[:, 128 * q:128 * q + 128], lst("BM"), True, True)
+        ts("pH KOF", "BK4", 64, quad("BK4"), T.pH[:, 320:384], kof, Op.add)
+        tt("pH SY", "SB", 64, quad("SB"), T.pH[:, 320:384], T.SY[:], Op.add)
 
     def base():
         ts("VC", "S1", 16, lst("S1"), lst("VC"), 4095, Op.bitwise_and)
         tt("S1", "S2", 32, lst("S2"), lst("S1"), lst("S1"), Op.mult)
         ts("S2", "S3", 16, lst("S3"), lst("S2"), 3, Op.arith_shift_right)
         ts("VC", "S4", 16, lst("S4"), lst("VC"), 37.0, Op.mult)
-        tt("S3 S4", "BA", 32, lst("BA"), lst("S4"), lst("S3"), Op.add)
+        tt("S3 S4", "S8", 32, lst("S8"), lst("S4"), lst("S3"), Op.add)
 
     def hits(t, onv):
         mark = 32.0 ** (t + 1 - TS)
         cp("OD OW%d " % t + tabs["HT"], tabs["HT"], puts(256), T.HT[:, 0:8448].indirect(T.OD[:]), T.OW[:, 256 * t:256 * t + 256])
+        mm("ID NM", "pH", 256, T.pH[:, 0:256], mat("ID"), T.NM[:], True, False)
         for k in range(16):
-            hb, b0 = "HB%d" % (k % 8), 256 * (k % 8)
-            src, key = T.HT[:].indirect(T.OM[:, 16 * k:16 * k + 16]), "%s OM" % tabs["HT"]
-            chain[0] = "V" if k in onv else "S"
-            if k in onv:
-                cp(key, hb, looks(256), T.HB[:, b0:b0 + 256], src)
-            else:
-                act(key, hb, looks(256), T.HB[:, b0:b0 + 256], src, AF.Copy)
+            hb, b0, q = "HB%d" % (k % 8), 256 * (k % 8), "V" if k in onv else "S"
+            chain[0] = q
+            look(q, "%s OM%d" % (tabs["HT"], k // 4), hb, 256, T.HB[:, b0:b0 + 256], T.HT[:].indirect(T.OM[:, 16 * k:16 * k + 16]))
             chain[0] = None
-            if k == 0:
-                mm("ID NM", "pH", 256, T.pH[:, 0:256], mat("ID"), T.NM[:], True, False)
-            mm("ID " + hb, "pH", 256, T.pH[:, 0:256], mat("ID"), T.HB[:, b0:b0 + 256], False, k == 15)
+            for m in range(4):
+                mm("ID " + hb, "pH", 64, T.pH[:, 64 * (k % 4):64 * (k % 4) + 64], mat("ID"), T.HB[:, b0 + m:b0 + 256:4], False, k == 15 and m == 3)
         scan("D0 pH", "HUL", 256, T.HUL[:], T.D0[:], T.pH[:, 0:256], -8192.0, Op.min, Op.max)
         tt("FR recvD%d" % t, "FS", 32, lst("FS"), T["DR%d" % t][:], lst("FR"), Op.add)
         if mark != 1.0:
@@ -321,109 +379,90 @@ def rank_program(g, core, T, topo):
         tt("S6 VN", "VC", 32, v, lst("S6"), lst("VN"), Op.add)
 
     def keep():
-        ts("FR", "THR", 16, lst("THR"), lst("FR"), 1000.0, Op.mult, 9.0, Op.add)
-        base()
-        spread("NF", T.NF, "FR")
-        ts("NF", "FO", 128, T.FO[:], T.NF[:], -1.0, Op.mult, float(D), Op.add)
-        tt("TR NF", "P1", 512, T.P1[:], T.TR[:], T.NF[:], Op.max)
+        cp("FR", "F6", 16, T.F6[:], lst("FR"))
+        for q in range(4):
+            mm("U%d F6" % q, "pH", 16, T.pH[:, 256 + q:320:4], mat("U%d" % q), T.F6[:], True, True)
+        fr = T.pH[:, 256:320]
+        ts("pH", "THR", 64, quad("THR"), fr, 1000.0, Op.mult, 9.0, Op.add)
+        ts("pH", "NF", 64, quad("NF"), fr, -float(D), Op.mult, float(D), Op.add)
+        ts("pH", "FO", 64, quad("FO"), fr, float(D), Op.mult)
+        ts("pH", "THG", 64, quad("THG"), fr, -2000.0, Op.mult, float(CAP - 512), Op.add)
+        cp("pH", "FB", 64, T.FB[:], fr)
 
-    cp("V0", "VN", 16, lst("VN"), T.V0[:])
+    for h in range(2):
+        sums(T.SD, "SD", h)
+        act("pS%d K2K" % h, "SQ%d" % h, 32, quad("SQ", h), T["pS%d" % h][:, 0:32], AF.Square, bias=k2k, scale=0.25)
+    ts("SQ0 SQ1 KOF", "SY", 64, T.SY[:], quad("SQ"), kof, Op.add)
     cp("V0", "VC", 16, lst("VC"), T.V0[:])
-    rowsum(T.SD, "SD", "SD")
-    squares("SZ")
-    for m in range(4):
-        ts("SZ.%d" % min(m, 2), "SY%d" % m, 16, T.SZ[:, 16 * m:16 * m + 16], T.SZ[:, 16 * m:16 * m + 16], -4.0 * KAPPA[m] ** 2 - 0.25, Op.add)
+    cp("V0", "S8", 16, lst("S8"), T.V0[:])
+    widen()
+    advance(True)
     base()
+    widen()
 
     for t in range(TS):
         last = t == TS - 1
-        Q = "QA" if t % 2 == 0 else "QB"
         zf = "ZF%d" % t
-        vk()
-        places()
+        announce(t)
         for b in range(4):
             step(t, b)
-        mm("ID NK", "pH", 256, T.pH[:, 256:512], mat("ID"), T.NK[:], True, False)
+        prepare(t)
+        if last:
+            for m in range(4):
+                for q in range(4):
+                    mm("YM%d%d TR0 TR1 TR2 TR3" % (m, q), "pH", 256, T.pH[:, 64 * m:64 * m + 64], T.YM[:, 512 * m + 128 * q:512 * m + 128 * q + 128], T.TR[:, q:256:4], q == 0, q == 3)
+            for m in range(4):
+                act("pH", "YT%d" % m, 64, T.YT[:, :, m, :], T.pH[:, 64 * m:64 * m + 64], AF.Copy)
+            dma("Y", "dy", 32, T.yt[:], T.YT[:], "YT0 YT1 YT2 YT3", "yt")
         halts(t)
-        shadows()
         if not last:
             send(t, "Z", T["ZP%d" % t][:], T[zf][:], zf + ".0 " + zf + ".1")
-        scan("D0 pH", "DUL", 256, T.DUL[:], T.D0[:], T.pH[:, 256:512], -8192.0, Op.min, Op.max)
-        tt("DUL VF", "L1", 32, lst("L1"), T.DUL[:, 15::16], lst("VF"), Op.max)
-        tt("L1 DM", "L2", 32, lst("L2"), lst("L1"), T.DM[:], Op.min)
         lq = "LQ%d" % t
-        cp("L2", lq, 16, T[lq][:], lst("L2"))
+        shadows("pH", True, "DUL", "L1", "L2", T[lq][:], lq)
         send(t, "L", T["RL%d" % t][:], T[lq][:], lq)
-        if t < 3:
-            wipe("QA" if t == 1 else "QB", 0, 16, lq)
-        tn = "TN0 TN1 TN2 TN3"
-        spread("NG", T.NG, "GO")
-        tt(tn + " NG", "M1", 512, T.M1[:], T.TN[:], T.NG[:], Op.max)
-        if t == 0:
-            cp("M1", "OM", 256, T.OM[:], T.M1[:])
-        else:
-            tt("M1 P1", "M2", 512, T.M2[:], T.M1[:], T.P1[:], Op.min)
-            cp("M2", "OM", 256, T.OM[:], T.M2[:])
-        rl = T["RL%d" % t]
-        rk = "recvL%d" % t
-        cp("%s CO %s" % (rk, tabs[Q]), tabs[Q], puts(256), T[Q][:, 0:8448].indirect(rl[:]), T.CO[:])
+        for b in range(4):
+            cols = slice(64 * b, 64 * b + 64)
+            tt("TR%d NG" % b, "M1%d" % b, 128, T.M1[:, cols], T.TR[:, cols], quad("NG"), Op.max)
+            cp("M1%d" % b, "OM%d" % b, 64, T.OM[:, cols], T.M1[:, cols])
+        for k in range(8):
+            n = dict(CLAIM_V).get(k, 0)
+            keys = []
+            for q, c0, c1 in (("V", 0, n), ("S", n, 32)):
+                if c1 > c0:
+                    keys.append("GB%d%s" % (k, q))
+                    c0, c1 = c0 + 32 * k, c1 + 32 * k
+                    look(q, "%s OM%d" % (tabs["Q"], k // 2), keys[-1], 16 * (c1 - c0), T.GB[:, 16 * c0:16 * c1], T.Q[:].indirect(T.OM[:, c0:c1]))
+            pt, a0, h = "pT%d" % (k % 2), 512 * (k % 4), k % 2
+            for m in range(4):
+                op("P", "ID " + " ".join(keys), pt, 128 * CYC, lambda e, m=m, k=k, pt=pt: e.transpose(T[pt][:, 128 * m:128 * m + 128], T.GB[:, 512 * k + m:512 * k + 512:4], mat("ID")))
+            ts("%s WT%d" % (pt, t), "LA%d" % (k % 4), 256, T.LA[:, a0:a0 + 512], T[pt][:, 0:512], T.WH[:, 2 * t + h:2 * t + h + 1], Op.mult)
+            ts(pt, "LB%d" % (k % 4), 256, T.LB[:, a0:a0 + 512], T[pt][:, 0:512], -size[t], Op.add, 0.0, Op.max)
+            for j in range(4):
+                a1 = a0 + 128 * j
+                mm("LA%d LB%d" % (k % 4, k % 4), "pC", 128, T.pC[:, 128:256], T.LA[:, a1:a1 + 128], T.LB[:, a1:a1 + 128], k == 0 and j == 0, k == 7 and j == 3)
+        rl, rk = T["RL%d" % t], "recvL%d" % t
         cp(rk, "LF", 16, lst("LF"), rl[:])
         ts("LF", "IW", 16, lst("IW"), lst("LF"), float(W), Op.is_lt)
-        ts("LF", "LD", 16, lst("LD"), lst("LF"), 1.0 / 16384, Op.mult)
-        if t == 0:
-            cp(tn, "TR", 256, T.TR[:], T.TN[:])
-        else:
-            tt(tn + " FO", "P2", 512, T.P2[:], T.TN[:], T.FO[:], Op.max)
-            tt("P1 P2", "TR", 512, T.TR[:], T.P2[:], T.P1[:], Op.min)
-        if last:
-            dma("Y", "dy", 32, T.yt[:], T.TR[:], "TR", "yt")
-
-        def turn(k):
-            b0, pt, a0 = 512 * k, "pT%d" % (k % 2), 512 * (k % 4)
-            for j in range(4):
-                op("P", "ID GB%d%s" % (k, "aabb"[j]), pt, 128 * CYC, lambda e, j=j: e.transpose(T[pt][:, POS[j]:POS[j] + 128], T.GB[:, b0 + 128 * j:b0 + 128 * j + 128], mat("ID")))
-            for h in range(2):
-                a1 = 256 * h
-                ts("%s WH%d0 WH%d1" % (pt, h, h), "LA%d" % (k % 4), 128, T.LA[:, a0 + a1:a0 + a1 + 256], T[pt][:, a1:a1 + 256], T.WH[:, h:h + 1], Op.mult)
-            ts(pt, "LB%d" % (k % 4), 256, T.LB[:, a0:a0 + 512], T[pt][:, 0:512], -1.0, Op.add, 0.0, Op.max)
-
-        def cells(k):
-            for j in range(4):
-                a0 = 512 * (k % 4) + 128 * j
-                mm("LA%d LB%d" % (k % 4, k % 4), "pC", 128, T.pC[:, 128:256], T.LA[:, a0:a0 + 128], T.LB[:, a0:a0 + 128], k == 0 and j == 0, k == 7 and j == 3)
-        for k in range(8):
-            key = "%s OM" % tabs[Q]
-            if k == 0:
-                cp(key, "GB0a", looks(256), T.GB[:, 0:256], T[Q][:].indirect(T.OM[:, 0:16]))
-                act(key, "GB0b", looks(256), T.GB[:, 256:512], T[Q][:].indirect(T.OM[:, 16:32]), AF.Copy)
-            else:
-                act(key, "GB%da GB%db" % (k, k), looks(512), T.GB[:, 512 * k:512 * k + 512], T[Q][:].indirect(T.OM[:, 32 * k:32 * k + 32]), AF.Copy)
-        for k in range(8):
-            turn(k)
-            cells(k)
-        tt("pC TH", "MC", 128, T.MC[:], T.pC[:, 128:256], T.TH[:], Op.is_ge)
-        tt("MC", "MD", 128, T.MD[:], T.MC[:, 0:64], T.MC[:, 64:128], Op.add)
-        tt("MD", "ME", 64, T.ME[:], T.MD[:, 0:32], T.MD[:, 32:64], Op.add)
-        tt("ME", "MF", 32, T.MF[:], T.ME[:, 0:16], T.ME[:, 16:32], Op.add)
+        cp("pC", "CW", 128, T.CW[:], T.pC[:, 128:256])
+        tt("CW BL TH0 TH1 TH2 TH3", "BD", looks(256), T.BD[:], T.CW[:].indirect(T.BL[:]), T.TH[:], Op.is_ge)
+        pick("pD0", 0, "BK", "BD", T.BD[:], "MUL")
         do = "DO%d" % t
-        tt("MF IW", do, 32, T[do][:], T.MF[:], lst("IW"), Op.is_lt)
+        tt("MUL IW", do, 32, T[do][:], T.MUL[:, 15::16], lst("IW"), Op.is_lt)
         mm("ON " + do, "pC", 16, T.pC[:, 0:16], mat("ON"), T[do][:], True, True)
         send(t, "D", T["DR%d" % t][:], T[do][:], do)
-        tt("LD MF", "E1", 32, lst("E1"), T.MF[:], lst("LD"), Op.max)
-        tt("E1 DS", "E2", 32, lst("E2"), lst("E1"), lst("DS"), Op.min)
-        ts("E2", "OD", 16, T.OD[:], lst("E2"), 16384.0, Op.mult)
+        tt("LF MUL", "E1", 32, lst("E1"), T.MUL[:, 15::16], lst("LF"), Op.max)
+        tt("E1 DM", "E2", 32, lst("E2"), lst("E1"), lst("DM"), Op.min)
+        cp("E2", "OD", 16, T.OD[:], lst("E2"))
         op("V", "pC", "AA", vc(16), lambda e: e.tensor_reduce(T.AA[:], T.pC[:, 0:16], AxisListType.X, Op.add))
         if not last:
             cp("OD recvZ%d" % t, XK, puts(256), T.X[:].indirect(T.OD[:]), T["ZP%d" % t][:])
-        ts("BA AA", "S7", 16, lst("S7"), lst("BA"), T.AA[:], Op.add)
-        ts("S7", "VN", 16, lst("VN"), lst("S7"), W - 1, Op.bitwise_and)
-        if t == 0:
-            wipe("QB", 16, 40, "DO0")
-        if 0 < t < 3:
-            wipe("QA" if t == 1 else "QB", 16, 40, do)
-        hits(t, (1, 3, 5, 7, 9, 11, 13, 15) if last else HITS_ON_VECTOR)
+        advance(not last)
+        hits(t, LAST_V if last else HITS_V)
         if not last:
             keep()
+            base()
+            if t < TS - 2:
+                widen()
     dma("Y", "dy", 32, T.ys[:], T.YS[:], "FR VC", "ys")
 
     N = len(ops)
@@ -472,8 +511,6 @@ def rank_program(g, core, T, topo):
             gap = GAP[ops[i]["chain"]] if ops[i]["chain"] and ops[i]["chain"] == ops[j]["chain"] else 0.0
             best = max(best, wake + ops[i]["lat"] + gap + prio[j])
         prio[i] = best + ops[i]["cost"] + ops[i]["first"]
-        if STIR:
-            prio[i] += STIR * ((i * 7919 + SEED * 104729) * 2654435761 % 4294967296) / 4294967296
     left = [len(preds[i]) for i in range(N)]
     ready = [0.0] * N
     free = {q: 0.0 for q in eng}
@@ -501,13 +538,13 @@ def rank_program(g, core, T, topo):
 
     order += ORDER
     while len(order) < N:
-        pick = None
+        pick_ = None
         for q in "VSPGY":
             if avail[q]:
                 t0 = max(free[q], min(ready[i] for i in avail[q]))
-                if pick is None or t0 < pick[0]:
-                    pick = (t0, q)
-        t0, q = pick
+                if pick_ is None or t0 < pick_[0]:
+                    pick_ = (t0, q)
+        t0, q = pick_
         line[q] = [i for i in line[q] if not over[i]]
         memo, i, wait = {}, None, None
         for c in sorted((c for c in avail[q] if ready[c] <= t0), key=lambda c: -prio[c]):

@@ -3,10 +3,10 @@ from concourse.mybir import AluOpType as Op, AxisListType, ActivationFunctionTyp
 W, L, D = 8192, 256, 8448
 KAPPA = (3, 29, 71, 113)
 TS, CAP = 4, 128
-FL = "L1 L2 R1 R2 LF IW E1 E2 FR FS VF BA BM S4 S5 S6 DM".split()
+FL = "L1 L2 R1 R2 LF IW E1 FR FS VF VG BM0 BM1 S4 S5 S6 DM".split()
 IL = "VN VC S1 S2 S3 S7 S8 S9".split()
-QL = "THR THG NF FO NG VK BK4 SB SQ".split()
-CM = "ID NI N5 NX BO TG ON BK TK T4 O4 B0 B1 B2 B3 C0 C1 C2 C3 U0 U1 U2 U3".split()
+QL = "THR VK BK4 SB SQ".split()
+CM = "ID NI BO TG ON BK TK T4 O4 A0 A1 A2 A3 B0 B1 B2 B3 C0 C1 C2 C3 U0 U1 U2 U3".split()
 
 SCRATCH = {
     "X": ("sbuf", [128, 8448], "bfloat16"),
@@ -17,7 +17,8 @@ SCRATCH = {
     "PI": ("sbuf", [128, 8], "int32"), "PF": ("sbuf", [128, 8], "float32"), "KP": ("sbuf", [128, 16], "float32"),
     "RM": ("sbuf", [128, 256], "float32"), "RD": ("sbuf", [128, 256], "float32"), "RP": ("sbuf", [128, 128], "float32"), "RG": ("sbuf", [128, 128], "float32"),
     "J0": ("sbuf", [128, 128], "float32"), "J1": ("sbuf", [128, 128], "float32"), "J2": ("sbuf", [128, 128], "float32"), "J3": ("sbuf", [128, 128], "float32"),
-    "J4": ("sbuf", [128, 512], "bfloat16"), "MK": ("sbuf", [128, 512], "bfloat16"),
+    "J4": ("sbuf", [128, 640], "bfloat16"), "MK": ("sbuf", [128, 640], "bfloat16"), "OF32": ("sbuf", [128, 128], "float32"), "SL": ("sbuf", [128, 128], "float32"),
+    "NH": ("sbuf", [128, 256], "bfloat16"), "NL": ("sbuf", [128, 256], "bfloat16"), "RL": ("sbuf", [128, 256], "float32"),
     "K1": ("sbuf", [128, 256], "float32"), "K2": ("sbuf", [128, 256], "float32"), "K3": ("sbuf", [128, 256], "float32"), "K4": ("sbuf", [128, 256], "float32"),
     "CM": ("sbuf", [128, 128 * len(CM)], "bfloat16"), "FL": ("sbuf", [128, 16 * len(FL)], "float32"), "IL": ("sbuf", [128, 16 * len(IL)], "int32"),
     "QL": ("sbuf", [128, 64 * len(QL)], "float32"), "UF": ("sbuf", [128, 512], "float32"), "YM": ("sbuf", [128, 2048], "float32"),
@@ -26,12 +27,12 @@ SCRATCH = {
     "WH": ("sbuf", [128, 10], "float32"), "OB": ("sbuf", [128, 64], "bfloat16"),
     "TN": ("sbuf", [128, 256], "int32"), "TR": ("sbuf", [128, 256], "float32"), "P1": ("sbuf", [128, 256], "float32"),
     "P2": ("sbuf", [128, 256], "float32"), "M1": ("sbuf", [128, 256], "float32"), "OM": ("sbuf", [128, 256], "uint16"),
-    "DV": ("sbuf", [128, 256], "uint16"), "OD": ("sbuf", [128, 16], "uint16"), "BL": ("sbuf", [128, 16], "uint16"),
+    "DV0": ("sbuf", [128, 256], "uint16"), "DV1": ("sbuf", [128, 256], "uint16"), "OV": ("sbuf", [128, 16], "uint16"), "EA": ("sbuf", [128, 16, 256], "bfloat16"), "OD": ("sbuf", [128, 16], "uint16"), "BL": ("sbuf", [128, 16], "uint16"),
     "HA": ("sbuf", [128, 64], "bfloat16"), "SC": ("sbuf", [128, 66], "bfloat16"), "GO": ("sbuf", [128, 64], "bfloat16"),
-    "FB": ("sbuf", [128, 64], "bfloat16"), "F6": ("sbuf", [128, 16], "bfloat16"), "SY": ("sbuf", [128, 64], "int32"),
+    "FB": ("sbuf", [128, 64], "bfloat16"), "F6": ("sbuf", [128, 32], "bfloat16"), "SY": ("sbuf", [128, 64], "int32"),
     "EB": ("sbuf", [128, 16, 256], "bfloat16"), "DUL": ("sbuf", [128, 256], "float32"), "HUL": ("sbuf", [128, 256], "float32"),
     "RUL": ("sbuf", [128, 256], "float32"), "BUL": ("sbuf", [128, 256], "float32"), "MUL": ("sbuf", [128, 256], "float32"),
-    "GQ": ("sbuf", [128, 256], "bfloat16"), "A1": ("sbuf", [128, 256], "bfloat16"), "A2": ("sbuf", [128, 256], "bfloat16"), "A3": ("sbuf", [128, 256], "bfloat16"),
+    "GQ": ("sbuf", [128, 256], "bfloat16"), "AB": ("sbuf", [128, 256], "bfloat16"),
     "TH": ("sbuf", [128, 256], "bfloat16"), "BB": ("sbuf", [128, 256], "bfloat16"), "BD": ("sbuf", [128, 256], "bfloat16"), "CW": ("sbuf", [128, 128], "float32"),
     "AA": ("sbuf", [128, 1], "float32"), "YT": ("sbuf", [128, 4, 4, 16], "float32"), "YS": ("sbuf", [128, 32], "float32"),
     "GB": ("sbuf", [128, 4096], "bfloat16"), "HB": ("sbuf", [128, 2048], "bfloat16"), "LA": ("sbuf", [128, 2048], "bfloat16"), "LB": ("sbuf", [128, 2048], "bfloat16"),
@@ -46,14 +47,19 @@ for _t in range(TS):
                     "MS%d" % _t: ("sbuf", [128, 32], "uint16"), "MR%d" % _t: ("sbuf", [128, 32], "uint16")})
 SEMAPHORES = ["cV", "cS", "cP", "cG", "dx", "dv", "ds", "dt", "dy", "loc"] + ["r%s%d" % (k, t) for k in "MLZD" for t in range(TS)]
 CYC, WAKE, SFIX, LOOK, PUT, REMOTE = 0.00083, 0.15, 0.15, 1.56, 3.8, 3.0
-MARGIN = 2
+ROUNDS, SLIP = 12, 0.0
 ORDER = []
-RUN_S = (16, 16)
-CLAIM_V = ((0, 16), (3, 32))
-HITS_V = (4, 9, 14)
+RUN = ((("V", 28), ("S", 18), ("S", 18)),)
+NS = len(RUN)
+CW = 64 // NS
+CLAIM_V = ((0, 16),)
+HITS_V = (1, 3, 5, 8, 10, 12, 14)
 LAST_V = (1, 3, 5, 7, 9, 11, 13, 15)
 GAP = {"S": 0.3, "V": 0.9}
 AHEAD = 0.0
+QV = 4000
+XS = 2
+MX = False
 
 
 def rank_program(g, core, T, topo):
@@ -82,7 +88,7 @@ def rank_program(g, core, T, topo):
         return part(k, 0, 16)
 
     def quad(k, h=None):
-        return part(k, 0, 64) if h is None else part(k, 32 * h, 32 * h + 32)
+        return part(k, 0, 64) if h is None else part(k, CW * h, CW * h + CW)
 
     def mat(k):
         return part(k, 0, 128)
@@ -156,7 +162,8 @@ def rank_program(g, core, T, topo):
     iota("J1", 128, T.J1[:], [[16, 8], [1, 4], [0, 4]], 0, 0)
     iota("J2", 128, T.J2[:], [[1, 8], [1000, 4], [0, 4]], 0, 0)
     iota("J3", 128, T.J3[:], [[0, 8], [1, 4], [0, 4]], 0, 0)
-    iota("J4", 512, T.J4[:], [[0, 128], [1, 4]], 0, 0)
+    iota("J4", 640, T.J4[:], [[0, 160], [1, 4]], 0, 0)
+    iota("RL", 256, T.RL[:], [[1, 256]], 0, 0)
     iota("KI", 4, T.KP[:, 0:4], [[1, 4]], 0, 0)
     for j in range(4):
         iota("IO%d" % j, 512, T.IO[:, 512 * j:512 * j + 512], [[1, 512]], 512 * j, 0)
@@ -183,22 +190,29 @@ def rank_program(g, core, T, topo):
     ts("K4", "D0", 256, T.D0[:], T.K4[:], 32768.0, Op.add)
     ts("RP PF", "ID", 128, mat("ID"), T.RP[:], p, Op.is_equal)
     ts("ID", "NI", 64, mat("NI"), mat("ID"), -1.0, Op.mult)
-    ts("ID", "N5", 64, mat("N5"), mat("ID"), -512.0, Op.mult)
-    ts("ID", "NX", 64, mat("NX"), mat("ID"), -1024.0, Op.mult)
     ts("RM PF", "K1", 256, T.K1[:], T.RM[:], pi, Op.is_equal)
     ts("RM PF", "K2", 128, T.K2[:, 0:128], T.RM[:, 0:128], pi, Op.is_gt)
     tt("K2 BO", "TG", 256, mat("TG"), T.K2[:, 0:128], mat("BO"), Op.mult)
-    ts("J4", "MK", 256, T.MK[:], T.J4[:], 1.0, Op.min)
+    ts("J4", "MK", 320, T.MK[:], T.J4[:], 1.0, Op.min)
+    fill("OF32", 128, T.OF32[:], 1.0)
     for r in range(4):
         ts("J2 PF", "B%d" % r, 128, mat("B%d" % r), T.J2[:], pg, Op.subtract, 1000.0 * r, Op.is_equal)
+        ts("B%d" % r, "A%d" % r, 64, mat("A%d" % r), mat("B%d" % r), -0.5, Op.mult)
         ts("J0 PF", "C%d" % r, 128, mat("C%d" % r), T.J0[:], p, Op.subtract, 1000.0 * r, Op.is_equal)
         ts("J1 PF", "UF%d" % r, 128, T.UF[:, 128 * r:128 * r + 128], T.J1[:], p, Op.subtract, -4.0 * r, Op.is_equal)
-        cp("UF%d" % r, "U%d" % r, 128, mat("U%d" % r), T.UF[:, 128 * r:128 * r + 128])
+        ts("UF%d" % r, "U%d" % r, 128, mat("U%d" % r), T.UF[:, 128 * r:128 * r + 128], float(D), Op.mult)
         for m in range(4):
-            ts("J0 PF", "YM%d%d" % (m, r), 128, T.YM[:, 512 * m + 128 * r:512 * m + 128 * r + 128], T.J0[:], p, Op.subtract, 1000.0 * r - m, Op.is_equal)
-    ts("J3 PF", "J3", 128, T.J3[:], T.J3[:], pr, Op.is_gt, 0.25, Op.mult)
-    tt("J3 BO", "T4", 256, mat("T4"), T.J3[:], mat("BO"), Op.mult)
-    ts("BO", "O4", 64, mat("O4"), mat("BO"), 0.25, Op.mult)
+            op("G", "OF32", "YM%d%d" % (m, r), 0.17 + 256 * CYC, lambda e, m=m, r=r: e.affine_select(
+                T.YM[:, 512 * m + 128 * r:512 * m + 128 * r + 128], T.OF32[:], [[16, 8], [1000, 4], [4, 4]], Op.is_equal, 0.0, m - 1000 * r, -1))
+    ts("J3 PF", "J3", 128, T.J3[:], T.J3[:], pr, Op.is_gt, 8192.0, Op.mult)
+    tt("J3 BO", "J3", 256, T.J3[:], T.J3[:], mat("BO"), Op.mult)
+    ts("ID", "O4", 64, mat("O4"), mat("ID"), -32768.0 * CAP, Op.mult)
+    tt("J3 O4", "T4", 256, mat("T4"), T.J3[:], mat("O4"), Op.add)
+    ts("BO", "O4", 64, mat("O4"), mat("BO"), 8192.0, Op.mult)
+    ts("K1", "NH", 256, T.NH[:], T.K1[:], float(2 ** 24 + W - 32768), Op.mult, -float(2 ** 24), Op.add)
+    tt("K1 RL", "NL", 512, T.NL[:], T.K1[:], T.RL[:], Op.mult)
+    ts("K1", "SL", 128, T.SL[:], T.K1[:, 0:128], -2.0 ** -46, Op.mult, 2.0 ** -46, Op.add)
+    ts("SL", "SL", 128, T.SL[:], T.SL[:], 2.0 ** -92, Op.max)
     ts("BO", "BK", 64, mat("BK"), mat("BO"), 32768.0, Op.mult)
     ts("ID", "KA", 128, T.KA[:, 0:128], mat("ID"), -16384.0, Op.mult)
     ts("TG", "KB", 128, T.KA[:, 128:256], mat("TG"), 32768.0, Op.mult)
@@ -212,7 +226,7 @@ def rank_program(g, core, T, topo):
     fill("ON", 64, mat("ON"), 1.0)
     fill("SC0", 1, T.SC[:, 0:1], 0.0)
     fill("THR", 64, quad("THR"), 9.0)
-    fill("THG", 64, quad("THG"), float(CAP - 512))
+    fill("FB", 32, T.FB[:], 16384.0)
     fill("FR", 16, lst("FR"), 0.0)
     fill("AA", 1, T.AA[:], 0.0)
     cp("TI", "TF", 4, T.TF[:], T.TI[:])
@@ -229,87 +243,111 @@ def rank_program(g, core, T, topo):
         ts("K3", "CO%d" % t, 256, T.CO[:, 256 * t:256 * t + 256], T.K3[:], size[t], Op.mult)
         ts("WH00 WH01 WH10 WH11", "WT%d" % t, 2, T.WH[:, 2 * t:2 * t + 2], T.WH[:, 8:10], size[t] ** -2, Op.mult)
     for j in range(0, 8464, 529):
-        fill("Q" + str(j), 265, T.Q[:, j:j + 529], 0.0)
+        if j < QV:
+            fill("Q" + str(j), 265, T.Q[:, j:j + 529], 0.0)
+        else:
+            iota("Q" + str(j), 529, T.Q[:, j:j + 529], [[0, 529]], 0, 0)
         iota("HT" + str(j), 529, T.HT[:, j:j + 529], [[0, 529]], 0, 0)
     tabs = {buf: " ".join(buf + str(j) for j in range(0, 8464, 529)) for buf in ("Q", "HT")}
 
     def hs(h):
-        return slice(128 * h, 128 * h + 128)
+        return slice(4 * CW * h, 4 * CW * h + 4 * CW)
 
-    def sums(src, key, h):
+    def both(k):
+        return " ".join(k + str(h) for h in range(NS))
+
+    def sums(m, src, key, h, first, final):
         for r in range(4):
-            mm("B%d %s" % (r, key), "pS%d" % h, 32, T["pS%d" % h][:, 0:32], mat("B%d" % r), src[:, 128 * h + r:128 * h + 128:4], r == 0, r == 3)
+            mm("%s%d %s" % (m, r, key), "pS%d" % h, CW, T["pS%d" % h][:, 0:CW], mat("%s%d" % (m, r)), src(slice(4 * CW * h + r, 4 * CW * h + 4 * CW, 4)), first and r == 0, final and r == 3)
 
-    def pick(bank, a, lhs, key, src, out):
-        mm("ID NM", bank, 256, T[bank][:, a:a + 256], mat("ID"), T.NM[:], True, False)
+    def pick(bank, a, lhs, key, src, out, under):
+        for k in under:
+            mm("ID " + k, bank, 256, T[bank][:, a:a + 256], mat("ID"), T[k][:], k == under[0], False)
         mm(lhs + " " + key, bank, 256, T[bank][:, a:a + 256], mat(lhs), src, False, True)
         scan("D0 " + bank, out, 256, T[out][:], T.D0[:], T[bank][:, a:a + 256], -8192.0, Op.min, Op.max)
 
     def step(t, b):
-        for h in range(2):
+        for h in range(NS):
             boost[0] = AHEAD * (1 - h)
-            s, d, cols = "pS%d" % h, "pD%d" % h, slice(32 * h, 32 * h + 32)
-            src, zk = (T.SD, "SD") if b == 0 else (T.Z, "Z%d" % h)
+            s, d, cols = "pS%d" % h, "pD%d" % h, slice(CW * h, CW * h + CW)
+            Z, zk = (T.SD, "SD") if b == 0 else (T.Z, "Z%d" % h)
             xi, tn, of = "XI%d" % h, "TN%d%d" % (b, h), "OF%d" % h
             if b:
-                sums(src, zk, h)
-                act(s + " K2K", "SQ%d" % h, 32, quad("SQ", h), T[s][:, 0:32], AF.Square, bias=k2k, scale=0.25)
-                tt("SQ%d VK" % h, xi, 64, T.XI[:, cols], quad("SQ", h), quad("VK", h), Op.add)
-            mm("NI " + zk, d, 128, T[d][:, 0:128], mat("NI"), src[:, hs(h)], True, False)
-            a = 64 * b + 32 * h
-            ts(xi, tn, 32, T.TN[:, a:a + 32], T.XI[:, cols], W - 1, Op.bitwise_and)
-            cp(tn, of, 32, T.OF[:, cols], T.TN[:, a:a + 32])
-            n = 32 - RUN_S[h]
-            keys = []
-            for q, c0, c1 in (("V", 0, n), ("S", n, 32)):
-                if c1 > c0:
-                    keys.append("GR%d%s" % (h, q))
-                    c0, c1 = c0 + 32 * h, c1 + 32 * h
-                    look(q, XK + " " + of, keys[-1], 16 * (c1 - c0), T.GR[:, 16 * c0:16 * c1], T.X[:, 0:W].indirect(T.OF[:, c0:c1]))
-            scan("MK " + " ".join(keys), "H%d" % h, 256, T.H[:, 512 * h:512 * h + 512], T.MK[:], T.GR[:, 512 * h:512 * h + 512], 0.0, Op.mult, Op.max)
-            mm("ID H%d" % h, d, 128, T[d][:, 0:128], mat("ID"), T.H[:, 512 * h + 3:512 * h + 512:4], False, True)
+                tt("SQ%d VK" % h, xi, 2 * CW, T.XI[:, cols], quad("SQ", h), quad("VK", h), Op.add)
+            mm("NI " + zk, d, 4 * CW, T[d][:, 0:4 * CW], mat("NI"), Z[:, hs(h)], True, False)
+            if b < 3 and MX:
+                sums("A", lambda l: Z[:, l], zk, h, True, False)
+            a = 64 * b + CW * h
+            ts(xi, tn, CW, T.TN[:, a:a + CW], T.XI[:, cols], W - 1, Op.bitwise_and)
+            cp(tn, of, CW, T.OF[:, cols], T.TN[:, a:a + CW])
+            c0, hk, mk = CW * h, "", ""
+            for j, (q, n) in enumerate(RUN[h]):
+                key, lanes, four = "%d.%d" % (h, j), slice(4 * c0, 4 * c0 + 4 * n), slice(16 * c0, 16 * c0 + 16 * n)
+                look(q, XK + " " + of, "GR" + key, 16 * n, T.GR[:, four], T.X[:, 0:W].indirect(T.OF[:, c0:c0 + n]))
+                scan("MK GR" + key, "H" + key, 8 * n, T.H[:, four], T.MK[:, 0:16 * n], T.GR[:, four], 0.0, Op.mult, Op.max)
+                if b < 3 and MX:
+                    tt("H%s %s" % (key, zk), "MX" + key, 8 * n, T.MX[:, lanes], T.H[:, 16 * c0 + 3:16 * c0 + 16 * n:4], Z[:, lanes], Op.max)
+                c0, hk, mk = c0 + n, hk + " H" + key, mk + " MX" + key
+            if b < 3 and MX:
+                sums("A", lambda l: T.H[:, 4 * l.start + 3:4 * l.stop:16], hk, h, False, False)
+                sums("B", lambda l: T.MX[:, l], mk, h, False, True)
+                act(s + " K2K", "SQ%d" % h, CW, quad("SQ", h), T[s][:, 0:CW], AF.Square, bias=k2k, scale=0.5)
+            mm("ID " + hk, d, 4 * CW, T[d][:, 0:4 * CW], mat("ID"), T.H[:, 16 * CW * h + 3:16 * CW * h + 16 * CW:4], False, True)
             if b < 3:
-                act(d, "Z%d" % h, 128, T.Z[:, hs(h)], T[d][:, 0:128], AF.Abs)
+                act(d, "Z%d" % h, 4 * CW, T.Z[:, hs(h)], T[d][:, 0:4 * CW], AF.Abs)
+                if not MX:
+                    sums("B", lambda l: T.Z[:, l], "Z%d" % h, h, True, True)
+                    act(s + " K2K", "SQ%d" % h, CW, quad("SQ", h), T[s][:, 0:CW], AF.Square, bias=k2k, scale=0.25)
             else:
-                act(d, "ZF%d.%d" % (t, h), 128, T["ZF%d" % t][:, hs(h)], T[d][:, 0:128], AF.Abs)
+                act(d, "ZF%d.%d" % (t, h), 4 * CW, T["ZF%d" % t][:, hs(h)], T[d][:, 0:4 * CW], AF.Abs)
         boost[0] = 0.0
-        cols, tn = slice(64 * b, 64 * b + 64), "TN%d0 TN%d1" % (b, b)
+
+    def trails(t, b):
+        cols, tn = slice(64 * b, 64 * b + 64), both("TN%d" % b)
         if t == 0:
             cp(tn, "TR%d" % b, 64, T.TR[:, cols], T.TN[:, cols])
         else:
-            tt("TR%d NF" % b, "P1%d" % b, 128, T.P1[:, cols], T.TR[:, cols], quad("NF"), Op.max)
-            tt(tn + " FO", "P2%d" % b, 128, T.P2[:, cols], T.TN[:, cols], quad("FO"), Op.max)
+            tt("TR%d pH" % b, "P1%d" % b, 64, T.P1[:, cols], T.pH[:, 320:384], T.TR[:, cols], Op.max)
+            tt(tn + " pH", "P2%d" % b, 64, T.P2[:, cols], T.pH[:, 256:320], T.TN[:, cols], Op.max)
             tt("P1%d P2%d" % (b, b), "TR%d" % b, 128, T.TR[:, cols], T.P2[:, cols], T.P1[:, cols], Op.min)
 
     def halts(t):
-        for h in range(2):
-            ts("ZF%d.%d TF" % (t, h), "F%d" % h, 64, T.F[:, hs(h)], T["ZF%d" % t][:, hs(h)], T.TF[:, t:t + 1], Op.is_ge)
-            sums(T.F, "F%d" % h, h)
-            tt("pS%d THR" % h, "HA%d" % h, 32, T.HA[:, 32 * h:32 * h + 32], T["pS%d" % h][:, 0:32], quad("THR", h), Op.is_ge)
-        if t:
-            mm("NX FB", "pC", 64, T.pC[:, 0:64], mat("NX"), T.FB[:], True, False)
-        mm("T4 HA0 HA1", "pC", 64, T.pC[:, 0:64], mat("T4"), T.HA[:], t == 0, False)
-        mm("N5 HA0 HA1", "pC", 64, T.pC[:, 0:64], mat("N5"), T.HA[:], False, False)
-        scan("OB HA0 HA1", "SC1", 32, T.SC[:, 1:65], T.OB[:], T.HA[:], 0.0, Op.mult, Op.add)
-        mm("O4 SC0 SC1", "pC", 64, T.pC[:, 0:64], mat("O4"), T.SC[:, 0:64], False, True)
-        ts("pC", "NG", 64, quad("NG"), T.pC[:, 0:64], float(CAP - 512), Op.is_ge, float(D), Op.mult)
-        tt("pC THG", "GO", 64, T.GO[:], T.pC[:, 0:64], quad("THG"), Op.is_lt)
+        for h in range(NS):
+            ts("ZF%d.%d TF" % (t, h), "F%d" % h, 2 * CW, T.F[:, hs(h)], T["ZF%d" % t][:, hs(h)], T.TF[:, t:t + 1], Op.is_ge)
+            sums("B", lambda l: T.F[:, l], "F%d" % h, h, True, True)
+            tt("pS%d THR" % h, "HA%d" % h, CW, T.HA[:, CW * h:CW * h + CW], T["pS%d" % h][:, 0:CW], quad("THR", h), Op.is_ge)
+        ha = both("HA")
         for q in range(4):
-            mm("C%d GO" % q, "pS1", 16, T.pS1[:, 64:80], mat("C%d" % q), T.GO[:, q:64:4], q == 0, q == 3)
+            mm("C%d %s" % (q, ha), "pS1", 16, T.pS1[:, 64:80], mat("C%d" % q), T.HA[:, q:64:4], q == 0, q == 3)
+        mm("ID FB", "pC", 64, T.pC[:, 0:64], mat("ID"), T.FB[:], True, False)
+        mm("T4 " + ha, "pC", 64, T.pC[:, 0:64], mat("T4"), T.HA[:], False, False)
+        scan("OB " + ha, "SC1", 32, T.SC[:, 1:65], T.OB[:], T.HA[:], 0.0, Op.mult, Op.add)
+        mm("O4 SC0 SC1", "pC", 64, T.pC[:, 0:64], mat("O4"), T.SC[:, 0:64], False, True)
+        for b in range(4):
+            cols = slice(64 * b, 64 * b + 64)
+            tt("TR%d pC" % b, "M1%d" % b, 64, T.M1[:, cols], T.pC[:, 0:64], T.TR[:, cols], Op.max)
+            ts("M1%d" % b, "OM%d" % b, 64, T.OM[:, cols], T.M1[:, cols], float(D), Op.min)
+        cp("pC", "GO", 64, T.GO[:], T.pC[:, 0:64])
+        for q in range(4):
+            mm("C%d GO" % q, "pS0", 16, T.pS0[:, 64:80], mat("C%d" % q), T.GO[:, q:64:4], q == 0, q == 3)
+        tt("pS0 VF", "VG", 16, lst("VG"), T.pS0[:, 64:80], lst("VF"), Op.max)
 
-    def shadows(bank, late, sums_, a, b, out, key):
+    def shadows(t, bank, late, out):
+        dv, bm, eb = "DV%d" % (t % 2), "BM%d" % (t % 2), "EB" if late else "EA"
         mm("ID NK", bank, 256, T[bank][:, 256:512], mat("ID"), T.NK[:], True, False)
         for c in range(16):
-            e, n = T.EB[:, c, 0:L - 16 * c], (L - 16 * c) // 2
+            e, n = T[eb][:, c, 0:L - 16 * c], (L - 16 * c) // 2
             if late:
-                ts("DV VF pS1", "EB%d" % c, n, e, T.DV[:, 16 * c:L], part("VF", c, c + 1), Op.is_equal, T.pS1[:, 64 + c:65 + c], Op.mult)
+                ts("%s %s pS1" % (dv, bm), eb + str(c), n, e, T[dv][:, 16 * c:L], part(bm, c, c + 1), Op.is_equal, T.pS1[:, 64 + c:65 + c], Op.mult)
             else:
-                ts("DV VF", "EB%d" % c, n, e, T.DV[:, 16 * c:L], part("VF", c, c + 1), Op.is_equal)
+                ts(dv + " " + bm, eb + str(c), n, e, T[dv][:, 16 * c:L], part(bm, c, c + 1), Op.is_equal)
             if c < 15:
-                mm("BK EB%d" % c, bank, L - 16 - 16 * c, T[bank][:, 272 + 16 * c:512], mat("BK"), T.EB[:, c, 16:L - 16 * c], False, False)
-        mm("TK " + " ".join("EB%d" % c for c in range(16)), bank, 256, T[bank][:, 256:512], mat("TK"), T.EB[:, :, 0:16], False, True)
-        scan("D0 " + bank, sums_, 256, T[sums_][:], T.D0[:], T[bank][:, 256:512], -8192.0, Op.min, Op.max)
-        tt(sums_ + " VF", a, 32, lst(a), T[sums_][:, 15::16], lst("VF"), Op.max)
+                mm("BK %s%d" % (eb, c), bank, L - 16 - 16 * c, T[bank][:, 272 + 16 * c:512], mat("BK"), T[eb][:, c, 16:L - 16 * c], False, False)
+        mm("TK " + " ".join(eb + str(c) for c in range(16)), bank, 256, T[bank][:, 256:512], mat("TK"), T[eb][:, :, 0:16], False, True)
+        scan("D0 " + bank, out, 256, T[out][:], T.D0[:], T[bank][:, 256:512], -8192.0, Op.min, Op.max)
+
+    def listed(sums_, v, a, b, out, key):
+        tt(sums_ + " " + v, a, 32, lst(a), T[sums_][:, 15::16], lst(v), Op.max)
         tt(a + " DM", b, 32, lst(b), lst(a), lst("DM"), Op.min)
         cp(b, key, 16, out, lst(b))
 
@@ -317,16 +355,14 @@ def rank_program(g, core, T, topo):
         ts("S8 AA", "S7", 16, lst("S7"), lst("S8"), T.AA[:], Op.add)
         ts("S7", "VN", 16, lst("VN"), lst("S7"), W - 1, Op.bitwise_and)
         if more:
-            for h in range(2):
-                ts("SB AA", "XI%d" % h, 32, T.XI[:, 32 * h:32 * h + 32], quad("SB", h), T.AA[:], Op.add)
+            ts("SB AA", both("XI"), 64, T.XI[:], quad("SB"), T.AA[:], Op.add)
             ts("BK4 AA", "VK", 64, quad("VK"), quad("BK4"), T.AA[:], Op.add)
 
     def announce(t):
         ms = "MS%d" % t
         cp("VN", ms + "v", 16, T[ms][:, 16:32], lst("VN"))
         cp("VN", "VF", 16, lst("VF"), lst("VN"))
-        cp(ms + "v " + IOK, "DV", looks(256), T.DV[:], T.IO[:].indirect(T[ms][:, 16:32]))
-        shadows("pC", False, "RUL", "R1", "R2", T[ms][:, 0:16], ms + "r")
+        listed("RUL", "VF", "R1", "R2", T[ms][:, 0:16], ms + "r")
         send(t, "M", T["MR%d" % t][:], T[ms][:], ms + "v " + ms + "r")
 
     def prepare(t):
@@ -334,21 +370,22 @@ def rank_program(g, core, T, topo):
         cp("%s CO%d %s" % (rk, t, tabs["Q"]), tabs["Q"], puts(256), T.Q[:, 0:8448].indirect(mr[:, 0:16]), T.CO[:, 256 * t:256 * t + 256])
         look("S", rk + " " + tabs["Q"], "GQ", 256, T.GQ[:], T.Q[:].indirect(mr[:, 16:32]))
         ts("GQ PF", "BB", 128, T.BB[:], T.GQ[:], 1.5 * s, Op.is_ge, p, Op.mult)
-        pick("pC", 0, "BO", "BB", T.BB[:], "BUL")
+        pick("pC", 0, "BO", "BB", T.BB[:], "BUL", ["NM"])
         cp("BUL", "BL", 16, T.BL[:], T.BUL[:, 15::16])
-        ts("GQ", "A1", 128, T.A1[:], T.GQ[:], s, Op.not_equal, 2.0 ** 46, Op.mult)
-        ts("GQ", "A2", 128, T.A2[:], T.GQ[:], 2 * s, Op.is_equal, 2.0 ** 90, Op.mult)
-        tt("A1 A2", "A3", 512, T.A3[:], T.A1[:], T.A2[:], Op.max)
+        act("GQ", "AB", 256, T.AB[:], T.GQ[:], AF.Abs, bias=-s)
         for k in range(4):
-            ts("A3", "TH%d" % k, 32, T.TH[:, 64 * k:64 * k + 64], T.A3[:, 64 * k:64 * k + 64], 1.0, Op.max, 0.75 * 2.0 ** (11 * (3 - k)), Op.mult)
+            ts("AB", "TH%d" % k, 32, T.TH[:, 64 * k:64 * k + 64], T.AB[:, 64 * k:64 * k + 64], s, Op.is_equal, 0.75 * 2.0 ** (11 * (3 - k) - 46), Op.max)
 
-    def widen():
+    def widen(t):
+        bm, dv = "BM%d" % (t % 2), "DV%d" % (t % 2)
         ts("S8", "S9", 16, lst("S9"), lst("S8"), W - 1, Op.bitwise_and)
-        cp("S9", "BM", 16, lst("BM"), lst("S9"))
+        cp("S9", bm, 16, lst(bm), lst("S9"))
         for q in range(4):
-            mm("UF%d BM" % q, "pH", 256, T.pH[:, 320 + q:384:4], T.UF[:, 128 * q:128 * q + 128], lst("BM"), True, True)
-        ts("pH KOF", "BK4", 64, quad("BK4"), T.pH[:, 320:384], kof, Op.add)
-        tt("pH SY", "SB", 64, quad("SB"), T.pH[:, 320:384], T.SY[:], Op.add)
+            mm("UF%d %s" % (q, bm), "pS1", 256, T.pS1[:, 384 + q:448:4], T.UF[:, 128 * q:128 * q + 128], lst(bm), True, True)
+        ts("pS1 KOF", "BK4", 64, quad("BK4"), T.pS1[:, 384:448], kof, Op.add)
+        tt("pS1 SY", "SB", 64, quad("SB"), T.pS1[:, 384:448], T.SY[:], Op.add)
+        cp("S9", "OV", 16, T.OV[:], lst("S9"))
+        cp("OV " + IOK, dv, looks(256), T[dv][:], T.IO[:].indirect(T.OV[:]))
 
     def base():
         ts("VC", "S1", 16, lst("S1"), lst("VC"), 4095, Op.bitwise_and)
@@ -363,7 +400,7 @@ def rank_program(g, core, T, topo):
         mm("ID NM", "pH", 256, T.pH[:, 0:256], mat("ID"), T.NM[:], True, False)
         for k in range(16):
             hb, b0, q = "HB%d" % (k % 8), 256 * (k % 8), "V" if k in onv else "S"
-            chain[0] = q
+            chain[0] = None
             look(q, "%s OM%d" % (tabs["HT"], k // 4), hb, 256, T.HB[:, b0:b0 + 256], T.HT[:].indirect(T.OM[:, 16 * k:16 * k + 16]))
             chain[0] = None
             for m in range(4):
@@ -379,26 +416,22 @@ def rank_program(g, core, T, topo):
         tt("S6 VN", "VC", 32, v, lst("S6"), lst("VN"), Op.add)
 
     def keep():
-        cp("FR", "F6", 16, T.F6[:], lst("FR"))
+        tt("HUL FS", "F6", 32, T.F6[:, 0:16], T.HUL[:, 15::16], lst("FS"), Op.is_lt)
+        tt("HUL FS", "F7", 32, T.F6[:, 16:32], T.HUL[:, 15::16], lst("FS"), Op.is_ge)
         for q in range(4):
-            mm("U%d F6" % q, "pH", 16, T.pH[:, 256 + q:320:4], mat("U%d" % q), T.F6[:], True, True)
-        fr = T.pH[:, 256:320]
-        ts("pH", "THR", 64, quad("THR"), fr, 1000.0, Op.mult, 9.0, Op.add)
-        ts("pH", "NF", 64, quad("NF"), fr, -float(D), Op.mult, float(D), Op.add)
-        ts("pH", "FO", 64, quad("FO"), fr, float(D), Op.mult)
-        ts("pH", "THG", 64, quad("THG"), fr, -2000.0, Op.mult, float(CAP - 512), Op.add)
-        cp("pH", "FB", 64, T.FB[:], fr)
+            mm("U%d F6 F7" % q, "pH", 32, T.pH[:, 256 + q:384:4], mat("U%d" % q), T.F6[:], True, True)
+        ts("pH", "THR", 64, quad("THR"), T.pH[:, 256:320], 9.0, Op.add)
+        ts("pH", "FB", 64, T.FB[:], T.pH[:, 256:320], -131072.0, Op.mult, 16384.0, Op.add)
 
-    for h in range(2):
-        sums(T.SD, "SD", h)
-        act("pS%d K2K" % h, "SQ%d" % h, 32, quad("SQ", h), T["pS%d" % h][:, 0:32], AF.Square, bias=k2k, scale=0.25)
-    ts("SQ0 SQ1 KOF", "SY", 64, T.SY[:], quad("SQ"), kof, Op.add)
+    for h in range(NS):
+        sums("B", lambda l: T.SD[:, l], "SD", h, True, True)
+        act("pS%d K2K" % h, "SQ%d" % h, CW, quad("SQ", h), T["pS%d" % h][:, 0:CW], AF.Square, bias=k2k, scale=0.25)
+    ts(both("SQ") + " KOF", "SY", 64, T.SY[:], quad("SQ"), kof, Op.add)
     cp("V0", "VC", 16, lst("VC"), T.V0[:])
     cp("V0", "S8", 16, lst("S8"), T.V0[:])
-    widen()
+    widen(0)
+    shadows(0, "pC", False, "RUL")
     advance(True)
-    base()
-    widen()
 
     for t in range(TS):
         last = t == TS - 1
@@ -406,24 +439,27 @@ def rank_program(g, core, T, topo):
         announce(t)
         for b in range(4):
             step(t, b)
+        base()
+        for b in range(4):
+            trails(t, b)
         prepare(t)
+        halts(t)
+        if not last:
+            send(t, "Z", T["ZP%d" % t][:], T[zf][:], both(zf + "."))
+        lq = "LQ%d" % t
+        shadows(t, "pH", True, "DUL")
+        listed("DUL", "VG", "L1", "L2", T[lq][:], lq)
+        send(t, "L", T["RL%d" % t][:], T[lq][:], lq)
         if last:
             for m in range(4):
                 for q in range(4):
-                    mm("YM%d%d TR0 TR1 TR2 TR3" % (m, q), "pH", 256, T.pH[:, 64 * m:64 * m + 64], T.YM[:, 512 * m + 128 * q:512 * m + 128 * q + 128], T.TR[:, q:256:4], q == 0, q == 3)
+                    mm("YM%d%d TR0 TR1 TR2 TR3" % (m, q), "pC", 256, T.pC[:, 64 * m:64 * m + 64], T.YM[:, 512 * m + 128 * q:512 * m + 128 * q + 128], T.TR[:, q:256:4], q == 0, q == 3)
             for m in range(4):
-                act("pH", "YT%d" % m, 64, T.YT[:, :, m, :], T.pH[:, 64 * m:64 * m + 64], AF.Copy)
+                act("pC", "YT%d" % m, 64, T.YT[:, :, m, :], T.pC[:, 64 * m:64 * m + 64], AF.Copy)
             dma("Y", "dy", 32, T.yt[:], T.YT[:], "YT0 YT1 YT2 YT3", "yt")
-        halts(t)
-        if not last:
-            send(t, "Z", T["ZP%d" % t][:], T[zf][:], zf + ".0 " + zf + ".1")
-        lq = "LQ%d" % t
-        shadows("pH", True, "DUL", "L1", "L2", T[lq][:], lq)
-        send(t, "L", T["RL%d" % t][:], T[lq][:], lq)
-        for b in range(4):
-            cols = slice(64 * b, 64 * b + 64)
-            tt("TR%d NG" % b, "M1%d" % b, 128, T.M1[:, cols], T.TR[:, cols], quad("NG"), Op.max)
-            cp("M1%d" % b, "OM%d" % b, 64, T.OM[:, cols], T.M1[:, cols])
+        else:
+            widen(t + 1)
+            shadows(t + 1, "pC", False, "RUL")
         for k in range(8):
             n = dict(CLAIM_V).get(k, 0)
             keys = []
@@ -439,30 +475,28 @@ def rank_program(g, core, T, topo):
             ts(pt, "LB%d" % (k % 4), 256, T.LB[:, a0:a0 + 512], T[pt][:, 0:512], -size[t], Op.add, 0.0, Op.max)
             for j in range(4):
                 a1 = a0 + 128 * j
-                mm("LA%d LB%d" % (k % 4, k % 4), "pC", 128, T.pC[:, 128:256], T.LA[:, a1:a1 + 128], T.LB[:, a1:a1 + 128], k == 0 and j == 0, k == 7 and j == 3)
+                mm("LA%d LB%d" % (k % 4, k % 4), "pD1", 128, T.pD1[:, 128:256], T.LA[:, a1:a1 + 128], T.LB[:, a1:a1 + 128], k == 0 and j == 0, k == 7 and j == 3)
         rl, rk = T["RL%d" % t], "recvL%d" % t
         cp(rk, "LF", 16, lst("LF"), rl[:])
-        ts("LF", "IW", 16, lst("IW"), lst("LF"), float(W), Op.is_lt)
-        cp("pC", "CW", 128, T.CW[:], T.pC[:, 128:256])
+        ts(rk, "IW", 16, lst("IW"), rl[:], float(W), Op.is_ge, -65536.0, Op.mult)
+        tt("pD1 SL", "CW", 128, T.CW[:], T.pD1[:, 128:256], T.SL[:], Op.mult)
         tt("CW BL TH0 TH1 TH2 TH3", "BD", looks(256), T.BD[:], T.CW[:].indirect(T.BL[:]), T.TH[:], Op.is_ge)
-        pick("pD0", 0, "BK", "BD", T.BD[:], "MUL")
+        pick("pD0", 0, "BK", "BD", T.BD[:], "MUL", ["NH", "NL"])
         do = "DO%d" % t
         tt("MUL IW", do, 32, T[do][:], T.MUL[:, 15::16], lst("IW"), Op.is_lt)
-        mm("ON " + do, "pC", 16, T.pC[:, 0:16], mat("ON"), T[do][:], True, True)
+        mm("ON " + do, "pS0", 16, T.pS0[:, 0:16], mat("ON"), T[do][:], True, True)
         send(t, "D", T["DR%d" % t][:], T[do][:], do)
         tt("LF MUL", "E1", 32, lst("E1"), T.MUL[:, 15::16], lst("LF"), Op.max)
-        tt("E1 DM", "E2", 32, lst("E2"), lst("E1"), lst("DM"), Op.min)
-        cp("E2", "OD", 16, T.OD[:], lst("E2"))
-        op("V", "pC", "AA", vc(16), lambda e: e.tensor_reduce(T.AA[:], T.pC[:, 0:16], AxisListType.X, Op.add))
+        cp("E1", "OD", 16, T.OD[:], lst("E1"))
+        op("V", "pS0", "AA", vc(16), lambda e: e.tensor_reduce(T.AA[:], T.pS0[:, 0:16], AxisListType.X, Op.add))
         if not last:
-            cp("OD recvZ%d" % t, XK, puts(256), T.X[:].indirect(T.OD[:]), T["ZP%d" % t][:])
+            for j in range(XS):
+                n = 16 // XS
+                cp("OD recvZ%d" % t, XK, puts(16 * n), T.X[:].indirect(T.OD[:, n * j:n * j + n]), T["ZP%d" % t][:, 16 * n * j:16 * n * j + 16 * n])
         advance(not last)
         hits(t, LAST_V if last else HITS_V)
         if not last:
             keep()
-            base()
-            if t < TS - 2:
-                widen()
     dma("Y", "dy", 32, T.ys[:], T.YS[:], "FR VC", "ys")
 
     N = len(ops)
@@ -479,8 +513,14 @@ def rank_program(g, core, T, topo):
             ends[o["chain"]] = i
         for k in o["r"] + o["w"]:
             if k[0] == "p":
-                for q, j in banks.get(k, {}).items():
-                    after(j, WAKE if q != o["q"] else 0.0)
+                before, now = banks.get(k, ([], []))
+                if now and ops[now[-1]]["q"] != o["q"]:
+                    before, now = now, []
+                for j in before:
+                    after(j, WAKE)
+                if now and o["q"] == "P":
+                    after(now[-1], 0.0)
+                banks[k] = (before, now + [i])
         for k in o["r"]:
             if k[0] != "p" and k in last_w:
                 after(last_w[k], WAKE)
@@ -490,9 +530,6 @@ def rank_program(g, core, T, topo):
                     after(last_w[k], WAKE)
                 for j in readers.get(k, []):
                     after(j, WAKE)
-        for k in o["r"] + o["w"]:
-            if k[0] == "p":
-                banks.setdefault(k, {})[o["q"]] = i
         for k in o["r"]:
             if k[0] != "p":
                 readers.setdefault(k, []).append(i)
@@ -511,71 +548,41 @@ def rank_program(g, core, T, topo):
             gap = GAP[ops[i]["chain"]] if ops[i]["chain"] and ops[i]["chain"] == ops[j]["chain"] else 0.0
             best = max(best, wake + ops[i]["lat"] + gap + prio[j])
         prio[i] = best + ops[i]["cost"] + ops[i]["first"]
-    left = [len(preds[i]) for i in range(N)]
-    ready = [0.0] * N
-    free = {q: 0.0 for q in eng}
-    avail = {q: [] for q in eng}
-    for i in range(N):
-        if left[i] == 0:
-            avail[ops[i]["q"]].append(i)
-    order = []
-    over = [False] * N
-    came = [0.0] * N
-    line = {q: sorted((i for i in range(N) if ops[i]["q"] == q), key=lambda i: -prio[i]) for q in eng}
 
-    def soonest(i, memo):
-        if left[i] == 0:
-            return ready[i]
-        if i not in memo:
-            best = 0.0
-            for j, wake in preds[i].items():
-                if over[j]:
-                    best = max(best, came[j] + ops[j]["lat"] + wake)
+    def place(turn, behind):
+        end = [0.0] * N
+        taken = {q: ([], []) for q in eng}
+        for i in turn:
+            t0 = max([end[j] + gap for j, gap in behind[i]] + [0.0])
+            cost = ops[i]["cost"]
+            a, z = taken[ops[i]["q"]]
+            lo, hi = 0, len(z)
+            while lo < hi:
+                mid = (lo + hi) // 2
+                if z[mid] <= t0:
+                    lo = mid + 1
                 else:
-                    best = max(best, max(soonest(j, memo), free[ops[j]["q"]]) + ops[j]["cost"] + ops[j]["lat"] + wake)
-            memo[i] = best
-        return memo[i]
-
-    order += ORDER
-    while len(order) < N:
-        pick_ = None
-        for q in "VSPGY":
-            if avail[q]:
-                t0 = max(free[q], min(ready[i] for i in avail[q]))
-                if pick_ is None or t0 < pick_[0]:
-                    pick_ = (t0, q)
-        t0, q = pick_
-        line[q] = [i for i in line[q] if not over[i]]
-        memo, i, wait = {}, None, None
-        for c in sorted((c for c in avail[q] if ready[c] <= t0), key=lambda c: -prio[c]):
-            cost = ops[c]["cost"]
-            block = None
-            for j in line[q][:8]:
-                if j == c or prio[j] < prio[c] + MARGIN * cost:
-                    break
-                e = soonest(j, memo)
-                if t0 < e < t0 + cost - 0.02:
-                    block = e if block is None else min(block, e)
-            if block is None:
-                i = c
-                break
-            wait = block if wait is None else min(wait, block)
-        if i is None:
-            free[q] = wait
-            continue
-        avail[q].remove(i)
-        done = t0 + ops[i]["cost"]
-        free[q] = came[i] = done
-        over[i] = True
-        order.append(i)
-        for j, wake in succs[i]:
-            ready[j] = max(ready[j], done + ops[i]["lat"] + wake)
-            left[j] -= 1
-            if left[j] == 0:
-                avail[ops[j]["q"]].append(j)
+                    hi = mid
+            while lo < len(a) and a[lo] < t0 + cost - SLIP:
+                t0 = max(t0, z[lo])
+                lo += 1
+            a.insert(lo, t0)
+            z.insert(lo, t0 + cost)
+            end[i] = t0 + cost
+        return end
 
     if not ORDER:
-        ORDER.extend(order)
+        ahead = [[(j, wake + ops[j]["lat"]) for j, wake in preds[i].items()] for i in range(N)]
+        back = [[(j, wake + ops[i]["lat"]) for j, wake in succs[i]] for i in range(N)]
+        turn, best = sorted(range(N), key=lambda i: (-prio[i], i)), None
+        for _ in range(ROUNDS):
+            end = place(turn, ahead)
+            if best is None or max(end) < best[0]:
+                best = (max(end), sorted(range(N), key=lambda i: (end[i] - ops[i]["cost"], i)))
+            end = place(sorted(range(N), key=lambda i: (-end[i], -i)), back)
+            turn = sorted(range(N), key=lambda i: (-end[i], i))
+        ORDER.extend(best[1])
+    order = ORDER
 
     count = {q: 0 for q in eng}
     clock = {q: {} for q in eng}

@@ -3,62 +3,69 @@ from concourse.mybir import AluOpType as Op, AxisListType, ActivationFunctionTyp
 W, L, D = 8192, 256, 8448
 KAPPA = (3, 29, 71, 113)
 TS, CAP = 4, 128
-FL = "L1 L2 R1 R2 LF IW E1 FR FS VF VG BM0 BM1 S4 S5 S6 DM".split()
+WB = "EX M4 LU LG LW LV L2 T1 TH T2 TC UW D2".split()
+FL = "L1 L3 R1 R2 LF IW E1 FR FS VF VD BM S4 S5 S6 DM".split()
 IL = "VN VC S1 S2 S3 S7 S8 S9".split()
 QL = "THR VK BK4 SB SQ".split()
-CM = "ID NI BO TG ON BK TK T4 O4 A0 A1 A2 A3 B0 B1 B2 B3 C0 C1 C2 C3 U0 U1 U2 U3".split()
+CM = "ID NI BO TG ON BK BE TK T4 O4 A0 A1 A2 A3 B0 B1 B2 B3 C0 C1 C2 C3 U0 U1 U2 U3".split()
 
 SCRATCH = {
-    "X": ("sbuf", [128, 8448], "bfloat16"),
-    "Q": ("sbuf", [128, 8464], "bfloat16"), "HT": ("sbuf", [128, 8464], "bfloat16"),
+    "X": ("sbuf", [128, 2 * D], "bfloat16"),
+    "Q": ("sbuf", [128, 8464], "bfloat16"), "HT": ("sbuf", [128, 2 * D], "bfloat16"),
     "OW": ("sbuf", [128, 1024], "bfloat16"),
     "IO": ("sbuf", [128, 8192], "float32"),
     "SD": ("sbuf", [128, 256], "bfloat16"), "V0": ("sbuf", [128, 16], "int32"), "TI": ("sbuf", [128, 4], "int32"), "TF": ("sbuf", [128, 4], "float32"),
     "PI": ("sbuf", [128, 8], "int32"), "PF": ("sbuf", [128, 8], "float32"), "KP": ("sbuf", [128, 16], "float32"),
     "RM": ("sbuf", [128, 256], "float32"), "RD": ("sbuf", [128, 256], "float32"), "RP": ("sbuf", [128, 128], "float32"), "RG": ("sbuf", [128, 128], "float32"),
     "J0": ("sbuf", [128, 128], "float32"), "J1": ("sbuf", [128, 128], "float32"), "J2": ("sbuf", [128, 128], "float32"), "J3": ("sbuf", [128, 128], "float32"),
-    "J4": ("sbuf", [128, 640], "bfloat16"), "MK": ("sbuf", [128, 640], "bfloat16"), "OF32": ("sbuf", [128, 128], "float32"), "SL": ("sbuf", [128, 128], "float32"),
-    "NH": ("sbuf", [128, 256], "bfloat16"), "NL": ("sbuf", [128, 256], "bfloat16"), "RL": ("sbuf", [128, 256], "float32"),
+    "J4": ("sbuf", [128, 512], "bfloat16"), "MK": ("sbuf", [128, 512], "bfloat16"), "OF32": ("sbuf", [128, 128], "float32"), "SL": ("sbuf", [128, 128], "float32"),
+    "NH": ("sbuf", [128, 256], "bfloat16"), "RL": ("sbuf", [128, 256], "float32"),
     "K1": ("sbuf", [128, 256], "float32"), "K2": ("sbuf", [128, 256], "float32"), "K3": ("sbuf", [128, 256], "float32"), "K4": ("sbuf", [128, 256], "float32"),
     "CM": ("sbuf", [128, 128 * len(CM)], "bfloat16"), "FL": ("sbuf", [128, 16 * len(FL)], "float32"), "IL": ("sbuf", [128, 16 * len(IL)], "int32"),
     "QL": ("sbuf", [128, 64 * len(QL)], "float32"), "UF": ("sbuf", [128, 512], "float32"), "YM": ("sbuf", [128, 2048], "float32"),
     "KA": ("sbuf", [128, 256], "float32"), "KC": ("sbuf", [128, 256], "float32"), "NK": ("sbuf", [128, 256], "bfloat16"),
     "NM": ("sbuf", [128, 256], "bfloat16"), "CO": ("sbuf", [128, 1024], "bfloat16"), "D0": ("sbuf", [128, 256], "float32"),
-    "WH": ("sbuf", [128, 10], "float32"), "OB": ("sbuf", [128, 64], "bfloat16"),
+    "OB": ("sbuf", [128, 64], "bfloat16"),
     "TN": ("sbuf", [128, 256], "int32"), "TR": ("sbuf", [128, 256], "float32"), "P1": ("sbuf", [128, 256], "float32"),
     "P2": ("sbuf", [128, 256], "float32"), "M1": ("sbuf", [128, 256], "float32"), "OM": ("sbuf", [128, 256], "uint16"),
-    "DV0": ("sbuf", [128, 256], "uint16"), "DV1": ("sbuf", [128, 256], "uint16"), "OV": ("sbuf", [128, 16], "uint16"), "EA": ("sbuf", [128, 16, 256], "bfloat16"), "OD": ("sbuf", [128, 16], "uint16"), "BL": ("sbuf", [128, 16], "uint16"),
-    "HA": ("sbuf", [128, 64], "bfloat16"), "SC": ("sbuf", [128, 66], "bfloat16"), "GO": ("sbuf", [128, 64], "bfloat16"),
+    "DV": ("sbuf", [128, 256], "uint16"), "OV": ("sbuf", [128, 16], "uint16"), "EA": ("sbuf", [128, 16, 256], "bfloat16"), "OD": ("sbuf", [128, 16], "uint16"), "BL": ("sbuf", [128, 16], "uint16"),
+    "HA": ("sbuf", [128, 64], "bfloat16"), "SC": ("sbuf", [128, 66], "bfloat16"), "HM": ("sbuf", [128, 64], "bfloat16"),
     "FB": ("sbuf", [128, 64], "bfloat16"), "F6": ("sbuf", [128, 32], "bfloat16"), "SY": ("sbuf", [128, 64], "int32"),
-    "EB": ("sbuf", [128, 16, 256], "bfloat16"), "DUL": ("sbuf", [128, 256], "float32"), "HUL": ("sbuf", [128, 256], "float32"),
+    "WB": ("sbuf", [128, 256 * len(WB)], "bfloat16"), "CV": ("sbuf", [128, 256], "float32"), "CX": ("sbuf", [128, 16], "uint16"), "HUL": ("sbuf", [128, 256], "float32"),
     "RUL": ("sbuf", [128, 256], "float32"), "BUL": ("sbuf", [128, 256], "float32"), "MUL": ("sbuf", [128, 256], "float32"),
     "GQ": ("sbuf", [128, 256], "bfloat16"), "AB": ("sbuf", [128, 256], "bfloat16"),
-    "TH": ("sbuf", [128, 256], "bfloat16"), "BB": ("sbuf", [128, 256], "bfloat16"), "BD": ("sbuf", [128, 256], "bfloat16"), "CW": ("sbuf", [128, 128], "float32"),
+    "BB": ("sbuf", [128, 256], "bfloat16"), "BD": ("sbuf", [128, 256], "bfloat16"), "CW": ("sbuf", [128, 128], "float32"),
     "AA": ("sbuf", [128, 1], "float32"), "YT": ("sbuf", [128, 4, 4, 16], "float32"), "YS": ("sbuf", [128, 32], "float32"),
-    "GB": ("sbuf", [128, 4096], "bfloat16"), "HB": ("sbuf", [128, 2048], "bfloat16"), "LA": ("sbuf", [128, 2048], "bfloat16"), "LB": ("sbuf", [128, 2048], "bfloat16"),
+    "GB": ("sbuf", [128, 4096], "bfloat16"), "HB": ("sbuf", [128, 4096], "bfloat16"), "LA": ("sbuf", [128, 2048], "bfloat16"), "LB": ("sbuf", [128, 2048], "bfloat16"),
     "Z": ("sbuf", [128, 256], "bfloat16"), "GR": ("sbuf", [128, 1024], "bfloat16"), "H": ("sbuf", [128, 1024], "bfloat16"), "F": ("sbuf", [128, 256], "bfloat16"),
     "XI": ("sbuf", [128, 64], "int32"), "OF": ("sbuf", [128, 64], "uint16"),
-    "pS0": ("psum", [128, 512], "float32"), "pS1": ("psum", [128, 512], "float32"), "pD0": ("psum", [128, 512], "float32"), "pD1": ("psum", [128, 512], "float32"),
+    "pS0": ("psum", [128, 512], "float32"), "pT2": ("psum", [128, 1024], "bfloat16"), "pD0": ("psum", [128, 512], "float32"), "pD1": ("psum", [128, 512], "float32"),
     "pT0": ("psum", [128, 1024], "bfloat16"), "pT1": ("psum", [128, 1024], "bfloat16"), "pC": ("psum", [128, 512], "float32"), "pH": ("psum", [128, 512], "float32"),
 }
 for _t in range(TS):
-    SCRATCH.update({"ZF%d" % _t: ("sbuf", [128, 256], "bfloat16"), "ZP%d" % _t: ("sbuf", [128, 256], "bfloat16"), "LQ%d" % _t: ("sbuf", [128, 16], "uint16"),
-                    "RL%d" % _t: ("sbuf", [128, 16], "uint16"), "DO%d" % _t: ("sbuf", [128, 16], "bfloat16"), "DR%d" % _t: ("sbuf", [128, 16], "bfloat16"),
+    SCRATCH.update({"ZF%d" % _t: ("sbuf", [128, 256], "bfloat16"), "ZP%d" % _t: ("sbuf", [128, 256], "bfloat16"), "GO%d" % _t: ("sbuf", [128, 64], "bfloat16"),
+                    "RG%d" % _t: ("sbuf", [128, 64], "bfloat16"), "DO%d" % _t: ("sbuf", [128, 16], "bfloat16"), "DR%d" % _t: ("sbuf", [128, 16], "bfloat16"),
                     "MS%d" % _t: ("sbuf", [128, 32], "uint16"), "MR%d" % _t: ("sbuf", [128, 32], "uint16")})
 SEMAPHORES = ["cV", "cS", "cP", "cG", "dx", "dv", "ds", "dt", "dy", "loc"] + ["r%s%d" % (k, t) for k in "MLZD" for t in range(TS)]
 CYC, WAKE, SFIX, LOOK, PUT, REMOTE = 0.00083, 0.15, 0.15, 1.56, 3.8, 3.0
-ROUNDS, SLIP = 12, 0.0
+ROUNDS, SLIP, MOVES = 8, 0.0, 300
+HS, QS = 2, 2
 ORDER = []
 RUN = ((("V", 28), ("S", 18), ("S", 18)),)
-NS = len(RUN)
+NS = 1
 CW = 64 // NS
-CLAIM_V = ((0, 16),)
-HITS_V = (1, 3, 5, 8, 10, 12, 14)
+CLAIM = (("S", 2), ("V", 2)) + (("S", 4),) * 6 + (("S", 2), ("V", 2))
+HITS_V = (3, 7, 11)
 LAST_V = (1, 3, 5, 7, 9, 11, 13, 15)
 GAP = {"S": 0.3, "V": 0.9}
 AHEAD = 0.0
-QV = 4000
+PAD = {}
+FIRST = 3.0
+IOS = 12
+NT = 3
+QV, QS2 = 1000, 4500
 XS = 2
+LA_S, LB_S = (), ()
 MX = False
 
 
@@ -72,13 +79,13 @@ def rank_program(g, core, T, topo):
     chain = [None]
 
     def op(q, reads, writes, cost, f, kind="c", sem=None, n=0, lat=0.0):
-        ops.append({"chain": chain[0], "first": boost[0], "q": q, "r": reads.split(), "w": writes.split(), "cost": cost, "f": f, "kind": kind, "sem": sem, "n": n, "lat": lat})
+        ops.append({"chain": chain[0], "first": boost[0], "q": q, "r": reads.split(), "w": writes.split(), "cost": cost, "f": f, "kind": kind, "sem": sem, "n": n, "lat": lat + PAD.get(writes, 0.0)})
 
     def dma(q, sem, total, out, in_, reads, writes):
         op(q, reads, writes, 0.1, lambda e: e.dma_start(out, in_).then_inc(T.sem[sem], 16), "d", sem, total, 7.0 if sem == "dx" else 2.5)
 
     def part(k, a, b, step=1):
-        for group, buf, w in ((FL, "FL", 16), (IL, "IL", 16), (QL, "QL", 64), (CM, "CM", 128)):
+        for group, buf, w in ((FL, "FL", 16), (IL, "IL", 16), (QL, "QL", 64), (CM, "CM", 128), (WB, "WB", 256)):
             if k in group:
                 o = w * group.index(k)
                 return T[buf][:, o + a:o + b:step]
@@ -89,6 +96,9 @@ def rank_program(g, core, T, topo):
 
     def quad(k, h=None):
         return part(k, 0, 64) if h is None else part(k, CW * h, CW * h + CW)
+
+    def wide(k):
+        return part(k, 0, 256)
 
     def mat(k):
         return part(k, 0, 128)
@@ -119,6 +129,7 @@ def rank_program(g, core, T, topo):
 
     def mm(reads, writes, n, out, lhsT, rhs, a, z):
         op("P", reads, writes, max(n, 64) * CYC, lambda e: e.matmul(out, lhsT, rhs, a, z))
+        ops[-1]["ends"] = (a, z)
 
     def scan(reads, writes, n, out, d0, d1, init, o0, o1):
         op("V", reads, writes, vc(n), lambda e: e.tensor_tensor_scan(out, d0, d1, init, o0, o1))
@@ -162,13 +173,18 @@ def rank_program(g, core, T, topo):
     iota("J1", 128, T.J1[:], [[16, 8], [1, 4], [0, 4]], 0, 0)
     iota("J2", 128, T.J2[:], [[1, 8], [1000, 4], [0, 4]], 0, 0)
     iota("J3", 128, T.J3[:], [[0, 8], [1, 4], [0, 4]], 0, 0)
-    iota("J4", 640, T.J4[:], [[0, 160], [1, 4]], 0, 0)
-    iota("RL", 256, T.RL[:], [[1, 256]], 0, 0)
+    fill("J4", 256, T.J4[:], 1.0)
+    op("G", "J4", "MK", 0.17 + 1024 * CYC, lambda e: e.affine_select(T.MK[:], T.J4[:], [[0, 128], [1, 4]], Op.not_equal, 0.0, 0, 0))
+    iota("RL", 256, T.RL[:], [[1, 256]], W - D, 0)
     iota("KI", 4, T.KP[:, 0:4], [[1, 4]], 0, 0)
-    for j in range(4):
-        iota("IO%d" % j, 512, T.IO[:, 512 * j:512 * j + 512], [[1, 512]], 512 * j, 0)
-        for a in range(1, 4):
-            act("IO%d" % j, "IO%d" % (j + 4 * a), 512, T.IO[:, 512 * j + 2048 * a:512 * j + 2048 * a + 512], T.IO[:, 512 * j:512 * j + 512], AF.Identity, bias=2048.0 * a)
+    boost[0] = FIRST
+    iota("IO0", 512, T.IO[:, 0:512], [[1, 512]], 0, 0)
+    for j in range(1, 16):
+        if j > IOS:
+            ts("IO0", "IO%d" % j, 512, T.IO[:, 512 * j:512 * j + 512], T.IO[:, 0:512], 512.0 * j, Op.add)
+        else:
+            act("IO0", "IO%d" % j, 512, T.IO[:, 512 * j:512 * j + 512], T.IO[:, 0:512], AF.Identity, bias=512.0 * j)
+    boost[0] = 0.0
     IOK = " ".join("IO%d" % j for j in range(16))
     ts("PI0", "PI1", 1, T.PI[:, 1:2], T.PI[:, 0:1], 15, Op.bitwise_and)
     ts("PI0", "PI2", 1, T.PI[:, 2:3], T.PI[:, 0:1], 4, Op.arith_shift_right)
@@ -193,7 +209,6 @@ def rank_program(g, core, T, topo):
     ts("RM PF", "K1", 256, T.K1[:], T.RM[:], pi, Op.is_equal)
     ts("RM PF", "K2", 128, T.K2[:, 0:128], T.RM[:, 0:128], pi, Op.is_gt)
     tt("K2 BO", "TG", 256, mat("TG"), T.K2[:, 0:128], mat("BO"), Op.mult)
-    ts("J4", "MK", 320, T.MK[:], T.J4[:], 1.0, Op.min)
     fill("OF32", 128, T.OF32[:], 1.0)
     for r in range(4):
         ts("J2 PF", "B%d" % r, 128, mat("B%d" % r), T.J2[:], pg, Op.subtract, 1000.0 * r, Op.is_equal)
@@ -209,8 +224,8 @@ def rank_program(g, core, T, topo):
     ts("ID", "O4", 64, mat("O4"), mat("ID"), -32768.0 * CAP, Op.mult)
     tt("J3 O4", "T4", 256, mat("T4"), T.J3[:], mat("O4"), Op.add)
     ts("BO", "O4", 64, mat("O4"), mat("BO"), 8192.0, Op.mult)
-    ts("K1", "NH", 256, T.NH[:], T.K1[:], float(2 ** 24 + W - 32768), Op.mult, -float(2 ** 24), Op.add)
-    tt("K1 RL", "NL", 512, T.NL[:], T.K1[:], T.RL[:], Op.mult)
+    tt("NM RL", "NH", 512, T.NH[:], T.NM[:], T.RL[:], Op.add)
+    ts("BO", "BE", 64, mat("BE"), mat("BO"), float(D), Op.mult)
     ts("K1", "SL", 128, T.SL[:], T.K1[:, 0:128], -2.0 ** -46, Op.mult, 2.0 ** -46, Op.add)
     ts("SL", "SL", 128, T.SL[:], T.SL[:], 2.0 ** -92, Op.max)
     ts("BO", "BK", 64, mat("BK"), mat("BO"), 32768.0, Op.mult)
@@ -220,6 +235,18 @@ def rank_program(g, core, T, topo):
     ts("RM PF", "KC", 256, T.KC[:], T.RM[:], pi, Op.not_equal, -float(2 ** 24 + 2 ** 14), Op.mult)
     ts("KC", "NK", 256, T.NK[:], T.KC[:], 16384.0, Op.add)
     ts("DMI PF", "DM", 16, lst("DM"), lst("DM"), pi, Op.add)
+    fill("P10", 64, T.P1[:, 0:64], 0.5)
+    fill("P11", 64, T.P1[:, 64:128], 0.5)
+    fill("P12 P13", 128, T.P1[:, 128:256], 0.0)
+    scan("P10 P11 P12 P13", "HUL", 128, T.HUL[:, 0:128], T.P1[:, 0:128], T.P1[:, 128:256], 2.0 ** 63, Op.mult, Op.add)
+    for h in range(2):
+        ts("HUL", "UW", 128, part("UW", 128 * h, 128 * h + 128), T.HUL[:, 0:128], 2.5, Op.mult)
+    tt("HUL ID", "CV", 256, T.CV[:, 0:128], T.HUL[:, 0:128], mat("ID"), Op.mult)
+    op("V", "CV", "UP", vc(128), lambda e: e.tensor_reduce(T.KP[:, 15:16], T.CV[:, 0:128], AxisListType.X, Op.add))
+    iota("L1", 16, lst("L1"), [[4, 16]], 0, 0)
+    ts("L1 PF", "CX", 16, T.CX[:], lst("L1"), pr, Op.add)
+    iota("M4", 256, wide("M4"), [[0, 64], [4, 4]], 0, 0)
+    ts("M4 PF", "M4", 128, wide("M4"), wide("M4"), pi, Op.is_equal)
     fill("OB", 32, T.OB[:], 1.0)
     for t in range(TS):
         fill("OW%d" % t, 128, T.OW[:, 256 * t:256 * t + 256], 32.0 ** (t + 1 - TS))
@@ -227,7 +254,9 @@ def rank_program(g, core, T, topo):
     fill("SC0", 1, T.SC[:, 0:1], 0.0)
     fill("THR", 64, quad("THR"), 9.0)
     fill("FB", 32, T.FB[:], 16384.0)
-    fill("FR", 16, lst("FR"), 0.0)
+    fill("FR", 16, T.F6[:, 0:16], 0.0)
+    for k in range(4):
+        fill("TC", 32, part("TC", 64 * k, 64 * k + 64), 0.75 * 2.0 ** (11 * (3 - k) - 46))
     fill("AA", 1, T.AA[:], 0.0)
     cp("TI", "TF", 4, T.TF[:], T.TI[:])
     ts("RD PF", "K2", 256, T.K2[:], T.RD[:], pi, Op.is_equal, 2.0, Op.mult)
@@ -236,15 +265,13 @@ def rank_program(g, core, T, topo):
     tt("K1 K3", "K3", 512, T.K3[:], T.K3[:], T.K1[:], Op.add)
     tt("K2 K3", "K3", 512, T.K3[:], T.K3[:], T.K2[:], Op.add)
     size = [2.0 ** (24 * t - 24) for t in range(TS)]
-    for h in range(2):
-        for a in range(2):
-            fill("WH%d%d" % (h, a), 1, T.WH[64 * a:64 * a + 64, 8 + h:9 + h], 2.0 ** (11 * (3 - 2 * h - a)))
     for t in range(TS):
         ts("K3", "CO%d" % t, 256, T.CO[:, 256 * t:256 * t + 256], T.K3[:], size[t], Op.mult)
-        ts("WH00 WH01 WH10 WH11", "WT%d" % t, 2, T.WH[:, 2 * t:2 * t + 2], T.WH[:, 8:10], size[t] ** -2, Op.mult)
     for j in range(0, 8464, 529):
         if j < QV:
             fill("Q" + str(j), 265, T.Q[:, j:j + 529], 0.0)
+        elif j < QS2:
+            act("Q0", "Q" + str(j), 529, T.Q[:, j:j + 529], T.Q[:, 0:529], AF.Copy)
         else:
             iota("Q" + str(j), 529, T.Q[:, j:j + 529], [[0, 529]], 0, 0)
         iota("HT" + str(j), 529, T.HT[:, j:j + 529], [[0, 529]], 0, 0)
@@ -267,40 +294,44 @@ def rank_program(g, core, T, topo):
         scan("D0 " + bank, out, 256, T[out][:], T.D0[:], T[bank][:, a:a + 256], -8192.0, Op.min, Op.max)
 
     def step(t, b):
-        for h in range(NS):
-            boost[0] = AHEAD * (1 - h)
-            s, d, cols = "pS%d" % h, "pD%d" % h, slice(CW * h, CW * h + CW)
-            Z, zk = (T.SD, "SD") if b == 0 else (T.Z, "Z%d" % h)
-            xi, tn, of = "XI%d" % h, "TN%d%d" % (b, h), "OF%d" % h
-            if b:
-                tt("SQ%d VK" % h, xi, 2 * CW, T.XI[:, cols], quad("SQ", h), quad("VK", h), Op.add)
-            mm("NI " + zk, d, 4 * CW, T[d][:, 0:4 * CW], mat("NI"), Z[:, hs(h)], True, False)
-            if b < 3 and MX:
-                sums("A", lambda l: Z[:, l], zk, h, True, False)
-            a = 64 * b + CW * h
-            ts(xi, tn, CW, T.TN[:, a:a + CW], T.XI[:, cols], W - 1, Op.bitwise_and)
-            cp(tn, of, CW, T.OF[:, cols], T.TN[:, a:a + CW])
-            c0, hk, mk = CW * h, "", ""
-            for j, (q, n) in enumerate(RUN[h]):
+        Z, zk = (T.SD, "SD SD") if b == 0 else (T.Z, "Z0 Z1")
+        if b:
+            tt("pS0 VK", "XI0", 64, T.XI[:], T.pS0[:, 64:128], quad("VK"), Op.add)
+        if b < 3 and MX:
+            sums("A", lambda l: Z[:, l], zk, 0, True, False)
+        ts("XI0", "TN%d0" % b, 64, T.TN[:, 64 * b:64 * b + 64], T.XI[:], W - 1, Op.bitwise_and)
+        cp("TN%d0" % b, "OF", 64, T.OF[:], T.TN[:, 64 * b:64 * b + 64])
+        c0, hk, mk, shares = 0, "", "", []
+        for h, share in enumerate(RUN):
+            c1, keys = c0, ""
+            for j, (q, n) in enumerate(share):
                 key, lanes, four = "%d.%d" % (h, j), slice(4 * c0, 4 * c0 + 4 * n), slice(16 * c0, 16 * c0 + 16 * n)
-                look(q, XK + " " + of, "GR" + key, 16 * n, T.GR[:, four], T.X[:, 0:W].indirect(T.OF[:, c0:c0 + n]))
+                look(q, XK + " OF", "GR" + key, 16 * n, T.GR[:, four], T.X[:, 0:W].indirect(T.OF[:, c0:c0 + n]))
                 scan("MK GR" + key, "H" + key, 8 * n, T.H[:, four], T.MK[:, 0:16 * n], T.GR[:, four], 0.0, Op.mult, Op.max)
                 if b < 3 and MX:
                     tt("H%s %s" % (key, zk), "MX" + key, 8 * n, T.MX[:, lanes], T.H[:, 16 * c0 + 3:16 * c0 + 16 * n:4], Z[:, lanes], Op.max)
-                c0, hk, mk = c0 + n, hk + " H" + key, mk + " MX" + key
-            if b < 3 and MX:
-                sums("A", lambda l: T.H[:, 4 * l.start + 3:4 * l.stop:16], hk, h, False, False)
-                sums("B", lambda l: T.MX[:, l], mk, h, False, True)
-                act(s + " K2K", "SQ%d" % h, CW, quad("SQ", h), T[s][:, 0:CW], AF.Square, bias=k2k, scale=0.5)
-            mm("ID " + hk, d, 4 * CW, T[d][:, 0:4 * CW], mat("ID"), T.H[:, 16 * CW * h + 3:16 * CW * h + 16 * CW:4], False, True)
+                c0, keys, mk = c0 + n, keys + " H" + key, mk + " MX" + key
+            hk += keys
+            shares.append((h, c1, c0, keys))
+        if b < 3 and MX:
+            sums("A", lambda l: T.H[:, 4 * l.start + 3:4 * l.stop:16], hk, 0, False, False)
+            sums("B", lambda l: T.MX[:, l], mk, 0, False, True)
+            act("K2K", "pS0", 64, T.pS0[:, 64:128], T.pS0[:, 0:64], AF.Square, bias=k2k, scale=0.5)
+        for h, c1, c0, keys in shares:
+            d, n, lanes = "pD%d" % h, 4 * (c0 - c1), slice(4 * c1, 4 * c0)
+            mm("NI " + zk, d, n, T[d][:, 0:n], mat("NI"), Z[:, lanes], True, False)
+            mm("ID " + keys, d, n, T[d][:, 0:n], mat("ID"), T.H[:, 16 * c1 + 3:16 * c0:4], False, True)
+        for h, c1, c0, keys in shares:
+            d, n, lanes = "pD%d" % h, 4 * (c0 - c1), slice(4 * c1, 4 * c0)
+            wide = h == len(RUN) - 1 == 0
             if b < 3:
-                act(d, "Z%d" % h, 4 * CW, T.Z[:, hs(h)], T[d][:, 0:4 * CW], AF.Abs)
-                if not MX:
-                    sums("B", lambda l: T.Z[:, l], "Z%d" % h, h, True, True)
-                    act(s + " K2K", "SQ%d" % h, CW, quad("SQ", h), T[s][:, 0:CW], AF.Square, bias=k2k, scale=0.25)
+                act(d, "Z0 Z1" if wide else "Z%d" % h, n, T.Z[:, lanes], T[d][:, 0:n], AF.Abs)
             else:
-                act(d, "ZF%d.%d" % (t, h), 4 * CW, T["ZF%d" % t][:, hs(h)], T[d][:, 0:4 * CW], AF.Abs)
-        boost[0] = 0.0
+                act(d, "ZF%d.%d" % (t, h), n, T["ZF%d" % t][:, lanes], T[d][:, 0:n], AF.Abs)
+                ts("ZF%d.%d TF" % (t, h), "F0 F1" if wide else "F%d" % h, n // 2, T.F[:, lanes], T["ZF%d" % t][:, lanes], T.TF[:, t:t + 1], Op.is_ge)
+        if b < 3 and not MX:
+            sums("B", lambda l: T.Z[:, l], "Z0 Z1", 0, True, True)
+            act("K2K", "pS0", 64, T.pS0[:, 64:128], T.pS0[:, 0:64], AF.Square, bias=k2k, scale=0.25)
 
     def trails(t, b):
         cols, tn = slice(64 * b, 64 * b + 64), both("TN%d" % b)
@@ -313,12 +344,10 @@ def rank_program(g, core, T, topo):
 
     def halts(t):
         for h in range(NS):
-            ts("ZF%d.%d TF" % (t, h), "F%d" % h, 2 * CW, T.F[:, hs(h)], T["ZF%d" % t][:, hs(h)], T.TF[:, t:t + 1], Op.is_ge)
-            sums("B", lambda l: T.F[:, l], "F%d" % h, h, True, True)
+            sums("B", lambda l: T.F[:, l], "F0 F1", h, True, True)
             tt("pS%d THR" % h, "HA%d" % h, CW, T.HA[:, CW * h:CW * h + CW], T["pS%d" % h][:, 0:CW], quad("THR", h), Op.is_ge)
         ha = both("HA")
-        for q in range(4):
-            mm("C%d %s" % (q, ha), "pS1", 16, T.pS1[:, 64:80], mat("C%d" % q), T.HA[:, q:64:4], q == 0, q == 3)
+        act(ha, "HM", 64, T.HM[:], T.HA[:], AF.Identity, bias=-2.0 ** 31, scale=2.0 ** 31)
         mm("ID FB", "pC", 64, T.pC[:, 0:64], mat("ID"), T.FB[:], True, False)
         mm("T4 " + ha, "pC", 64, T.pC[:, 0:64], mat("T4"), T.HA[:], False, False)
         scan("OB " + ha, "SC1", 32, T.SC[:, 1:65], T.OB[:], T.HA[:], 0.0, Op.mult, Op.add)
@@ -327,20 +356,34 @@ def rank_program(g, core, T, topo):
             cols = slice(64 * b, 64 * b + 64)
             tt("TR%d pC" % b, "M1%d" % b, 64, T.M1[:, cols], T.pC[:, 0:64], T.TR[:, cols], Op.max)
             ts("M1%d" % b, "OM%d" % b, 64, T.OM[:, cols], T.M1[:, cols], float(D), Op.min)
-        cp("pC", "GO", 64, T.GO[:], T.pC[:, 0:64])
-        for q in range(4):
-            mm("C%d GO" % q, "pS0", 16, T.pS0[:, 64:80], mat("C%d" % q), T.GO[:, q:64:4], q == 0, q == 3)
-        tt("pS0 VF", "VG", 16, lst("VG"), T.pS0[:, 64:80], lst("VF"), Op.max)
+        tt("pC HM", "GO%d" % t, 64, T["GO%d" % t][:], T.pC[:, 0:64], T.HM[:], Op.is_lt)
 
-    def shadows(t, bank, late, out):
-        dv, bm, eb = "DV%d" % (t % 2), "BM%d" % (t % 2), "EB" if late else "EA"
+    def firsts(t):
+        rg, rk = T["RG%d" % t], "recvL%d" % t
+        tt(rk + " CX M4", "EX", looks(256), wide("EX"), rg[:].indirect(T.CX[:]), wide("M4"), Op.mult)
+        for h in range(2):
+            mm("EX BO", "pH", 128, T.pH[:, 128 * h:128 * h + 128], part("EX", 128 * h, 128 * h + 128), mat("BO"), True, True)
+        tt("pH LU", "LW", 256, wide("LW"), T.pH[:, 0:256], wide("LU"), Op.mult)
+        tt("pH LG", "LV", 128, part("LV", 0, 128), T.pH[:, 0:128], part("LG", 0, 128), Op.mult)
+        mm("LW L2", "pH", 128, T.pH[:, 256:384], part("LW", 0, 128), part("L2", 0, 128), True, True)
+        mm("LW L2", "pH", 128, T.pH[:, 384:512], part("LW", 128, 256), part("L2", 128, 256), True, False)
+        mm("LV L2", "pH", 128, T.pH[:, 384:512], part("LV", 0, 128), part("L2", 0, 128), False, True)
+        act("pH", "CV", 256, T.CV[:], T.pH[:, 256:512], AF.Copy)
+        for h in range(2):
+            a = 128 * h
+            tt("CV BL TH", "D2%d" % h, looks(128), part("D2", a, a + 128), T.CV[:, a:a + 128].indirect(T.BL[:, 8 * h:8 * h + 8]), part("T2", a, a + 128), Op.is_ge)
+        for q in range(4):
+            mm("C%d %s" % (q, rk), "pS0", 16, T.pS0[:, 64:80], mat("C%d" % q), rg[:, q:64:4], q == 0, q == 3)
+        act("pS0", "IW", 16, lst("IW"), T.pS0[:, 64:80], AF.Identity, bias=-65536.0, scale=65536.0)
+        tt("pS0 VD", "L1", 16, lst("L1"), T.pS0[:, 64:80], lst("VD"), Op.mult)
+        tt("L1 DM", "LF", 32, lst("LF"), lst("L1"), lst("DM"), Op.add)
+
+    def shadows(bank, out):
+        dv, bm, eb = "DV", "BM", "EA"
         mm("ID NK", bank, 256, T[bank][:, 256:512], mat("ID"), T.NK[:], True, False)
         for c in range(16):
             e, n = T[eb][:, c, 0:L - 16 * c], (L - 16 * c) // 2
-            if late:
-                ts("%s %s pS1" % (dv, bm), eb + str(c), n, e, T[dv][:, 16 * c:L], part(bm, c, c + 1), Op.is_equal, T.pS1[:, 64 + c:65 + c], Op.mult)
-            else:
-                ts(dv + " " + bm, eb + str(c), n, e, T[dv][:, 16 * c:L], part(bm, c, c + 1), Op.is_equal)
+            ts(dv + " " + bm, eb + str(c), n, e, T[dv][:, 16 * c:L], part(bm, c, c + 1), Op.is_equal)
             if c < 15:
                 mm("BK %s%d" % (eb, c), bank, L - 16 - 16 * c, T[bank][:, 272 + 16 * c:512], mat("BK"), T[eb][:, c, 16:L - 16 * c], False, False)
         mm("TK " + " ".join(eb + str(c) for c in range(16)), bank, 256, T[bank][:, 256:512], mat("TK"), T[eb][:, :, 0:16], False, True)
@@ -356,7 +399,7 @@ def rank_program(g, core, T, topo):
         ts("S7", "VN", 16, lst("VN"), lst("S7"), W - 1, Op.bitwise_and)
         if more:
             ts("SB AA", both("XI"), 64, T.XI[:], quad("SB"), T.AA[:], Op.add)
-            ts("BK4 AA", "VK", 64, quad("VK"), quad("BK4"), T.AA[:], Op.add)
+            act("BK4 AA", "VK", 64, quad("VK"), quad("BK4"), AF.Identity, bias=T.AA[:])
 
     def announce(t):
         ms = "MS%d" % t
@@ -367,23 +410,35 @@ def rank_program(g, core, T, topo):
 
     def prepare(t):
         mr, rk, s = T["MR%d" % t], "recvM%d" % t, size[t]
-        cp("%s CO%d %s" % (rk, t, tabs["Q"]), tabs["Q"], puts(256), T.Q[:, 0:8448].indirect(mr[:, 0:16]), T.CO[:, 256 * t:256 * t + 256])
+        for j in range(QS):
+            n = 16 // QS
+            cp("%s CO%d %s" % (rk, t, tabs["Q"]), tabs["Q"], puts(16 * n), T.Q[:, 0:8448].indirect(mr[:, n * j:n * j + n]), T.CO[:, 256 * t + 16 * n * j:256 * t + 16 * n * (j + 1)])
         look("S", rk + " " + tabs["Q"], "GQ", 256, T.GQ[:], T.Q[:].indirect(mr[:, 16:32]))
         ts("GQ PF", "BB", 128, T.BB[:], T.GQ[:], 1.5 * s, Op.is_ge, p, Op.mult)
         pick("pC", 0, "BO", "BB", T.BB[:], "BUL", ["NM"])
         cp("BUL", "BL", 16, T.BL[:], T.BUL[:, 15::16])
         act("GQ", "AB", 256, T.AB[:], T.GQ[:], AF.Abs, bias=-s)
-        for k in range(4):
-            ts("AB", "TH%d" % k, 32, T.TH[:, 64 * k:64 * k + 64], T.AB[:, 64 * k:64 * k + 64], s, Op.is_equal, 0.75 * 2.0 ** (11 * (3 - k) - 46), Op.max)
+        ts("AB", "T1", 128, wide("T1"), T.AB[:], s, Op.is_equal, 2.0 ** 80, Op.mult)
+        for j, k in enumerate(("TC", "UW")):
+            mm("ID T1", "pD1", 256, T.pD1[:, 256 * j:256 * j + 256], mat("ID"), wide("T1"), True, False)
+            mm("ID " + k, "pD1", 256, T.pD1[:, 256 * j:256 * j + 256], mat("ID"), wide(k), False, True)
+        act("pD1", "TH", 512, part("TH", 0, 512), T.pD1[:], AF.Copy)
+        for j, k in enumerate(("AB", "AB", "GQ", "GQ")):
+            op("P", "ID " + k, "pT0", 128 * CYC, lambda e, j=j, k=k: e.transpose(T.pT0[:, 128 * j:128 * j + 128], T[k][:, 128 * (j % 2):128 * (j % 2) + 128], mat("ID")))
+        ts("pT0 UP", "LU", 128, wide("LU"), T.pT0[:, 0:256], s, Op.not_equal, T.KP[:, 15:16], Op.mult)
+        ts("pT0", "LG", 64, part("LG", 0, 128), T.pT0[:, 0:128], s, Op.not_equal, 2.0 ** 64, Op.mult)
+        ts("pT0", "L2", 128, wide("L2"), T.pT0[:, 256:512], 1.5 * s, Op.is_ge)
+        cp(rk, "L3", 16, lst("L3"), mr[:, 16:32])
+        tt("L3 DM", "VD", 32, lst("VD"), lst("L3"), lst("DM"), Op.subtract)
 
     def widen(t):
-        bm, dv = "BM%d" % (t % 2), "DV%d" % (t % 2)
+        bm, dv = "BM", "DV"
         ts("S8", "S9", 16, lst("S9"), lst("S8"), W - 1, Op.bitwise_and)
         cp("S9", bm, 16, lst(bm), lst("S9"))
         for q in range(4):
-            mm("UF%d %s" % (q, bm), "pS1", 256, T.pS1[:, 384 + q:448:4], T.UF[:, 128 * q:128 * q + 128], lst(bm), True, True)
-        ts("pS1 KOF", "BK4", 64, quad("BK4"), T.pS1[:, 384:448], kof, Op.add)
-        tt("pS1 SY", "SB", 64, quad("SB"), T.pS1[:, 384:448], T.SY[:], Op.add)
+            mm("UF%d %s" % (q, bm), "pC", 256, T.pC[:, 128 + q:192:4], T.UF[:, 128 * q:128 * q + 128], lst(bm), True, True)
+        act("pC KOF", "BK4", 64, quad("BK4"), T.pC[:, 128:192], AF.Identity, bias=kof)
+        tt("pC SY", "SB", 64, quad("SB"), T.pC[:, 128:192], T.SY[:], Op.add)
         cp("S9", "OV", 16, T.OV[:], lst("S9"))
         cp("OV " + IOK, dv, looks(256), T[dv][:], T.IO[:].indirect(T.OV[:]))
 
@@ -396,32 +451,33 @@ def rank_program(g, core, T, topo):
 
     def hits(t, onv):
         mark = 32.0 ** (t + 1 - TS)
-        cp("OD OW%d " % t + tabs["HT"], tabs["HT"], puts(256), T.HT[:, 0:8448].indirect(T.OD[:]), T.OW[:, 256 * t:256 * t + 256])
+        for j in range(HS):
+            n = 16 // HS
+            cp("OD%d OD%d OW%d " % (n * j * XS // 16, (n * j + n - 1) * XS // 16, t) + tabs["HT"], tabs["HT"], puts(16 * n), T.HT[:].indirect(T.OD[:, n * j:n * j + n]), T.OW[:, 256 * t:256 * t + 16 * n])
         mm("ID NM", "pH", 256, T.pH[:, 0:256], mat("ID"), T.NM[:], True, False)
         for k in range(16):
-            hb, b0, q = "HB%d" % (k % 8), 256 * (k % 8), "V" if k in onv else "S"
-            chain[0] = None
-            look(q, "%s OM%d" % (tabs["HT"], k // 4), hb, 256, T.HB[:, b0:b0 + 256], T.HT[:].indirect(T.OM[:, 16 * k:16 * k + 16]))
+            hb, b0, q = "HB%d" % k, 256 * k, "V" if k in onv else "S"
+            chain[0] = q
+            look(q, "%s OM%d" % (tabs["HT"], k // 4), hb, 256, T.HB[:, b0:b0 + 256], T.HT[:, 0:8464].indirect(T.OM[:, 16 * k:16 * k + 16]))
             chain[0] = None
             for m in range(4):
                 mm("ID " + hb, "pH", 64, T.pH[:, 64 * (k % 4):64 * (k % 4) + 64], mat("ID"), T.HB[:, b0 + m:b0 + 256:4], False, k == 15 and m == 3)
         scan("D0 pH", "HUL", 256, T.HUL[:], T.D0[:], T.pH[:, 0:256], -8192.0, Op.min, Op.max)
-        tt("FR recvD%d" % t, "FS", 32, lst("FS"), T["DR%d" % t][:], lst("FR"), Op.add)
+        tt("FR recvD%d" % t, "FS", 32, lst("FS"), T["DR%d" % t][:], T.F6[:, 0:16], Op.add)
         if mark != 1.0:
-            ts("FS", "FS", 16, lst("FS"), lst("FS"), mark, Op.mult)
-        fr, v = (T.YS[:, 16:32], T.YS[:, 0:16]) if t == TS - 1 else (lst("FR"), lst("VC"))
+            act("FS", "FS", 16, lst("FS"), lst("FS"), AF.Copy, scale=mark)
+        fr, v = (T.YS[:, 16:32], T.YS[:, 0:16]) if t == TS - 1 else (T.F6[:, 0:16], lst("VC"))
         tt("VC VN", "S5", 32, lst("S5"), lst("VC"), lst("VN"), Op.subtract)
         tt("HUL FS", "FR", 32, fr, T.HUL[:, 15::16], lst("FS"), Op.is_lt)
         tt("S5 FR", "S6", 32, lst("S6"), lst("S5"), fr, Op.mult)
         tt("S6 VN", "VC", 32, v, lst("S6"), lst("VN"), Op.add)
 
     def keep():
-        tt("HUL FS", "F6", 32, T.F6[:, 0:16], T.HUL[:, 15::16], lst("FS"), Op.is_lt)
         tt("HUL FS", "F7", 32, T.F6[:, 16:32], T.HUL[:, 15::16], lst("FS"), Op.is_ge)
         for q in range(4):
-            mm("U%d F6 F7" % q, "pH", 32, T.pH[:, 256 + q:384:4], mat("U%d" % q), T.F6[:], True, True)
-        ts("pH", "THR", 64, quad("THR"), T.pH[:, 256:320], 9.0, Op.add)
-        ts("pH", "FB", 64, T.FB[:], T.pH[:, 256:320], -131072.0, Op.mult, 16384.0, Op.add)
+            mm("U%d FR F7" % q, "pH", 32, T.pH[:, 256 + q:384:4], mat("U%d" % q), T.F6[:], True, True)
+        act("pH", "THR", 64, quad("THR"), T.pH[:, 256:320], AF.Identity, bias=9.0)
+        act("pH", "FB", 64, T.FB[:], T.pH[:, 256:320], AF.Identity, bias=16384.0, scale=-131072.0)
 
     for h in range(NS):
         sums("B", lambda l: T.SD[:, l], "SD", h, True, True)
@@ -430,7 +486,7 @@ def rank_program(g, core, T, topo):
     cp("V0", "VC", 16, lst("VC"), T.V0[:])
     cp("V0", "S8", 16, lst("S8"), T.V0[:])
     widen(0)
-    shadows(0, "pC", False, "RUL")
+    shadows("pC", "RUL")
     advance(True)
 
     for t in range(TS):
@@ -445,11 +501,9 @@ def rank_program(g, core, T, topo):
         prepare(t)
         halts(t)
         if not last:
-            send(t, "Z", T["ZP%d" % t][:], T[zf][:], both(zf + "."))
-        lq = "LQ%d" % t
-        shadows(t, "pH", True, "DUL")
-        listed("DUL", "VG", "L1", "L2", T[lq][:], lq)
-        send(t, "L", T["RL%d" % t][:], T[lq][:], lq)
+            send(t, "Z", T["ZP%d" % t][:], T[zf][:], " ".join("%s.%d" % (zf, h) for h in range(len(RUN))))
+        send(t, "L", T["RG%d" % t][:], T["GO%d" % t][:], "GO%d" % t)
+        firsts(t)
         if last:
             for m in range(4):
                 for q in range(4):
@@ -457,42 +511,51 @@ def rank_program(g, core, T, topo):
             for m in range(4):
                 act("pC", "YT%d" % m, 64, T.YT[:, :, m, :], T.pC[:, 64 * m:64 * m + 64], AF.Copy)
             dma("Y", "dy", 32, T.yt[:], T.YT[:], "YT0 YT1 YT2 YT3", "yt")
+            ops[-1]["lat"] = 4.0
         else:
             widen(t + 1)
-            shadows(t + 1, "pC", False, "RUL")
-        for k in range(8):
-            n = dict(CLAIM_V).get(k, 0)
-            keys = []
-            for q, c0, c1 in (("V", 0, n), ("S", n, 32)):
-                if c1 > c0:
-                    keys.append("GB%d%s" % (k, q))
-                    c0, c1 = c0 + 32 * k, c1 + 32 * k
-                    look(q, "%s OM%d" % (tabs["Q"], k // 2), keys[-1], 16 * (c1 - c0), T.GB[:, 16 * c0:16 * c1], T.Q[:].indirect(T.OM[:, c0:c1]))
-            pt, a0, h = "pT%d" % (k % 2), 512 * (k % 4), k % 2
-            for m in range(4):
-                op("P", "ID " + " ".join(keys), pt, 128 * CYC, lambda e, m=m, k=k, pt=pt: e.transpose(T[pt][:, 128 * m:128 * m + 128], T.GB[:, 512 * k + m:512 * k + 512:4], mat("ID")))
-            ts("%s WT%d" % (pt, t), "LA%d" % (k % 4), 256, T.LA[:, a0:a0 + 512], T[pt][:, 0:512], T.WH[:, 2 * t + h:2 * t + h + 1], Op.mult)
-            ts(pt, "LB%d" % (k % 4), 256, T.LB[:, a0:a0 + 512], T[pt][:, 0:512], -size[t], Op.add, 0.0, Op.max)
-            for j in range(4):
-                a1 = a0 + 128 * j
-                mm("LA%d LB%d" % (k % 4, k % 4), "pD1", 128, T.pD1[:, 128:256], T.LA[:, a1:a1 + 128], T.LB[:, a1:a1 + 128], k == 0 and j == 0, k == 7 and j == 3)
-        rl, rk = T["RL%d" % t], "recvL%d" % t
-        cp(rk, "LF", 16, lst("LF"), rl[:])
-        ts(rk, "IW", 16, lst("IW"), rl[:], float(W), Op.is_ge, -65536.0, Op.mult)
-        tt("pD1 SL", "CW", 128, T.CW[:], T.pD1[:, 128:256], T.SL[:], Op.mult)
-        tt("CW BL TH0 TH1 TH2 TH3", "BD", looks(256), T.BD[:], T.CW[:].indirect(T.BL[:]), T.TH[:], Op.is_ge)
-        pick("pD0", 0, "BK", "BD", T.BD[:], "MUL", ["NH", "NL"])
+            shadows("pC", "RUL")
+        j0 = 0
+        for k, (q, n) in enumerate(CLAIM):
+            pt, a0 = "pT%d" % (k % NT), 128 * (j0 % 16)
+            look(q, "%s OM%d" % (tabs["Q"], j0 // 8), "GB%d" % k, 128 * n, T.GB[:, 128 * j0:128 * (j0 + n)], T.Q[:].indirect(T.OM[:, 8 * j0:8 * (j0 + n)]))
+            for j in range(n):
+                op("P", "ID GB%d" % k, pt, 128 * CYC, lambda e, j=j, a=128 * (j0 + j), pt=pt: e.transpose(T[pt][:, 128 * j:128 * j + 128], T.GB[:, a:a + 128], mat("ID")))
+            for c in sorted(set((j0 + j) % 8 // 2 for j in range(n))):
+                js = [j for j in range(n) if (j0 + j) % 8 // 2 == c]
+                a, z = 128 * js[0], 128 * js[-1] + 128
+                la, w = " ".join("LA%d" % ((j0 + j) % 16) for j in js), 2.0 ** (11 * (3 - c)) * size[t] ** -2
+                if k in LA_S:
+                    act(pt, la, z - a, T.LA[:, a0 + a:a0 + z], T[pt][:, a:z], AF.Copy, scale=w)
+                else:
+                    ts(pt, la, (z - a) // 2, T.LA[:, a0 + a:a0 + z], T[pt][:, a:z], w, Op.mult)
+            lb = " ".join("LB%d" % ((j0 + j) % 16) for j in range(n))
+            if k in LB_S:
+                act(pt, lb, 128 * n, T.LB[:, a0:a0 + 128 * n], T[pt][:, 0:128 * n], AF.Relu, bias=-size[t])
+            else:
+                ts(pt, lb, 64 * n, T.LB[:, a0:a0 + 128 * n], T[pt][:, 0:128 * n], -size[t], Op.add, 0.0, Op.max)
+            for j in range(j0, j0 + n):
+                a1 = 128 * (j % 16)
+                mm("LA%d LB%d" % (j % 16, j % 16), "pD1", 128, T.pD1[:, 128:256], T.LA[:, a1:a1 + 128], T.LB[:, a1:a1 + 128], j == 0, j == 31)
+            j0 += n
         do = "DO%d" % t
-        tt("MUL IW", do, 32, T[do][:], T.MUL[:, 15::16], lst("IW"), Op.is_lt)
-        mm("ON " + do, "pS0", 16, T.pS0[:, 0:16], mat("ON"), T[do][:], True, True)
-        send(t, "D", T["DR%d" % t][:], T[do][:], do)
-        tt("LF MUL", "E1", 32, lst("E1"), T.MUL[:, 15::16], lst("LF"), Op.max)
-        cp("E1", "OD", 16, T.OD[:], lst("E1"))
-        op("V", "pS0", "AA", vc(16), lambda e: e.tensor_reduce(T.AA[:], T.pS0[:, 0:16], AxisListType.X, Op.add))
-        if not last:
-            for j in range(XS):
-                n = 16 // XS
-                cp("OD recvZ%d" % t, XK, puts(16 * n), T.X[:].indirect(T.OD[:, n * j:n * j + n]), T["ZP%d" % t][:, 16 * n * j:16 * n * j + 16 * n])
+        tt("pD1 SL", "CW", 128, T.CW[:], T.pD1[:, 128:256], T.SL[:], Op.mult)
+        n = 16 // XS
+        for j in range(XS):
+            c, l, bank, sum_ = slice(n * j, n * j + n), slice(16 * n * j, 16 * n * (j + 1)), ("pD0", "pH")[j], T.MUL[:, 16 * n * j + 15:16 * n * (j + 1):16]
+            tt("CW BL TH", "BD%d" % j, looks(16 * n), T.BD[:, l], T.CW[:].indirect(T.BL[:, c]), part("TH", l.start, l.stop), Op.is_ge)
+            mm("ID NH", bank, 16 * n, T[bank][:, l], mat("ID"), T.NH[:, l], True, False)
+            mm("BE D20 D21", bank, 16 * n, T[bank][:, l], mat("BE"), part("D2", l.start, l.stop), False, False)
+            mm("BE BD%d" % j, bank, 16 * n, T[bank][:, l], mat("BE"), T.BD[:, l], False, True)
+            scan("D0 " + bank, "MUL%d" % j, 16 * n, T.MUL[:, l], T.D0[:, l], T[bank][:, l], -8192.0, Op.min, Op.max)
+            tt("IW MUL%d" % j, "%s.%d" % (do, j), 32, T[do][:, c], sum_, part("IW", c.start, c.stop), Op.is_lt)
+            mm("ON %s.%d" % (do, j), "pS0", 16, T.pS0[:, 0:n], mat("ON"), T[do][:, c], j == 0, j == XS - 1)
+            tt("LF MUL%d" % j, "E1%d" % j, 32, part("E1", c.start, c.stop), sum_, part("LF", c.start, c.stop), Op.max)
+            cp("E1%d" % j, "OD%d" % j, 16, T.OD[:, c], part("E1", c.start, c.stop))
+            if not last:
+                cp("OD%d recvZ%d" % (j, t), XK, puts(16 * n), T.X[:].indirect(T.OD[:, c]), T["ZP%d" % t][:, l])
+        send(t, "D", T["DR%d" % t][:], T[do][:], " ".join("%s.%d" % (do, j) for j in range(XS)))
+        op("V", "pS0", "AA", vc(16), lambda e: e.tensor_reduce(T.AA[:], T.pS0[:, 0:n], AxisListType.X, Op.add))
         advance(not last)
         hits(t, LAST_V if last else HITS_V)
         if not last:
@@ -501,7 +564,7 @@ def rank_program(g, core, T, topo):
 
     N = len(ops)
     preds = [dict() for _ in ops]
-    last_w, readers, banks = {}, {}, {}
+    last_w, readers, banks, group = {}, {}, {}, {}
     ends = {}
     for i, o in enumerate(ops):
         def after(j, wake):
@@ -518,8 +581,11 @@ def rank_program(g, core, T, topo):
                     before, now = now, []
                 for j in before:
                     after(j, WAKE)
-                if now and o["q"] == "P":
-                    after(now[-1], 0.0)
+                if o["q"] == "P":
+                    first, final = o.get("ends", (True, True))
+                    for j in (group.get(k, []) if first or final else group[k][:1]):
+                        after(j, 0.0)
+                    group[k] = [i] if first else group[k] + [i]
                 banks[k] = (before, now + [i])
         for k in o["r"]:
             if k[0] != "p" and k in last_w:
@@ -575,13 +641,60 @@ def rank_program(g, core, T, topo):
         ahead = [[(j, wake + ops[j]["lat"]) for j, wake in preds[i].items()] for i in range(N)]
         back = [[(j, wake + ops[i]["lat"]) for j, wake in succs[i]] for i in range(N)]
         turn, best = sorted(range(N), key=lambda i: (-prio[i], i)), None
+
+        def span(end):
+            return max(end[i] + ops[i]["lat"] for i in range(N))
+
+        def started(end):
+            return sorted(range(N), key=lambda i: (end[i] - ops[i]["cost"], i))
         for _ in range(ROUNDS):
             end = place(turn, ahead)
-            if best is None or max(end) < best[0]:
-                best = (max(end), sorted(range(N), key=lambda i: (end[i] - ops[i]["cost"], i)))
+            if best is None or span(end) < best[0]:
+                best = (span(end), end)
             end = place(sorted(range(N), key=lambda i: (-end[i], -i)), back)
             turn = sorted(range(N), key=lambda i: (-end[i], i))
-        ORDER.extend(best[1])
+        seed = 1
+        for _ in range(MOVES):
+            end = best[1]
+            turn = started(end)
+            before, last = {}, {}
+            for i in turn:
+                before[i], last[ops[i]["q"]] = last.get(ops[i]["q"]), i
+            i, held = max(range(N), key=lambda i: end[i] + ops[i]["lat"]), []
+            while i is not None:
+                ready, j = max([(end[j] + gap, j) for j, gap in ahead[i]] + [(0.0, None)])
+                if end[i] - ops[i]["cost"] > ready + 1e-6:
+                    held.append((i, ready))
+                    j = before[i]
+                i = j
+            if not held:
+                break
+            seed = (seed * 1103515245 + 12345) % 2147483648
+            i, ready = held[(seed >> 8) % len(held)]
+            key = {k: float(n) for n, k in enumerate(turn)}
+            j = before[i]
+            if seed >> 6 & 1:
+                key[j], todo = key[i] + 0.5, [j]
+                while todo:
+                    k = todo.pop()
+                    for m, _g in back[k]:
+                        if key[m] <= key[k]:
+                            key[m] = key[k] + 1e-4
+                            todo.append(m)
+            else:
+                while seed >> 7 & 1 and before[j] is not None and end[before[j]] > ready:
+                    j = before[j]
+                key[i], todo = key[j] - 0.5, [i]
+                while todo:
+                    k = todo.pop()
+                    for m, _g in ahead[k]:
+                        if key[m] >= key[k]:
+                            key[m] = key[k] - 1e-4
+                            todo.append(m)
+            end = place(sorted(range(N), key=lambda k: (key[k], k)), ahead)
+            if span(end) <= best[0]:
+                best = (span(end), end)
+        ORDER.extend(started(best[1]))
     order = ORDER
 
     count = {q: 0 for q in eng}

@@ -3,18 +3,18 @@ from concourse.mybir import AluOpType as Op, AxisListType, ActivationFunctionTyp
 W, L, D = 8192, 256, 8448
 KAPPA = (3, 29, 71, 113)
 TS, CAP = 4, 128
-WB = "EX M4 LU LG LW LV L2 T1 TH T2 TC UW D2".split()
+WB = "EX LU LW LV L2 T1 TH T2 TC UW D2".split()
 FL = "L1 L3 R1 R2 LF IW E1 FR FS VF VD BM S4 S5 S6 DM".split()
 IL = "VN VC S1 S2 S3 S7 S8 S9".split()
 QL = "THR VK BK4 SB SQ".split()
-CM = "ID NI BO TG ON BK BE TK T4 O4 A0 A1 A2 A3 B0 B1 B2 B3 C0 C1 C2 C3 U0 U1 U2 U3".split()
+CM = "ID NI BO TG ON BK BE TK T4 O4 A0 A1 A2 A3 B0 B1 B2 B3 C0 C1 C2 C3 U0 U1 U2 U3 W0 W1 W2 W3".split()
 
 SCRATCH = {
     "X": ("sbuf", [128, 2 * D], "bfloat16"),
     "Q": ("sbuf", [128, 8464], "bfloat16"), "HT": ("sbuf", [128, 2 * D], "bfloat16"),
     "OW": ("sbuf", [128, 1024], "bfloat16"),
-    "IO": ("sbuf", [128, 8192], "float32"),
-    "SD": ("sbuf", [128, 256], "bfloat16"), "V0": ("sbuf", [128, 16], "int32"), "TI": ("sbuf", [128, 4], "int32"), "TF": ("sbuf", [128, 4], "float32"),
+    "RF": ("sbuf", [128, 512], "float32"), "RE": ("sbuf", [128, 6], "float32"),
+    "SD": ("sbuf", [128, 256], "bfloat16"), "V0": ("sbuf", [128, 16], "int32"), "TI": ("sbuf", [128, 4], "int32"), "TF": ("sbuf", [128, 8], "float32"),
     "PI": ("sbuf", [128, 8], "int32"), "PF": ("sbuf", [128, 8], "float32"), "KP": ("sbuf", [128, 16], "float32"),
     "RM": ("sbuf", [128, 256], "float32"), "RD": ("sbuf", [128, 256], "float32"), "RP": ("sbuf", [128, 128], "float32"), "RG": ("sbuf", [128, 128], "float32"),
     "J0": ("sbuf", [128, 128], "float32"), "J1": ("sbuf", [128, 128], "float32"), "J2": ("sbuf", [128, 128], "float32"), "J3": ("sbuf", [128, 128], "float32"),
@@ -28,45 +28,50 @@ SCRATCH = {
     "OB": ("sbuf", [128, 64], "bfloat16"),
     "TN": ("sbuf", [128, 256], "int32"), "TR": ("sbuf", [128, 256], "float32"), "P1": ("sbuf", [128, 256], "float32"),
     "P2": ("sbuf", [128, 256], "float32"), "M1": ("sbuf", [128, 256], "float32"), "OM": ("sbuf", [128, 256], "uint16"),
-    "DV": ("sbuf", [128, 256], "uint16"), "OV": ("sbuf", [128, 16], "uint16"), "EA": ("sbuf", [128, 16, 256], "bfloat16"), "OD": ("sbuf", [128, 16], "uint16"), "BL": ("sbuf", [128, 16], "uint16"),
-    "HA": ("sbuf", [128, 64], "bfloat16"), "SC": ("sbuf", [128, 66], "bfloat16"), "HM": ("sbuf", [128, 64], "bfloat16"),
+    "DV": ("sbuf", [128, 256], "uint16"), "EA": ("sbuf", [128, 16, 256], "bfloat16"), "OD": ("sbuf", [128, 16], "uint16"), "BL": ("sbuf", [128, 16], "uint16"),
+    "SC": ("sbuf", [128, 66], "bfloat16"), "HM": ("sbuf", [128, 64], "bfloat16"),
     "FB": ("sbuf", [128, 64], "bfloat16"), "F6": ("sbuf", [128, 32], "bfloat16"), "SY": ("sbuf", [128, 64], "int32"),
-    "WB": ("sbuf", [128, 256 * len(WB)], "bfloat16"), "CV": ("sbuf", [128, 256], "float32"), "CX": ("sbuf", [128, 16], "uint16"), "HUL": ("sbuf", [128, 256], "float32"),
+    "WB": ("sbuf", [128, 256 * len(WB)], "bfloat16"), "CV": ("sbuf", [128, 256], "float32"), "HUL": ("sbuf", [128, 256], "float32"),
     "RUL": ("sbuf", [128, 256], "float32"), "BUL": ("sbuf", [128, 256], "float32"), "MUL": ("sbuf", [128, 256], "float32"),
     "GQ": ("sbuf", [128, 256], "bfloat16"), "AB": ("sbuf", [128, 256], "bfloat16"),
     "BB": ("sbuf", [128, 256], "bfloat16"), "BD": ("sbuf", [128, 256], "bfloat16"), "CW": ("sbuf", [128, 128], "float32"),
     "AA": ("sbuf", [128, 1], "float32"), "YT": ("sbuf", [128, 4, 4, 16], "float32"), "YS": ("sbuf", [128, 32], "float32"),
     "GB": ("sbuf", [128, 4096], "bfloat16"), "HB": ("sbuf", [128, 4096], "bfloat16"), "LA": ("sbuf", [128, 2048], "bfloat16"), "LB": ("sbuf", [128, 2048], "bfloat16"),
-    "Z": ("sbuf", [128, 256], "bfloat16"), "GR": ("sbuf", [128, 1024], "bfloat16"), "H": ("sbuf", [128, 1024], "bfloat16"), "F": ("sbuf", [128, 256], "bfloat16"),
+    "MX": ("sbuf", [128, 256], "bfloat16"), "Z": ("sbuf", [128, 256], "bfloat16"), "GR": ("sbuf", [128, 1024], "bfloat16"), "H": ("sbuf", [128, 1024], "bfloat16"), "F": ("sbuf", [128, 512], "bfloat16"),
     "XI": ("sbuf", [128, 64], "int32"), "OF": ("sbuf", [128, 64], "uint16"),
     "pS0": ("psum", [128, 512], "float32"), "pT2": ("psum", [128, 1024], "bfloat16"), "pD0": ("psum", [128, 512], "float32"), "pD1": ("psum", [128, 512], "float32"),
     "pT0": ("psum", [128, 1024], "bfloat16"), "pT1": ("psum", [128, 1024], "bfloat16"), "pC": ("psum", [128, 512], "float32"), "pH": ("psum", [128, 512], "float32"),
 }
 for _t in range(TS):
-    SCRATCH.update({"ZF%d" % _t: ("sbuf", [128, 256], "bfloat16"), "ZP%d" % _t: ("sbuf", [128, 256], "bfloat16"), "GO%d" % _t: ("sbuf", [128, 64], "bfloat16"),
-                    "RG%d" % _t: ("sbuf", [128, 64], "bfloat16"), "DO%d" % _t: ("sbuf", [128, 16], "bfloat16"), "DR%d" % _t: ("sbuf", [128, 16], "bfloat16"),
+    SCRATCH.update({"ZF%d" % _t: ("sbuf", [128, 256], "bfloat16"), "ZP%d" % _t: ("sbuf", [128, 256], "bfloat16"), "GO%d" % _t: ("sbuf", [128, 128], "bfloat16"),
+                    "RG%d" % _t: ("sbuf", [128, 128], "bfloat16"), "DO%d" % _t: ("sbuf", [128, 16], "bfloat16"), "DR%d" % _t: ("sbuf", [128, 16], "bfloat16"),
                     "MS%d" % _t: ("sbuf", [128, 32], "uint16"), "MR%d" % _t: ("sbuf", [128, 32], "uint16")})
-SEMAPHORES = ["cV", "cS", "cP", "cG", "dx", "dv", "ds", "dt", "dy", "loc"] + ["r%s%d" % (k, t) for k in "MLZD" for t in range(TS)]
-CYC, WAKE, SFIX, LOOK, PUT, REMOTE = 0.00083, 0.15, 0.15, 1.56, 3.8, 3.0
-ROUNDS, SLIP, MOVES = 8, 0.0, 300
-HS, QS = 2, 2
+SEMAPHORES = ["cV", "cS", "cP", "cG", "dx", "dv", "ds", "dt", "dy", "loc", "rN0"] + ["r%s%d" % (k, t) for k in "MLKZD" for t in range(TS)]
+CYC, WAKE, SFIX, LOOK, PUT, REMOTE = 0.00083, 0.25, 0.03, 1.56, 3.8, 3.5
+OWN, VFIX, PCYC, PFIX = 0.24, 0.002, 0.00045, 0.003
+ROUNDS, SLIP, MOVES, STIR = 4, 0.0, 300, 100
+POOL, URGE, MIXES = 30, 8.0, 700
+HS, QS = 1, 1
 ORDER = []
-RUN = ((("V", 28), ("S", 18), ("S", 18)),)
-NS = 1
+RUN = ((("S", 18), ("S", 18), ("V", 28)),)
+NS = len(RUN)
 CW = 64 // NS
-CLAIM = (("S", 2), ("V", 2)) + (("S", 4),) * 6 + (("S", 2), ("V", 2))
-HITS_V = (3, 7, 11)
+CLAIM = (("S", 2), ("V", 2), ("V", 2), ("S", 2)) + (("S", 4),) * 5 + (("S", 2), ("S", 2))
+HITS_V = (5, 11)
 LAST_V = (1, 3, 5, 7, 9, 11, 13, 15)
 GAP = {"S": 0.3, "V": 0.9}
 AHEAD = 0.0
 PAD = {}
+EARLY = 5.0
+BANK = 0.0
+YLAT = 55.0
 FIRST = 3.0
 IOS = 12
 NT = 3
 QV, QS2 = 1000, 4500
 XS = 2
 LA_S, LB_S = (), ()
-MX = False
+MX = True
 
 
 def rank_program(g, core, T, topo):
@@ -79,6 +84,8 @@ def rank_program(g, core, T, topo):
     chain = [None]
 
     def op(q, reads, writes, cost, f, kind="c", sem=None, n=0, lat=0.0):
+        if q == "V" and any(k[0] == "p" for k in reads.split()):
+            cost += BANK
         ops.append({"chain": chain[0], "first": boost[0], "q": q, "r": reads.split(), "w": writes.split(), "cost": cost, "f": f, "kind": kind, "sem": sem, "n": n, "lat": lat + PAD.get(writes, 0.0)})
 
     def dma(q, sem, total, out, in_, reads, writes):
@@ -104,7 +111,7 @@ def rank_program(g, core, T, topo):
         return part(k, 0, 128)
 
     def vc(n):
-        return 0.02 + max(n, 64) * CYC
+        return VFIX + max(n, 64) * CYC
 
     def ts(reads, writes, n, out, in0, s1, o1, s2=None, o2=None):
         if o2 is None:
@@ -119,7 +126,7 @@ def rank_program(g, core, T, topo):
         op("V", reads, writes, vc(n), lambda e: e.tensor_copy(out, in_))
 
     def act(reads, writes, n, out, in_, fn, bias=0.0, scale=1.0):
-        op("S", reads, writes, SFIX + n * CYC, lambda e: e.activation(out, in_, fn, bias=bias, scale=scale))
+        op("S", reads, writes, SFIX + max(n, 64) * CYC, lambda e: e.activation(out, in_, fn, bias=bias, scale=scale))
 
     def look(q, reads, writes, n, out, src):
         if q == "V":
@@ -128,7 +135,7 @@ def rank_program(g, core, T, topo):
             op("S", reads, writes, 0.065 + LOOK * n * CYC, lambda e: e.activation(out, src, AF.Copy))
 
     def mm(reads, writes, n, out, lhsT, rhs, a, z):
-        op("P", reads, writes, max(n, 64) * CYC, lambda e: e.matmul(out, lhsT, rhs, a, z))
+        op("P", reads, writes, PFIX + max(n, 64) * PCYC, lambda e: e.matmul(out, lhsT, rhs, a, z))
         ops[-1]["ends"] = (a, z)
 
     def scan(reads, writes, n, out, d0, d1, init, o0, o1):
@@ -177,15 +184,6 @@ def rank_program(g, core, T, topo):
     op("G", "J4", "MK", 0.17 + 1024 * CYC, lambda e: e.affine_select(T.MK[:], T.J4[:], [[0, 128], [1, 4]], Op.not_equal, 0.0, 0, 0))
     iota("RL", 256, T.RL[:], [[1, 256]], W - D, 0)
     iota("KI", 4, T.KP[:, 0:4], [[1, 4]], 0, 0)
-    boost[0] = FIRST
-    iota("IO0", 512, T.IO[:, 0:512], [[1, 512]], 0, 0)
-    for j in range(1, 16):
-        if j > IOS:
-            ts("IO0", "IO%d" % j, 512, T.IO[:, 512 * j:512 * j + 512], T.IO[:, 0:512], 512.0 * j, Op.add)
-        else:
-            act("IO0", "IO%d" % j, 512, T.IO[:, 512 * j:512 * j + 512], T.IO[:, 0:512], AF.Identity, bias=512.0 * j)
-    boost[0] = 0.0
-    IOK = " ".join("IO%d" % j for j in range(16))
     ts("PI0", "PI1", 1, T.PI[:, 1:2], T.PI[:, 0:1], 15, Op.bitwise_and)
     ts("PI0", "PI2", 1, T.PI[:, 2:3], T.PI[:, 0:1], 4, Op.arith_shift_right)
     ts("PI0", "PI3", 1, T.PI[:, 3:4], T.PI[:, 0:1], 2, Op.arith_shift_right, 3, Op.bitwise_and)
@@ -210,7 +208,12 @@ def rank_program(g, core, T, topo):
     ts("RM PF", "K2", 128, T.K2[:, 0:128], T.RM[:, 0:128], pi, Op.is_gt)
     tt("K2 BO", "TG", 256, mat("TG"), T.K2[:, 0:128], mat("BO"), Op.mult)
     fill("OF32", 128, T.OF32[:], 1.0)
+    for k in range(4):
+        fill("WH", 1, T.RE[64 * (k % 2):64 * (k % 2) + 64, 4 + k // 2:5 + k // 2], 2.0 ** (11 * (3 - k)))
+    ts("KI PF", "RE", 4, T.RE[:, 0:4], T.KP[:, 0:4], 4.0, Op.mult, pi, Op.is_equal)
     for r in range(4):
+        ts("BO RE", "RF%d" % r, 128, T.RF[:, 128 * r:128 * r + 128], mat("BO"), T.RE[:, r:r + 1], Op.mult)
+        ts("BO RE", "W%d" % r, 64, mat("W%d" % r), mat("BO"), T.RE[:, r:r + 1], Op.mult)
         ts("J2 PF", "B%d" % r, 128, mat("B%d" % r), T.J2[:], pg, Op.subtract, 1000.0 * r, Op.is_equal)
         ts("B%d" % r, "A%d" % r, 64, mat("A%d" % r), mat("B%d" % r), -0.5, Op.mult)
         ts("J0 PF", "C%d" % r, 128, mat("C%d" % r), T.J0[:], p, Op.subtract, 1000.0 * r, Op.is_equal)
@@ -218,7 +221,7 @@ def rank_program(g, core, T, topo):
         ts("UF%d" % r, "U%d" % r, 128, mat("U%d" % r), T.UF[:, 128 * r:128 * r + 128], float(D), Op.mult)
         for m in range(4):
             op("G", "OF32", "YM%d%d" % (m, r), 0.17 + 256 * CYC, lambda e, m=m, r=r: e.affine_select(
-                T.YM[:, 512 * m + 128 * r:512 * m + 128 * r + 128], T.OF32[:], [[16, 8], [1000, 4], [4, 4]], Op.is_equal, 0.0, m - 1000 * r, -1))
+                T.YM[:, 512 * m + 128 * r:512 * m + 128 * r + 128], T.OF32[:], [[16, 8], [1000, 4], [4, 4]], Op.is_equal, 0.0, m - 1000 * r, -1), lat=YLAT)
     ts("J3 PF", "J3", 128, T.J3[:], T.J3[:], pr, Op.is_gt, 8192.0, Op.mult)
     tt("J3 BO", "J3", 256, T.J3[:], T.J3[:], mat("BO"), Op.mult)
     ts("ID", "O4", 64, mat("O4"), mat("ID"), -32768.0 * CAP, Op.mult)
@@ -243,10 +246,6 @@ def rank_program(g, core, T, topo):
         ts("HUL", "UW", 128, part("UW", 128 * h, 128 * h + 128), T.HUL[:, 0:128], 2.5, Op.mult)
     tt("HUL ID", "CV", 256, T.CV[:, 0:128], T.HUL[:, 0:128], mat("ID"), Op.mult)
     op("V", "CV", "UP", vc(128), lambda e: e.tensor_reduce(T.KP[:, 15:16], T.CV[:, 0:128], AxisListType.X, Op.add))
-    iota("L1", 16, lst("L1"), [[4, 16]], 0, 0)
-    ts("L1 PF", "CX", 16, T.CX[:], lst("L1"), pr, Op.add)
-    iota("M4", 256, wide("M4"), [[0, 64], [4, 4]], 0, 0)
-    ts("M4 PF", "M4", 128, wide("M4"), wide("M4"), pi, Op.is_equal)
     fill("OB", 32, T.OB[:], 1.0)
     for t in range(TS):
         fill("OW%d" % t, 128, T.OW[:, 256 * t:256 * t + 256], 32.0 ** (t + 1 - TS))
@@ -258,7 +257,8 @@ def rank_program(g, core, T, topo):
     for k in range(4):
         fill("TC", 32, part("TC", 64 * k, 64 * k + 64), 0.75 * 2.0 ** (11 * (3 - k) - 46))
     fill("AA", 1, T.AA[:], 0.0)
-    cp("TI", "TF", 4, T.TF[:], T.TI[:])
+    cp("TI", "TF", 4, T.TF[:, 0:4], T.TI[:])
+    ts("TI", "TG4", 4, T.TF[:, 4:8], T.TI[:], 1.0, Op.max, -1.0, Op.mult)
     ts("RD PF", "K2", 256, T.K2[:], T.RD[:], pi, Op.is_equal, 2.0, Op.mult)
     tt("K1 K2", "K3", 512, T.K3[:], T.K1[:], T.K2[:], Op.mult)
     ts("K3", "K3", 256, T.K3[:], T.K3[:], 4194304.0, Op.mult)
@@ -284,8 +284,9 @@ def rank_program(g, core, T, topo):
         return " ".join(k + str(h) for h in range(NS))
 
     def sums(m, src, key, h, first, final):
+        bank, a, n = ("pS0", 0, 64) if h is None else (("pS0", "pD0")[h], CW * h, CW)
         for r in range(4):
-            mm("%s%d %s" % (m, r, key), "pS%d" % h, CW, T["pS%d" % h][:, 0:CW], mat("%s%d" % (m, r)), src(slice(4 * CW * h + r, 4 * CW * h + 4 * CW, 4)), first and r == 0, final and r == 3)
+            mm("%s%d %s" % (m, r, key), bank, n, T[bank][:, 0:n], mat("%s%d" % (m, r)), src(slice(4 * a + r, 4 * a + 4 * n, 4)), first and r == 0, final and r == 3)
 
     def pick(bank, a, lhs, key, src, out, under):
         for k in under:
@@ -294,44 +295,37 @@ def rank_program(g, core, T, topo):
         scan("D0 " + bank, out, 256, T[out][:], T.D0[:], T[bank][:, a:a + 256], -8192.0, Op.min, Op.max)
 
     def step(t, b):
-        Z, zk = (T.SD, "SD SD") if b == 0 else (T.Z, "Z0 Z1")
-        if b:
-            tt("pS0 VK", "XI0", 64, T.XI[:], T.pS0[:, 64:128], quad("VK"), Op.add)
-        if b < 3 and MX:
-            sums("A", lambda l: Z[:, l], zk, 0, True, False)
-        ts("XI0", "TN%d0" % b, 64, T.TN[:, 64 * b:64 * b + 64], T.XI[:], W - 1, Op.bitwise_and)
-        cp("TN%d0" % b, "OF", 64, T.OF[:], T.TN[:, 64 * b:64 * b + 64])
-        c0, hk, mk, shares = 0, "", "", []
-        for h, share in enumerate(RUN):
-            c1, keys = c0, ""
-            for j, (q, n) in enumerate(share):
-                key, lanes, four = "%d.%d" % (h, j), slice(4 * c0, 4 * c0 + 4 * n), slice(16 * c0, 16 * c0 + 16 * n)
-                look(q, XK + " OF", "GR" + key, 16 * n, T.GR[:, four], T.X[:, 0:W].indirect(T.OF[:, c0:c0 + n]))
-                scan("MK GR" + key, "H" + key, 8 * n, T.H[:, four], T.MK[:, 0:16 * n], T.GR[:, four], 0.0, Op.mult, Op.max)
-                if b < 3 and MX:
-                    tt("H%s %s" % (key, zk), "MX" + key, 8 * n, T.MX[:, lanes], T.H[:, 16 * c0 + 3:16 * c0 + 16 * n:4], Z[:, lanes], Op.max)
-                c0, keys, mk = c0 + n, keys + " H" + key, mk + " MX" + key
-            hk += keys
-            shares.append((h, c1, c0, keys))
-        if b < 3 and MX:
-            sums("A", lambda l: T.H[:, 4 * l.start + 3:4 * l.stop:16], hk, 0, False, False)
-            sums("B", lambda l: T.MX[:, l], mk, 0, False, True)
-            act("K2K", "pS0", 64, T.pS0[:, 64:128], T.pS0[:, 0:64], AF.Square, bias=k2k, scale=0.5)
-        for h, c1, c0, keys in shares:
-            d, n, lanes = "pD%d" % h, 4 * (c0 - c1), slice(4 * c1, 4 * c0)
-            mm("NI " + zk, d, n, T[d][:, 0:n], mat("NI"), Z[:, lanes], True, False)
-            mm("ID " + keys, d, n, T[d][:, 0:n], mat("ID"), T.H[:, 16 * c1 + 3:16 * c0:4], False, True)
-        for h, c1, c0, keys in shares:
-            d, n, lanes = "pD%d" % h, 4 * (c0 - c1), slice(4 * c1, 4 * c0)
-            wide = h == len(RUN) - 1 == 0
+        for h in range(NS):
+            Z, zk = (T.SD, "SD") if b == 0 else (T.Z, "Z%d" % h)
+            bank, cols, a, w = ("pS0", "pD0")[h], slice(CW * h, CW * h + CW), 64 * b + CW * h, 4 * CW
+            xi, tn, of = "XI%d" % h, "TN%d%d" % (b, h), "OF%d" % h
+            if b:
+                tt(bank + " VK", xi, CW, T.XI[:, cols], T[bank][:, 64:64 + CW], quad("VK", h), Op.add)
             if b < 3:
-                act(d, "Z0 Z1" if wide else "Z%d" % h, n, T.Z[:, lanes], T[d][:, 0:n], AF.Abs)
+                sums("A", lambda l: Z[:, l], zk, h, True, False)
+            if NS == 1:
+                mm("ID " + zk, "pD0", 256, T.pD0[:, 0:256], mat("ID"), Z[:], True, True)
+            ts(xi, tn, CW, T.TN[:, a:a + CW], T.XI[:, cols], W - 1, Op.bitwise_and)
+            cp(tn, of, CW, T.OF[:, cols], T.TN[:, a:a + CW])
+            c0, hk, mk = CW * h, "", ""
+            for j, (q, n) in enumerate(RUN[h]):
+                key, lanes, four = "%d.%d" % (h, j), slice(4 * c0, 4 * c0 + 4 * n), slice(16 * c0, 16 * c0 + 16 * n)
+                look(q, XK + " " + of, "GR" + key, 16 * n, T.GR[:, four], T.X[:, 0:W].indirect(T.OF[:, c0:c0 + n]))
+                scan("MK GR" + key, "H" + key, 8 * n, T.H[:, four], T.MK[:, 0:16 * n], T.GR[:, four], 0.0, Op.mult, Op.max)
+                z, zz, cost = (T.pD0, "pD0", 4 * n) if NS == 1 else (Z, zk, 8 * n)
+                tt("H%s %s" % (key, zz), "MX" + key, cost, T.MX[:, lanes], z[:, lanes], T.H[:, 16 * c0 + 3:16 * c0 + 16 * n:4], Op.max if b < 3 else Op.subtract)
+                c0, hk, mk = c0 + n, hk + " H" + key, mk + " MX" + key
+            if b < 3:
+                sums("A", lambda l: T.H[:, 4 * l.start + 3:4 * l.stop:16], hk, h, False, False)
+                sums("B", lambda l: T.MX[:, l], mk, h, False, True)
+                act("K2K", bank, CW, T[bank][:, 64:64 + CW], T[bank][:, 0:CW], AF.Square, bias=k2k, scale=0.5)
+                mm("NI " + zk, "pD1", w, T.pD1[:, 0:w], mat("NI"), Z[:, hs(h)], True, False)
+                mm("ID " + hk, "pD1", w, T.pD1[:, 0:w], mat("ID"), T.H[:, 4 * w * h + 3:4 * w * h + 4 * w:4], False, True)
+                act("pD1", "Z%d" % h, w, T.Z[:, hs(h)], T.pD1[:, 0:w], AF.Abs)
             else:
-                act(d, "ZF%d.%d" % (t, h), n, T["ZF%d" % t][:, lanes], T[d][:, 0:n], AF.Abs)
-                ts("ZF%d.%d TF" % (t, h), "F0 F1" if wide else "F%d" % h, n // 2, T.F[:, lanes], T["ZF%d" % t][:, lanes], T.TF[:, t:t + 1], Op.is_ge)
-        if b < 3 and not MX:
-            sums("B", lambda l: T.Z[:, l], "Z0 Z1", 0, True, True)
-            act("K2K", "pS0", 64, T.pS0[:, 64:128], T.pS0[:, 0:64], AF.Square, bias=k2k, scale=0.25)
+                ts(mk + " TF", "FA%d" % h, w // 2, T.F[:, hs(h)], T.MX[:, hs(h)], T.TF[:, t:t + 1], Op.is_ge)
+                ts(mk + " TG4", "FB%d" % h, w // 2, T.F[:, 256 + w * h:256 + w * h + w], T.MX[:, hs(h)], T.TF[:, 4 + t:5 + t], Op.is_le)
+                act(mk, "ZF%d.%d" % (t, h), w, T["ZF%d" % t][:, hs(h)], T.MX[:, hs(h)], AF.Abs)
 
     def trails(t, b):
         cols, tn = slice(64 * b, 64 * b + 64), both("TN%d" % b)
@@ -343,37 +337,41 @@ def rank_program(g, core, T, topo):
             tt("P1%d P2%d" % (b, b), "TR%d" % b, 128, T.TR[:, cols], T.P2[:, cols], T.P1[:, cols], Op.min)
 
     def halts(t):
-        for h in range(NS):
-            sums("B", lambda l: T.F[:, l], "F0 F1", h, True, True)
-            tt("pS%d THR" % h, "HA%d" % h, CW, T.HA[:, CW * h:CW * h + CW], T["pS%d" % h][:, 0:CW], quad("THR", h), Op.is_ge)
-        ha = both("HA")
-        act(ha, "HM", 64, T.HM[:], T.HA[:], AF.Identity, bias=-2.0 ** 31, scale=2.0 ** 31)
+        sums("B", lambda l: T.F[:, l], both("FA"), None, True, False)
+        sums("B", lambda l: T.F[:, 256 + l.start:512:4], both("FB"), None, False, True)
+        ha, HA = "HA%d" % t, T["GO%d" % t][:, 0:64]
+        tt("pS0 THR", ha, 64, HA, T.pS0[:, 0:64], quad("THR"), Op.is_ge)
+        send(t, "L", T["RG%d" % t][:, 0:64], HA, ha)
+        ts(ha, "HM", 32, T.HM[:], HA, -1.0, Op.add, 2.0 ** 31, Op.mult)
         mm("ID FB", "pC", 64, T.pC[:, 0:64], mat("ID"), T.FB[:], True, False)
-        mm("T4 " + ha, "pC", 64, T.pC[:, 0:64], mat("T4"), T.HA[:], False, False)
-        scan("OB " + ha, "SC1", 32, T.SC[:, 1:65], T.OB[:], T.HA[:], 0.0, Op.mult, Op.add)
+        mm("T4 " + ha, "pC", 64, T.pC[:, 0:64], mat("T4"), HA, False, False)
+        scan("OB " + ha, "SC1", 32, T.SC[:, 1:65], T.OB[:], HA, 0.0, Op.mult, Op.add)
         mm("O4 SC0 SC1", "pC", 64, T.pC[:, 0:64], mat("O4"), T.SC[:, 0:64], False, True)
         for b in range(4):
             cols = slice(64 * b, 64 * b + 64)
             tt("TR%d pC" % b, "M1%d" % b, 64, T.M1[:, cols], T.pC[:, 0:64], T.TR[:, cols], Op.max)
             ts("M1%d" % b, "OM%d" % b, 64, T.OM[:, cols], T.M1[:, cols], float(D), Op.min)
-        tt("pC HM", "GO%d" % t, 64, T["GO%d" % t][:], T.pC[:, 0:64], T.HM[:], Op.is_lt)
+        tt("pC HM", "GO%d" % t, 64, T["GO%d" % t][:, 64:128], T.pC[:, 0:64], T.HM[:], Op.is_lt)
+        send(t, "K", T["RG%d" % t][:, 64:128], T["GO%d" % t][:, 64:128], "GO%d" % t)
 
     def firsts(t):
         rg, rk = T["RG%d" % t], "recvL%d" % t
-        tt(rk + " CX M4", "EX", looks(256), wide("EX"), rg[:].indirect(T.CX[:]), wide("M4"), Op.mult)
+        for r in range(4):
+            mm("W%d %s" % (r, rk), "pH", 64, T.pH[:, r:256:4], mat("W%d" % r), rg[:, 0:64], True, True)
+        tt("pH LU", "EX", 256, wide("EX"), T.pH[:, 0:256], wide("LU"), Op.mult)
         for h in range(2):
-            mm("EX BO", "pH", 128, T.pH[:, 128 * h:128 * h + 128], part("EX", 128 * h, 128 * h + 128), mat("BO"), True, True)
-        tt("pH LU", "LW", 256, wide("LW"), T.pH[:, 0:256], wide("LU"), Op.mult)
-        tt("pH LG", "LV", 128, part("LV", 0, 128), T.pH[:, 0:128], part("LG", 0, 128), Op.mult)
-        mm("LW L2", "pH", 128, T.pH[:, 256:384], part("LW", 0, 128), part("L2", 0, 128), True, True)
-        mm("LW L2", "pH", 128, T.pH[:, 384:512], part("LW", 128, 256), part("L2", 128, 256), True, False)
-        mm("LV L2", "pH", 128, T.pH[:, 384:512], part("LV", 0, 128), part("L2", 0, 128), False, True)
-        act("pH", "CV", 256, T.CV[:], T.pH[:, 256:512], AF.Copy)
+            mm("EX ID", "pH", 128, T.pH[:, 256 + 128 * h:384 + 128 * h], part("EX", 128 * h, 128 * h + 128), mat("ID"), True, True)
+        ts("pH UP", "LW", 256, wide("LW"), T.pH[:, 256:512], T.KP[:, 15:16], Op.mult)
+        ts("pH", "LV", 128, part("LV", 0, 128), T.pH[:, 256:384], 2.0 ** 64, Op.mult)
+        mm("LW L2", "pH", 128, T.pH[:, 0:128], part("LW", 0, 128), part("L2", 0, 128), True, True)
+        mm("LW L2", "pH", 128, T.pH[:, 128:256], part("LW", 128, 256), part("L2", 128, 256), True, False)
+        mm("LV L2", "pH", 128, T.pH[:, 128:256], part("LV", 0, 128), part("L2", 0, 128), False, True)
+        act("pH", "CV", 256, T.CV[:], T.pH[:, 0:256], AF.Copy)
         for h in range(2):
             a = 128 * h
             tt("CV BL TH", "D2%d" % h, looks(128), part("D2", a, a + 128), T.CV[:, a:a + 128].indirect(T.BL[:, 8 * h:8 * h + 8]), part("T2", a, a + 128), Op.is_ge)
         for q in range(4):
-            mm("C%d %s" % (q, rk), "pS0", 16, T.pS0[:, 64:80], mat("C%d" % q), rg[:, q:64:4], q == 0, q == 3)
+            mm("C%d recvK%d" % (q, t), "pS0", 16, T.pS0[:, 64:80], mat("C%d" % q), rg[:, 64 + q:128:4], q == 0, q == 3)
         act("pS0", "IW", 16, lst("IW"), T.pS0[:, 64:80], AF.Identity, bias=-65536.0, scale=65536.0)
         tt("pS0 VD", "L1", 16, lst("L1"), T.pS0[:, 64:80], lst("VD"), Op.mult)
         tt("L1 DM", "LF", 32, lst("LF"), lst("L1"), lst("DM"), Op.add)
@@ -406,10 +404,16 @@ def rank_program(g, core, T, topo):
         cp("VN", ms + "v", 16, T[ms][:, 16:32], lst("VN"))
         cp("VN", "VF", 16, lst("VF"), lst("VN"))
         listed("RUL", "VF", "R1", "R2", T[ms][:, 0:16], ms + "r")
-        send(t, "M", T["MR%d" % t][:], T[ms][:], ms + "v " + ms + "r")
+        if t:
+            send(t, "M", T["MR%d" % t][:], T[ms][:], ms + "v " + ms + "r")
+        else:
+            send(t, "N", T.MR0[:, 16:32], T.MS0[:, 16:32], ms + "v MK RD")
+            ops[-1]["lat"] += EARLY
+            ops[-1]["cost"] = 1.0
+            send(t, "M", T.MR0[:, 0:16], T.MS0[:, 0:16], ms + "r")
 
     def prepare(t):
-        mr, rk, s = T["MR%d" % t], "recvM%d" % t, size[t]
+        mr, rk, s = T["MR%d" % t], "recvM%d" % t + " recvN0" * (t == 0), size[t]
         for j in range(QS):
             n = 16 // QS
             cp("%s CO%d %s" % (rk, t, tabs["Q"]), tabs["Q"], puts(16 * n), T.Q[:, 0:8448].indirect(mr[:, n * j:n * j + n]), T.CO[:, 256 * t + 16 * n * j:256 * t + 16 * n * (j + 1)])
@@ -423,11 +427,10 @@ def rank_program(g, core, T, topo):
             mm("ID T1", "pD1", 256, T.pD1[:, 256 * j:256 * j + 256], mat("ID"), wide("T1"), True, False)
             mm("ID " + k, "pD1", 256, T.pD1[:, 256 * j:256 * j + 256], mat("ID"), wide(k), False, True)
         act("pD1", "TH", 512, part("TH", 0, 512), T.pD1[:], AF.Copy)
-        for j, k in enumerate(("AB", "AB", "GQ", "GQ")):
-            op("P", "ID " + k, "pT0", 128 * CYC, lambda e, j=j, k=k: e.transpose(T.pT0[:, 128 * j:128 * j + 128], T[k][:, 128 * (j % 2):128 * (j % 2) + 128], mat("ID")))
-        ts("pT0 UP", "LU", 128, wide("LU"), T.pT0[:, 0:256], s, Op.not_equal, T.KP[:, 15:16], Op.mult)
-        ts("pT0", "LG", 64, part("LG", 0, 128), T.pT0[:, 0:128], s, Op.not_equal, 2.0 ** 64, Op.mult)
-        ts("pT0", "L2", 128, wide("L2"), T.pT0[:, 256:512], 1.5 * s, Op.is_ge)
+        for j in range(2):
+            op("P", "ID GQ", "pT0", PFIX + 128 * PCYC, lambda e, j=j: e.transpose(T.pT0[:, 128 * j:128 * j + 128], T.GQ[:, 128 * j:128 * j + 128], mat("ID")))
+        ts("AB", "LU", 128, wide("LU"), T.AB[:], s, Op.not_equal)
+        ts("pT0", "L2", 128, wide("L2"), T.pT0[:, 0:256], 1.5 * s, Op.is_ge)
         cp(rk, "L3", 16, lst("L3"), mr[:, 16:32])
         tt("L3 DM", "VD", 32, lst("VD"), lst("L3"), lst("DM"), Op.subtract)
 
@@ -439,8 +442,9 @@ def rank_program(g, core, T, topo):
             mm("UF%d %s" % (q, bm), "pC", 256, T.pC[:, 128 + q:192:4], T.UF[:, 128 * q:128 * q + 128], lst(bm), True, True)
         act("pC KOF", "BK4", 64, quad("BK4"), T.pC[:, 128:192], AF.Identity, bias=kof)
         tt("pC SY", "SB", 64, quad("SB"), T.pC[:, 128:192], T.SY[:], Op.add)
-        cp("S9", "OV", 16, T.OV[:], lst("S9"))
-        cp("OV " + IOK, dv, looks(256), T[dv][:], T.IO[:].indirect(T.OV[:]))
+        for r in range(4):
+            mm("RF%d BK4" % r, "pC", 256, T.pC[:, 256 + r:512:4], T.RF[:, 128 * r:128 * r + 128], quad("BK4"), True, True)
+        ts("pC", dv, 256, T[dv][:], T.pC[:, 256:512], 4.0 * KAPPA[0] ** 2 + 0.25, Op.add)
 
     def base():
         ts("VC", "S1", 16, lst("S1"), lst("VC"), 4095, Op.bitwise_and)
@@ -479,10 +483,9 @@ def rank_program(g, core, T, topo):
         act("pH", "THR", 64, quad("THR"), T.pH[:, 256:320], AF.Identity, bias=9.0)
         act("pH", "FB", 64, T.FB[:], T.pH[:, 256:320], AF.Identity, bias=16384.0, scale=-131072.0)
 
-    for h in range(NS):
-        sums("B", lambda l: T.SD[:, l], "SD", h, True, True)
-        act("pS%d K2K" % h, "SQ%d" % h, CW, quad("SQ", h), T["pS%d" % h][:, 0:CW], AF.Square, bias=k2k, scale=0.25)
-    ts(both("SQ") + " KOF", "SY", 64, T.SY[:], quad("SQ"), kof, Op.add)
+    sums("B", lambda l: T.SD[:, l], "SD", None, True, True)
+    act("pS0 K2K", "SQ", 64, quad("SQ"), T.pS0[:, 0:64], AF.Square, bias=k2k, scale=0.25)
+    ts("SQ KOF", "SY", 64, T.SY[:], quad("SQ"), kof, Op.add)
     cp("V0", "VC", 16, lst("VC"), T.V0[:])
     cp("V0", "S8", 16, lst("S8"), T.V0[:])
     widen(0)
@@ -501,8 +504,7 @@ def rank_program(g, core, T, topo):
         prepare(t)
         halts(t)
         if not last:
-            send(t, "Z", T["ZP%d" % t][:], T[zf][:], " ".join("%s.%d" % (zf, h) for h in range(len(RUN))))
-        send(t, "L", T["RG%d" % t][:], T["GO%d" % t][:], "GO%d" % t)
+            send(t, "Z", T["ZP%d" % t][:], T[zf][:], both(zf + "."))
         firsts(t)
         if last:
             for m in range(4):
@@ -520,15 +522,14 @@ def rank_program(g, core, T, topo):
             pt, a0 = "pT%d" % (k % NT), 128 * (j0 % 16)
             look(q, "%s OM%d" % (tabs["Q"], j0 // 8), "GB%d" % k, 128 * n, T.GB[:, 128 * j0:128 * (j0 + n)], T.Q[:].indirect(T.OM[:, 8 * j0:8 * (j0 + n)]))
             for j in range(n):
-                op("P", "ID GB%d" % k, pt, 128 * CYC, lambda e, j=j, a=128 * (j0 + j), pt=pt: e.transpose(T[pt][:, 128 * j:128 * j + 128], T.GB[:, a:a + 128], mat("ID")))
-            for c in sorted(set((j0 + j) % 8 // 2 for j in range(n))):
-                js = [j for j in range(n) if (j0 + j) % 8 // 2 == c]
-                a, z = 128 * js[0], 128 * js[-1] + 128
-                la, w = " ".join("LA%d" % ((j0 + j) % 16) for j in js), 2.0 ** (11 * (3 - c)) * size[t] ** -2
-                if k in LA_S:
-                    act(pt, la, z - a, T.LA[:, a0 + a:a0 + z], T[pt][:, a:z], AF.Copy, scale=w)
-                else:
-                    ts(pt, la, (z - a) // 2, T.LA[:, a0 + a:a0 + z], T[pt][:, a:z], w, Op.mult)
+                src = T.GB[:, 128 * j0 + j:128 * (j0 + 4):4] if n == 4 else T.GB[:, 128 * (j0 + j):128 * (j0 + j + 1)]
+                op("P", "ID GB%d" % k, pt, PFIX + 128 * PCYC, lambda e, j=j, src=src, pt=pt: e.transpose(T[pt][:, 128 * j:128 * j + 128], src, mat("ID")))
+            la = " ".join("LA%d" % ((j0 + j) % 16) for j in range(n))
+            if n == 4:
+                h = j0 % 8 // 4
+                ts(pt + " WH", la, 256, T.LA[:, a0:a0 + 512], T[pt][:, 0:512], T.RE[:, 4 + h:5 + h], Op.mult, size[t] ** -2, Op.mult)
+            else:
+                ts(pt, la, 64 * n, T.LA[:, a0:a0 + 128 * n], T[pt][:, 0:128 * n], 2.0 ** (11 * (3 - j0 % 8 // 2)) * size[t] ** -2, Op.mult)
             lb = " ".join("LB%d" % ((j0 + j) % 16) for j in range(n))
             if k in LB_S:
                 act(pt, lb, 128 * n, T.LB[:, a0:a0 + 128 * n], T[pt][:, 0:128 * n], AF.Relu, bias=-size[t])
@@ -555,7 +556,7 @@ def rank_program(g, core, T, topo):
             if not last:
                 cp("OD%d recvZ%d" % (j, t), XK, puts(16 * n), T.X[:].indirect(T.OD[:, c]), T["ZP%d" % t][:, l])
         send(t, "D", T["DR%d" % t][:], T[do][:], " ".join("%s.%d" % (do, j) for j in range(XS)))
-        op("V", "pS0", "AA", vc(16), lambda e: e.tensor_reduce(T.AA[:], T.pS0[:, 0:n], AxisListType.X, Op.add))
+        op("V", "pS0", "AA", vc(16), lambda e, n=n: e.tensor_reduce(T.AA[:], T.pS0[:, 0:n], AxisListType.X, Op.add))
         advance(not last)
         hits(t, LAST_V if last else HITS_V)
         if not last:
@@ -569,6 +570,8 @@ def rank_program(g, core, T, topo):
     for i, o in enumerate(ops):
         def after(j, wake):
             if j != i:
+                if wake and ops[j]["q"] == o["q"] and ops[j]["kind"] == "c":
+                    wake = OWN
                 preds[i][j] = max(preds[i].get(j, 0.0), wake)
         if o["chain"]:
             if o["chain"] in ends:
@@ -615,22 +618,23 @@ def rank_program(g, core, T, topo):
             best = max(best, wake + ops[i]["lat"] + gap + prio[j])
         prio[i] = best + ops[i]["cost"] + ops[i]["first"]
 
+    costs, queues = [o["cost"] for o in ops], [o["q"] for o in ops]
+
     def place(turn, behind):
         end = [0.0] * N
         taken = {q: ([], []) for q in eng}
         for i in turn:
-            t0 = max([end[j] + gap for j, gap in behind[i]] + [0.0])
-            cost = ops[i]["cost"]
-            a, z = taken[ops[i]["q"]]
-            lo, hi = 0, len(z)
-            while lo < hi:
-                mid = (lo + hi) // 2
-                if z[mid] <= t0:
-                    lo = mid + 1
-                else:
-                    hi = mid
-            while lo < len(a) and a[lo] < t0 + cost - SLIP:
-                t0 = max(t0, z[lo])
+            t0 = 0.0
+            for j, gap in behind[i]:
+                if end[j] + gap > t0:
+                    t0 = end[j] + gap
+            cost = costs[i]
+            a, z = taken[queues[i]]
+            lo = n = len(z)
+            while lo and z[lo - 1] > t0:
+                lo -= 1
+            while lo < n and a[lo] < t0 + cost:
+                t0 = z[lo]
                 lo += 1
             a.insert(lo, t0)
             z.insert(lo, t0 + cost)
@@ -647,13 +651,35 @@ def rank_program(g, core, T, topo):
 
         def started(end):
             return sorted(range(N), key=lambda i: (end[i] - ops[i]["cost"], i))
-        for _ in range(ROUNDS):
-            end = place(turn, ahead)
-            if best is None or span(end) < best[0]:
-                best = (span(end), end)
-            end = place(sorted(range(N), key=lambda i: (-end[i], -i)), back)
-            turn = sorted(range(N), key=lambda i: (-end[i], i))
-        seed = 1
+        def polish(turn, rounds):
+            best = None
+            for n in range(rounds):
+                end = place(turn, ahead)
+                if best is None or span(end) < best[0]:
+                    best = (span(end), end)
+                if n < rounds - 1:
+                    end = place(sorted(range(N), key=lambda i: (-end[i], -i)), back)
+                    turn = sorted(range(N), key=lambda i: (-end[i], i))
+            return best
+        seed, pool = 1, [polish(turn, ROUNDS)]
+        for _ in range(POOL):
+            key = list(prio)
+            for i in range(N - 1, -1, -1):
+                seed = (seed * 1103515245 + 12345) % 2147483648
+                key[i] = max([key[i] + URGE * (seed >> 12 & 255) / 255 * (seed >> 8 & 7 == 0)] + [key[j] + 1e-4 for j, _g in back[i]])
+            pool.append(polish(sorted(range(N), key=lambda i: (-key[i], i)), ROUNDS))
+        for _ in range(MIXES):
+            seed = (seed * 1103515245 + 12345) % 2147483648
+            pool.sort(key=lambda x: x[0])
+            one, other = pool[(seed >> 8) % len(pool)], pool[(seed >> 16) % len(pool)]
+            seed = (seed * 1103515245 + 12345) % 2147483648
+            cut = one[0] * (seed >> 8 & 1023) / 1024
+            head = [i for i in started(one[1]) if one[1][i] - ops[i]["cost"] < cut]
+            seen = set(head)
+            child = polish(head + [i for i in started(other[1]) if i not in seen], 1 + (seed >> 20 & 1))
+            if child[0] < pool[-1][0] and all(abs(child[0] - x[0]) > 1e-6 for x in pool):
+                pool[-1] = child
+        best = min(pool, key=lambda x: x[0])
         for _ in range(MOVES):
             end = best[1]
             turn = started(end)
@@ -673,7 +699,14 @@ def rank_program(g, core, T, topo):
             i, ready = held[(seed >> 8) % len(held)]
             key = {k: float(n) for n, k in enumerate(turn)}
             j = before[i]
-            if seed >> 6 & 1:
+            if seed >> 5 & 1:
+                n = int(key[i])
+                for k in turn[max(0, n - 20 - (seed >> 10 & 127)):n + 10]:
+                    seed = (seed * 1103515245 + 12345) % 2147483648
+                    key[k] += STIR * ((seed >> 8 & 255) / 255 - 0.5) * (seed >> 16 & 3 == 0)
+                for k in range(N):
+                    key[k] = max([key[k]] + [key[m] + 1e-4 for m, _g in ahead[k]])
+            elif seed >> 6 & 1:
                 key[j], todo = key[i] + 0.5, [j]
                 while todo:
                     k = todo.pop()

from concourse.mybir import AluOpType as Op, AxisListType, ActivationFunctionType as AF

W, L, D = 8192, 256, 8448
KAPPA = (3, 29, 71, 113)
TS, CAP = 4, 128
WB = "EX LU LW LV L2 T1 TH T2 TC UW D2".split()
FL = "L1 L3 R1 R2 LF IW E1 FR FS VF VD BM S4 S5 S6 DM".split()
IL = "VN VC S1 S2 S3 S7 S8 S9".split()
QL = "THR VK BK4 SB SQ".split()
CM = "ID NI BO TG ON BK BE TK T4 O4 A0 A1 A2 A3 B0 B1 B2 B3 C0 C1 C2 C3 U0 U1 U2 U3 W0 W1 W2 W3".split()

SCRATCH = {
    "X": ("sbuf", [128, 2 * D], "bfloat16"),
    "Q": ("sbuf", [128, 8464], "bfloat16"), "HT": ("sbuf", [128, 2 * D], "bfloat16"),
    "OW": ("sbuf", [128, 1024], "bfloat16"),
    "RF": ("sbuf", [128, 512], "float32"), "RE": ("sbuf", [128, 6], "float32"),
    "SD": ("sbuf", [128, 256], "bfloat16"), "V0": ("sbuf", [128, 16], "int32"), "TI": ("sbuf", [128, 4], "int32"), "TF": ("sbuf", [128, 8], "float32"),
    "PI": ("sbuf", [128, 8], "int32"), "PF": ("sbuf", [128, 8], "float32"), "KP": ("sbuf", [128, 16], "float32"),
    "RM": ("sbuf", [128, 256], "float32"), "RD": ("sbuf", [128, 256], "float32"), "RP": ("sbuf", [128, 128], "float32"), "RG": ("sbuf", [128, 128], "float32"),
    "J0": ("sbuf", [128, 128], "float32"), "J1": ("sbuf", [128, 128], "float32"), "J2": ("sbuf", [128, 128], "float32"), "J3": ("sbuf", [128, 128], "float32"),
    "J4": ("sbuf", [128, 512], "bfloat16"), "MK": ("sbuf", [128, 512], "bfloat16"), "OF32": ("sbuf", [128, 128], "float32"), "SL": ("sbuf", [128, 128], "float32"),
    "NH": ("sbuf", [128, 256], "bfloat16"), "RL": ("sbuf", [128, 256], "float32"),
    "K1": ("sbuf", [128, 256], "float32"), "K2": ("sbuf", [128, 256], "float32"), "K3": ("sbuf", [128, 256], "float32"), "K4": ("sbuf", [128, 256], "float32"),
    "CM": ("sbuf", [128, 128 * len(CM)], "bfloat16"), "FL": ("sbuf", [128, 16 * len(FL)], "float32"), "IL": ("sbuf", [128, 16 * len(IL)], "int32"),
    "QL": ("sbuf", [128, 64 * len(QL)], "float32"), "UF": ("sbuf", [128, 512], "float32"), "YM": ("sbuf", [128, 2048], "float32"),
    "KA": ("sbuf", [128, 256], "float32"), "KC": ("sbuf", [128, 256], "float32"), "NK": ("sbuf", [128, 256], "bfloat16"),
    "NM": ("sbuf", [128, 256], "bfloat16"), "CO": ("sbuf", [128, 1024], "bfloat16"), "D0": ("sbuf", [128, 256], "float32"),
    "OB": ("sbuf", [128, 64], "bfloat16"),
    "TN": ("sbuf", [128, 256], "int32"), "TR": ("sbuf", [128, 256], "float32"), "P1": ("sbuf", [128, 256], "float32"),
    "P2": ("sbuf", [128, 256], "float32"), "M1": ("sbuf", [128, 256], "float32"), "OM": ("sbuf", [128, 256], "uint16"),
    "DV": ("sbuf", [128, 256], "uint16"), "EA": ("sbuf", [128, 16, 256], "bfloat16"), "OD": ("sbuf", [128, 16], "uint16"), "BL": ("sbuf", [128, 16], "uint16"),
    "SC": ("sbuf", [128, 66], "bfloat16"), "HM": ("sbuf", [128, 64], "bfloat16"),
    "FB": ("sbuf", [128, 64], "bfloat16"), "F6": ("sbuf", [128, 32], "bfloat16"), "SY": ("sbuf", [128, 64], "int32"),
    "WB": ("sbuf", [128, 256 * len(WB)], "bfloat16"), "CV": ("sbuf", [128, 256], "float32"), "HUL": ("sbuf", [128, 256], "float32"),
    "RUL": ("sbuf", [128, 256], "float32"), "BUL": ("sbuf", [128, 256], "float32"), "MUL": ("sbuf", [128, 256], "float32"),
    "GQ": ("sbuf", [128, 256], "bfloat16"), "AB": ("sbuf", [128, 256], "bfloat16"),
    "BB": ("sbuf", [128, 256], "bfloat16"), "BD": ("sbuf", [128, 256], "bfloat16"), "CW": ("sbuf", [128, 128], "float32"),
    "AA": ("sbuf", [128, 1], "float32"), "YT": ("sbuf", [128, 4, 4, 16], "float32"), "YS": ("sbuf", [128, 32], "float32"),
    "GB": ("sbuf", [128, 4096], "bfloat16"), "HB": ("sbuf", [128, 4096], "bfloat16"), "LA": ("sbuf", [128, 2048], "bfloat16"), "LB": ("sbuf", [128, 2048], "bfloat16"),
    "MX": ("sbuf", [128, 256], "bfloat16"), "Z": ("sbuf", [128, 256], "bfloat16"), "GR": ("sbuf", [128, 1024], "bfloat16"), "H": ("sbuf", [128, 1024], "bfloat16"), "F": ("sbuf", [128, 512], "bfloat16"),
    "XI": ("sbuf", [128, 64], "int32"), "OF": ("sbuf", [128, 64], "uint16"),
    "pS0": ("psum", [128, 512], "float32"), "pT2": ("psum", [128, 1024], "bfloat16"), "pD0": ("psum", [128, 512], "float32"), "pD1": ("psum", [128, 512], "float32"),
    "pT0": ("psum", [128, 1024], "bfloat16"), "pT1": ("psum", [128, 1024], "bfloat16"), "pC": ("psum", [128, 512], "float32"), "pH": ("psum", [128, 512], "float32"),
}
for _t in range(TS):
    SCRATCH.update({"ZF%d" % _t: ("sbuf", [128, 256], "bfloat16"), "ZP%d" % _t: ("sbuf", [128, 256], "bfloat16"), "GO%d" % _t: ("sbuf", [128, 128], "bfloat16"),
                    "RG%d" % _t: ("sbuf", [128, 128], "bfloat16"), "DO%d" % _t: ("sbuf", [128, 16], "bfloat16"), "DR%d" % _t: ("sbuf", [128, 16], "bfloat16"),
                    "MS%d" % _t: ("sbuf", [128, 32], "uint16"), "MR%d" % _t: ("sbuf", [128, 32], "uint16")})
SEMAPHORES = ["cV", "cS", "cP", "cG", "dx", "dv", "ds", "dt", "dy", "loc", "rN0"] + ["r%s%d" % (k, t) for k in "MLKZD" for t in range(TS)]
CYC, WAKE, SFIX, LOOK, PUT, REMOTE = 0.00083, 0.25, 0.03, 1.56, 3.8, 3.5
OWN, VFIX, PCYC, PFIX = 0.24, 0.002, 0.00045, 0.003
ROUNDS, SLIP, MOVES, STIR = 4, 0.0, 300, 100
POOL, URGE, MIXES = 30, 8.0, 700
HS, QS = 1, 1
ORDER = []
RUN = ((("S", 18), ("S", 18), ("V", 28)),)
NS = len(RUN)
CW = 64 // NS
CLAIM = (("S", 2), ("V", 2), ("V", 2), ("S", 2)) + (("S", 4),) * 5 + (("S", 2), ("S", 2))
HITS_V = (5, 11)
LAST_V = (1, 3, 5, 7, 9, 11, 13, 15)
GAP = {"S": 0.3, "V": 0.9}
AHEAD = 0.0
PAD = {}
EARLY = 5.0
BANK = 0.0
YLAT = 55.0
FIRST = 3.0
IOS = 12
NT = 3
QV, QS2 = 1000, 4500
XS = 2
LA_S, LB_S = (), ()
MX = True


def rank_program(g, core, T, topo):
    rank = T.rank_of(core)
    if rank is None:
        return
    eng = {"V": g.vector, "S": g.scalar, "P": g.tensor, "G": g, "Y": g.sync}
    ops = []
    boost = [0.0]
    chain = [None]

    def op(q, reads, writes, cost, f, kind="c", sem=None, n=0, lat=0.0):
        if q == "V" and any(k[0] == "p" for k in reads.split()):
            cost += BANK
        ops.append({"chain": chain[0], "first": boost[0], "q": q, "r": reads.split(), "w": writes.split(), "cost": cost, "f": f, "kind": kind, "sem": sem, "n": n, "lat": lat + PAD.get(writes, 0.0)})

    def dma(q, sem, total, out, in_, reads, writes):
        op(q, reads, writes, 0.1, lambda e: e.dma_start(out, in_).then_inc(T.sem[sem], 16), "d", sem, total, 7.0 if sem == "dx" else 2.5)

    def part(k, a, b, step=1):
        for group, buf, w in ((FL, "FL", 16), (IL, "IL", 16), (QL, "QL", 64), (CM, "CM", 128), (WB, "WB", 256)):
            if k in group:
                o = w * group.index(k)
                return T[buf][:, o + a:o + b:step]
        return T[k][:, a:b:step]

    def lst(k):
        return part(k, 0, 16)

    def quad(k, h=None):
        return part(k, 0, 64) if h is None else part(k, CW * h, CW * h + CW)

    def wide(k):
        return part(k, 0, 256)

    def mat(k):
        return part(k, 0, 128)

    def vc(n):
        return VFIX + max(n, 64) * CYC

    def ts(reads, writes, n, out, in0, s1, o1, s2=None, o2=None):
        if o2 is None:
            op("V", reads, writes, vc(n), lambda e: e.tensor_scalar(out, in0, s1, None, o1))
        else:
            op("V", reads, writes, vc(n), lambda e: e.tensor_scalar(out, in0, s1, s2, o1, o2))

    def tt(reads, writes, n, out, in0, in1, o):
        op("V", reads, writes, vc(n), lambda e: e.tensor_tensor(out, in0, in1, o))

    def cp(reads, writes, n, out, in_):
        op("V", reads, writes, vc(n), lambda e: e.tensor_copy(out, in_))

    def act(reads, writes, n, out, in_, fn, bias=0.0, scale=1.0):
        op("S", reads, writes, SFIX + max(n, 64) * CYC, lambda e: e.activation(out, in_, fn, bias=bias, scale=scale))

    def look(q, reads, writes, n, out, src):
        if q == "V":
            op("V", reads, writes, 0.05 + LOOK * n * CYC, lambda e: e.tensor_copy(out, src))
        else:
            op("S", reads, writes, 0.065 + LOOK * n * CYC, lambda e: e.activation(out, src, AF.Copy))

    def mm(reads, writes, n, out, lhsT, rhs, a, z):
        op("P", reads, writes, PFIX + max(n, 64) * PCYC, lambda e: e.matmul(out, lhsT, rhs, a, z))
        ops[-1]["ends"] = (a, z)

    def scan(reads, writes, n, out, d0, d1, init, o0, o1):
        op("V", reads, writes, vc(n), lambda e: e.tensor_tensor_scan(out, d0, d1, init, o0, o1))

    def fill(key, n, ap, c):
        op("V", "", key, vc(n), lambda e: e.memset(ap, c))

    def iota(key, n, out, pat, base, cm):
        op("G", "", key, 0.13 + 2 * n * CYC, lambda e: e.iota(out, pat, base, cm, allow_small_or_imprecise_dtypes=True))

    def looks(n):
        return LOOK * n + 36

    def puts(n):
        return PUT * n + 36
    sent = [0]

    def send(t, kind, dst, src, keys):
        to = T.cores[rank ^ (1 + t % (len(T.cores) - 1))]
        rid, pid = topo.addr(to)[:2]
        m = topo.mask(core, to)
        n = bin(m).count("1")
        sem = "r%s%d" % (kind, t)
        sent[0] += n
        op("G", keys, "recv%s%d" % (kind, t), 0.3, lambda e: e.remote_dma(dst, src, T.sem[sem], T.sem.loc, pid, rid, m), "r", sem, n, REMOTE)

    XK = "Xa Xb"
    dma("Y", "dx", 32, T.X[0:64, 0:W], T.x[0:64, :], "", "Xa")
    dma("Y", "dx", 32, T.X[64:128, 0:W], T.x[64:128, :], "", "Xb")
    dma("S", "dv", 16, T.V0[:], T.v0[:], "", "V0")
    dma("S", "ds", 16, T.SD[:], T.sd[:], "", "SD")
    dma("S", "dt", 16, T.TI[:], T.th[:], "", "TI")

    iota("PI0", 1, T.PI[:, 0:1], [[0, 1]], 0, 1)
    iota("RM", 256, T.RM[:], [[0, 16], [1, 16]], 0, 0)
    iota("RP", 128, T.RP[:], [[1, 128]], 0, 0)
    iota("RG", 128, T.RG[:], [[1, 8], [0, 16]], 0, 0)
    iota("RD", 256, T.RD[:], [[1, 16], [0, 16]], 0, 0)
    iota("DMI", 16, lst("DM"), [[16, 16]], W, 0)
    iota("J0", 128, T.J0[:], [[16, 8], [1000, 4], [4, 4]], 0, 0)
    iota("J1", 128, T.J1[:], [[16, 8], [1, 4], [0, 4]], 0, 0)
    iota("J2", 128, T.J2[:], [[1, 8], [1000, 4], [0, 4]], 0, 0)
    iota("J3", 128, T.J3[:], [[0, 8], [1, 4], [0, 4]], 0, 0)
    fill("J4", 256, T.J4[:], 1.0)
    op("G", "J4", "MK", 0.17 + 1024 * CYC, lambda e: e.affine_select(T.MK[:], T.J4[:], [[0, 128], [1, 4]], Op.not_equal, 0.0, 0, 0))
    iota("RL", 256, T.RL[:], [[1, 256]], W - D, 0)
    iota("KI", 4, T.KP[:, 0:4], [[1, 4]], 0, 0)
    ts("PI0", "PI1", 1, T.PI[:, 1:2], T.PI[:, 0:1], 15, Op.bitwise_and)
    ts("PI0", "PI2", 1, T.PI[:, 2:3], T.PI[:, 0:1], 4, Op.arith_shift_right)
    ts("PI0", "PI3", 1, T.PI[:, 3:4], T.PI[:, 0:1], 2, Op.arith_shift_right, 3, Op.bitwise_and)
    ts("PI0", "PI4", 1, T.PI[:, 4:5], T.PI[:, 0:1], 3, Op.bitwise_and)
    cp("PI0 PI1 PI2 PI3 PI4", "PF", 5, T.PF[:, 0:5], T.PI[:, 0:5])
    p, pi, pg, pr, pm = [T.PF[:, j:j + 1] for j in range(5)]
    for m in range(4):
        fill("KV%d" % m, 1, T.KP[:, 4 + m:5 + m], 2.0 * KAPPA[m])
    ts("KI PF", "KE", 4, T.KP[:, 8:12], T.KP[:, 0:4], pm, Op.is_equal)
    tt("KE KV0 KV1 KV2 KV3", "KF", 8, T.KP[:, 8:12], T.KP[:, 8:12], T.KP[:, 4:8], Op.mult)
    op("V", "KF", "K2K", vc(4), lambda e: e.tensor_reduce(T.KP[:, 12:13], T.KP[:, 8:12], AxisListType.X, Op.add))
    ts("K2K", "KSQ", 1, T.KP[:, 13:14], T.KP[:, 12:13], T.KP[:, 12:13], Op.mult, -1.0, Op.mult)
    ts("KSQ", "KOF", 1, T.KP[:, 14:15], T.KP[:, 13:14], -0.25, Op.add)
    k2k, kof = T.KP[:, 12:13], T.KP[:, 14:15]
    ts("RM PF", "NM", 256, T.NM[:], T.RM[:], pi, Op.not_equal, -float(2 ** 24), Op.mult)
    ts("RG PF", "BO", 128, mat("BO"), T.RG[:], pg, Op.is_equal)
    ts("RM", "K4", 256, T.K4[:], T.RM[:], 0.0, Op.is_equal, -65536.0, Op.mult)
    ts("K4", "D0", 256, T.D0[:], T.K4[:], 32768.0, Op.add)
    ts("RP PF", "ID", 128, mat("ID"), T.RP[:], p, Op.is_equal)
    ts("ID", "NI", 64, mat("NI"), mat("ID"), -1.0, Op.mult)
    ts("RM PF", "K1", 256, T.K1[:], T.RM[:], pi, Op.is_equal)
    ts("RM PF", "K2", 128, T.K2[:, 0:128], T.RM[:, 0:128], pi, Op.is_gt)
    tt("K2 BO", "TG", 256, mat("TG"), T.K2[:, 0:128], mat("BO"), Op.mult)
    fill("OF32", 128, T.OF32[:], 1.0)
    for k in range(4):
        fill("WH", 1, T.RE[64 * (k % 2):64 * (k % 2) + 64, 4 + k // 2:5 + k // 2], 2.0 ** (11 * (3 - k)))
    ts("KI PF", "RE", 4, T.RE[:, 0:4], T.KP[:, 0:4], 4.0, Op.mult, pi, Op.is_equal)
    for r in range(4):
        ts("BO RE", "RF%d" % r, 128, T.RF[:, 128 * r:128 * r + 128], mat("BO"), T.RE[:, r:r + 1], Op.mult)
        ts("BO RE", "W%d" % r, 64, mat("W%d" % r), mat("BO"), T.RE[:, r:r + 1], Op.mult)
        ts("J2 PF", "B%d" % r, 128, mat("B%d" % r), T.J2[:], pg, Op.subtract, 1000.0 * r, Op.is_equal)
        ts("B%d" % r, "A%d" % r, 64, mat("A%d" % r), mat("B%d" % r), -0.5, Op.mult)
        ts("J0 PF", "C%d" % r, 128, mat("C%d" % r), T.J0[:], p, Op.subtract, 1000.0 * r, Op.is_equal)
        ts("J1 PF", "UF%d" % r, 128, T.UF[:, 128 * r:128 * r + 128], T.J1[:], p, Op.subtract, -4.0 * r, Op.is_equal)
        ts("UF%d" % r, "U%d" % r, 128, mat("U%d" % r), T.UF[:, 128 * r:128 * r + 128], float(D), Op.mult)
        for m in range(4):
            op("G", "OF32", "YM%d%d" % (m, r), 0.17 + 256 * CYC, lambda e, m=m, r=r: e.affine_select(
                T.YM[:, 512 * m + 128 * r:512 * m + 128 * r + 128], T.OF32[:], [[16, 8], [1000, 4], [4, 4]], Op.is_equal, 0.0, m - 1000 * r, -1), lat=YLAT)
    ts("J3 PF", "J3", 128, T.J3[:], T.J3[:], pr, Op.is_gt, 8192.0, Op.mult)
    tt("J3 BO", "J3", 256, T.J3[:], T.J3[:], mat("BO"), Op.mult)
    ts("ID", "O4", 64, mat("O4"), mat("ID"), -32768.0 * CAP, Op.mult)
    tt("J3 O4", "T4", 256, mat("T4"), T.J3[:], mat("O4"), Op.add)
    ts("BO", "O4", 64, mat("O4"), mat("BO"), 8192.0, Op.mult)
    tt("NM RL", "NH", 512, T.NH[:], T.NM[:], T.RL[:], Op.add)
    ts("BO", "BE", 64, mat("BE"), mat("BO"), float(D), Op.mult)
    ts("K1", "SL", 128, T.SL[:], T.K1[:, 0:128], -2.0 ** -46, Op.mult, 2.0 ** -46, Op.add)
    ts("SL", "SL", 128, T.SL[:], T.SL[:], 2.0 ** -92, Op.max)
    ts("BO", "BK", 64, mat("BK"), mat("BO"), 32768.0, Op.mult)
    ts("ID", "KA", 128, T.KA[:, 0:128], mat("ID"), -16384.0, Op.mult)
    ts("TG", "KB", 128, T.KA[:, 128:256], mat("TG"), 32768.0, Op.mult)
    tt("KA KB", "TK", 256, mat("TK"), T.KA[:, 0:128], T.KA[:, 128:256], Op.add)
    ts("RM PF", "KC", 256, T.KC[:], T.RM[:], pi, Op.not_equal, -float(2 ** 24 + 2 ** 14), Op.mult)
    ts("KC", "NK", 256, T.NK[:], T.KC[:], 16384.0, Op.add)
    ts("DMI PF", "DM", 16, lst("DM"), lst("DM"), pi, Op.add)
    fill("P10", 64, T.P1[:, 0:64], 0.5)
    fill("P11", 64, T.P1[:, 64:128], 0.5)
    fill("P12 P13", 128, T.P1[:, 128:256], 0.0)
    scan("P10 P11 P12 P13", "HUL", 128, T.HUL[:, 0:128], T.P1[:, 0:128], T.P1[:, 128:256], 2.0 ** 63, Op.mult, Op.add)
    for h in range(2):
        ts("HUL", "UW", 128, part("UW", 128 * h, 128 * h + 128), T.HUL[:, 0:128], 2.5, Op.mult)
    tt("HUL ID", "CV", 256, T.CV[:, 0:128], T.HUL[:, 0:128], mat("ID"), Op.mult)
    op("V", "CV", "UP", vc(128), lambda e: e.tensor_reduce(T.KP[:, 15:16], T.CV[:, 0:128], AxisListType.X, Op.add))
    fill("OB", 32, T.OB[:], 1.0)
    for t in range(TS):
        fill("OW%d" % t, 128, T.OW[:, 256 * t:256 * t + 256], 32.0 ** (t + 1 - TS))
    fill("ON", 64, mat("ON"), 1.0)
    fill("SC0", 1, T.SC[:, 0:1], 0.0)
    fill("THR", 64, quad("THR"), 9.0)
    fill("FB", 32, T.FB[:], 16384.0)
    fill("FR", 16, T.F6[:, 0:16], 0.0)
    for k in range(4):
        fill("TC", 32, part("TC", 64 * k, 64 * k + 64), 0.75 * 2.0 ** (11 * (3 - k) - 46))
    fill("AA", 1, T.AA[:], 0.0)
    cp("TI", "TF", 4, T.TF[:, 0:4], T.TI[:])
    ts("TI", "TG4", 4, T.TF[:, 4:8], T.TI[:], 1.0, Op.max, -1.0, Op.mult)
    ts("RD PF", "K2", 256, T.K2[:], T.RD[:], pi, Op.is_equal, 2.0, Op.mult)
    tt("K1 K2", "K3", 512, T.K3[:], T.K1[:], T.K2[:], Op.mult)
    ts("K3", "K3", 256, T.K3[:], T.K3[:], 4194304.0, Op.mult)
    tt("K1 K3", "K3", 512, T.K3[:], T.K3[:], T.K1[:], Op.add)
    tt("K2 K3", "K3", 512, T.K3[:], T.K3[:], T.K2[:], Op.add)
    size = [2.0 ** (24 * t - 24) for t in range(TS)]
    for t in range(TS):
        ts("K3", "CO%d" % t, 256, T.CO[:, 256 * t:256 * t + 256], T.K3[:], size[t], Op.mult)
    for j in range(0, 8464, 529):
        if j < QV:
            fill("Q" + str(j), 265, T.Q[:, j:j + 529], 0.0)
        elif j < QS2:
            act("Q0", "Q" + str(j), 529, T.Q[:, j:j + 529], T.Q[:, 0:529], AF.Copy)
        else:
            iota("Q" + str(j), 529, T.Q[:, j:j + 529], [[0, 529]], 0, 0)
        iota("HT" + str(j), 529, T.HT[:, j:j + 529], [[0, 529]], 0, 0)
    tabs = {buf: " ".join(buf + str(j) for j in range(0, 8464, 529)) for buf in ("Q", "HT")}

    def hs(h):
        return slice(4 * CW * h, 4 * CW * h + 4 * CW)

    def both(k):
        return " ".join(k + str(h) for h in range(NS))

    def sums(m, src, key, h, first, final):
        bank, a, n = ("pS0", 0, 64) if h is None else (("pS0", "pD0")[h], CW * h, CW)
        for r in range(4):
            mm("%s%d %s" % (m, r, key), bank, n, T[bank][:, 0:n], mat("%s%d" % (m, r)), src(slice(4 * a + r, 4 * a + 4 * n, 4)), first and r == 0, final and r == 3)

    def pick(bank, a, lhs, key, src, out, under):
        for k in under:
            mm("ID " + k, bank, 256, T[bank][:, a:a + 256], mat("ID"), T[k][:], k == under[0], False)
        mm(lhs + " " + key, bank, 256, T[bank][:, a:a + 256], mat(lhs), src, False, True)
        scan("D0 " + bank, out, 256, T[out][:], T.D0[:], T[bank][:, a:a + 256], -8192.0, Op.min, Op.max)

    def step(t, b):
        for h in range(NS):
            Z, zk = (T.SD, "SD") if b == 0 else (T.Z, "Z%d" % h)
            bank, cols, a, w = ("pS0", "pD0")[h], slice(CW * h, CW * h + CW), 64 * b + CW * h, 4 * CW
            xi, tn, of = "XI%d" % h, "TN%d%d" % (b, h), "OF%d" % h
            if b:
                tt(bank + " VK", xi, CW, T.XI[:, cols], T[bank][:, 64:64 + CW], quad("VK", h), Op.add)
            if b < 3:
                sums("A", lambda l: Z[:, l], zk, h, True, False)
            if NS == 1:
                mm("ID " + zk, "pD0", 256, T.pD0[:, 0:256], mat("ID"), Z[:], True, True)
            ts(xi, tn, CW, T.TN[:, a:a + CW], T.XI[:, cols], W - 1, Op.bitwise_and)
            cp(tn, of, CW, T.OF[:, cols], T.TN[:, a:a + CW])
            c0, hk, mk = CW * h, "", ""
            for j, (q, n) in enumerate(RUN[h]):
                key, lanes, four = "%d.%d" % (h, j), slice(4 * c0, 4 * c0 + 4 * n), slice(16 * c0, 16 * c0 + 16 * n)
                look(q, XK + " " + of, "GR" + key, 16 * n, T.GR[:, four], T.X[:, 0:W].indirect(T.OF[:, c0:c0 + n]))
                scan("MK GR" + key, "H" + key, 8 * n, T.H[:, four], T.MK[:, 0:16 * n], T.GR[:, four], 0.0, Op.mult, Op.max)
                z, zz, cost = (T.pD0, "pD0", 4 * n) if NS == 1 else (Z, zk, 8 * n)
                tt("H%s %s" % (key, zz), "MX" + key, cost, T.MX[:, lanes], z[:, lanes], T.H[:, 16 * c0 + 3:16 * c0 + 16 * n:4], Op.max if b < 3 else Op.subtract)
                c0, hk, mk = c0 + n, hk + " H" + key, mk + " MX" + key
            if b < 3:
                sums("A", lambda l: T.H[:, 4 * l.start + 3:4 * l.stop:16], hk, h, False, False)
                sums("B", lambda l: T.MX[:, l], mk, h, False, True)
                act("K2K", bank, CW, T[bank][:, 64:64 + CW], T[bank][:, 0:CW], AF.Square, bias=k2k, scale=0.5)
                mm("NI " + zk, "pD1", w, T.pD1[:, 0:w], mat("NI"), Z[:, hs(h)], True, False)
                mm("ID " + hk, "pD1", w, T.pD1[:, 0:w], mat("ID"), T.H[:, 4 * w * h + 3:4 * w * h + 4 * w:4], False, True)
                act("pD1", "Z%d" % h, w, T.Z[:, hs(h)], T.pD1[:, 0:w], AF.Abs)
            else:
                ts(mk + " TF", "FA%d" % h, w // 2, T.F[:, hs(h)], T.MX[:, hs(h)], T.TF[:, t:t + 1], Op.is_ge)
                ts(mk + " TG4", "FB%d" % h, w // 2, T.F[:, 256 + w * h:256 + w * h + w], T.MX[:, hs(h)], T.TF[:, 4 + t:5 + t], Op.is_le)
                act(mk, "ZF%d.%d" % (t, h), w, T["ZF%d" % t][:, hs(h)], T.MX[:, hs(h)], AF.Abs)

    def trails(t, b):
        cols, tn = slice(64 * b, 64 * b + 64), both("TN%d" % b)
        if t == 0:
            cp(tn, "TR%d" % b, 64, T.TR[:, cols], T.TN[:, cols])
        else:
            tt("TR%d pH" % b, "P1%d" % b, 64, T.P1[:, cols], T.pH[:, 320:384], T.TR[:, cols], Op.max)
            tt(tn + " pH", "P2%d" % b, 64, T.P2[:, cols], T.pH[:, 256:320], T.TN[:, cols], Op.max)
            tt("P1%d P2%d" % (b, b), "TR%d" % b, 128, T.TR[:, cols], T.P2[:, cols], T.P1[:, cols], Op.min)

    def halts(t):
        sums("B", lambda l: T.F[:, l], both("FA"), None, True, False)
        sums("B", lambda l: T.F[:, 256 + l.start:512:4], both("FB"), None, False, True)
        ha, HA = "HA%d" % t, T["GO%d" % t][:, 0:64]
        tt("pS0 THR", ha, 64, HA, T.pS0[:, 0:64], quad("THR"), Op.is_ge)
        send(t, "L", T["RG%d" % t][:, 0:64], HA, ha)
        ts(ha, "HM", 32, T.HM[:], HA, -1.0, Op.add, 2.0 ** 31, Op.mult)
        mm("ID FB", "pC", 64, T.pC[:, 0:64], mat("ID"), T.FB[:], True, False)
        mm("T4 " + ha, "pC", 64, T.pC[:, 0:64], mat("T4"), HA, False, False)
        scan("OB " + ha, "SC1", 32, T.SC[:, 1:65], T.OB[:], HA, 0.0, Op.mult, Op.add)
        mm("O4 SC0 SC1", "pC", 64, T.pC[:, 0:64], mat("O4"), T.SC[:, 0:64], False, True)
        for b in range(4):
            cols = slice(64 * b, 64 * b + 64)
            tt("TR%d pC" % b, "M1%d" % b, 64, T.M1[:, cols], T.pC[:, 0:64], T.TR[:, cols], Op.max)
            ts("M1%d" % b, "OM%d" % b, 64, T.OM[:, cols], T.M1[:, cols], float(D), Op.min)
        tt("pC HM", "GO%d" % t, 64, T["GO%d" % t][:, 64:128], T.pC[:, 0:64], T.HM[:], Op.is_lt)
        send(t, "K", T["RG%d" % t][:, 64:128], T["GO%d" % t][:, 64:128], "GO%d" % t)

    def firsts(t):
        rg, rk = T["RG%d" % t], "recvL%d" % t
        for r in range(4):
            mm("W%d %s" % (r, rk), "pH", 64, T.pH[:, r:256:4], mat("W%d" % r), rg[:, 0:64], True, True)
        tt("pH LU", "EX", 256, wide("EX"), T.pH[:, 0:256], wide("LU"), Op.mult)
        for h in range(2):
            mm("EX ID", "pH", 128, T.pH[:, 256 + 128 * h:384 + 128 * h], part("EX", 128 * h, 128 * h + 128), mat("ID"), True, True)
        ts("pH UP", "LW", 256, wide("LW"), T.pH[:, 256:512], T.KP[:, 15:16], Op.mult)
        ts("pH", "LV", 128, part("LV", 0, 128), T.pH[:, 256:384], 2.0 ** 64, Op.mult)
        mm("LW L2", "pH", 128, T.pH[:, 0:128], part("LW", 0, 128), part("L2", 0, 128), True, True)
        mm("LW L2", "pH", 128, T.pH[:, 128:256], part("LW", 128, 256), part("L2", 128, 256), True, False)
        mm("LV L2", "pH", 128, T.pH[:, 128:256], part("LV", 0, 128), part("L2", 0, 128), False, True)
        act("pH", "CV", 256, T.CV[:], T.pH[:, 0:256], AF.Copy)
        for h in range(2):
            a = 128 * h
            tt("CV BL TH", "D2%d" % h, looks(128), part("D2", a, a + 128), T.CV[:, a:a + 128].indirect(T.BL[:, 8 * h:8 * h + 8]), part("T2", a, a + 128), Op.is_ge)
        for q in range(4):
            mm("C%d recvK%d" % (q, t), "pS0", 16, T.pS0[:, 64:80], mat("C%d" % q), rg[:, 64 + q:128:4], q == 0, q == 3)
        act("pS0", "IW", 16, lst("IW"), T.pS0[:, 64:80], AF.Identity, bias=-65536.0, scale=65536.0)
        tt("pS0 VD", "L1", 16, lst("L1"), T.pS0[:, 64:80], lst("VD"), Op.mult)
        tt("L1 DM", "LF", 32, lst("LF"), lst("L1"), lst("DM"), Op.add)

    def shadows(bank, out):
        dv, bm, eb = "DV", "BM", "EA"
        mm("ID NK", bank, 256, T[bank][:, 256:512], mat("ID"), T.NK[:], True, False)
        for c in range(16):
            e, n = T[eb][:, c, 0:L - 16 * c], (L - 16 * c) // 2
            ts(dv + " " + bm, eb + str(c), n, e, T[dv][:, 16 * c:L], part(bm, c, c + 1), Op.is_equal)
            if c < 15:
                mm("BK %s%d" % (eb, c), bank, L - 16 - 16 * c, T[bank][:, 272 + 16 * c:512], mat("BK"), T[eb][:, c, 16:L - 16 * c], False, False)
        mm("TK " + " ".join(eb + str(c) for c in range(16)), bank, 256, T[bank][:, 256:512], mat("TK"), T[eb][:, :, 0:16], False, True)
        scan("D0 " + bank, out, 256, T[out][:], T.D0[:], T[bank][:, 256:512], -8192.0, Op.min, Op.max)

    def listed(sums_, v, a, b, out, key):
        tt(sums_ + " " + v, a, 32, lst(a), T[sums_][:, 15::16], lst(v), Op.max)
        tt(a + " DM", b, 32, lst(b), lst(a), lst("DM"), Op.min)
        cp(b, key, 16, out, lst(b))

    def advance(more):
        ts("S8 AA", "S7", 16, lst("S7"), lst("S8"), T.AA[:], Op.add)
        ts("S7", "VN", 16, lst("VN"), lst("S7"), W - 1, Op.bitwise_and)
        if more:
            ts("SB AA", both("XI"), 64, T.XI[:], quad("SB"), T.AA[:], Op.add)
            act("BK4 AA", "VK", 64, quad("VK"), quad("BK4"), AF.Identity, bias=T.AA[:])

    def announce(t):
        ms = "MS%d" % t
        cp("VN", ms + "v", 16, T[ms][:, 16:32], lst("VN"))
        cp("VN", "VF", 16, lst("VF"), lst("VN"))
        listed("RUL", "VF", "R1", "R2", T[ms][:, 0:16], ms + "r")
        if t:
            send(t, "M", T["MR%d" % t][:], T[ms][:], ms + "v " + ms + "r")
        else:
            send(t, "N", T.MR0[:, 16:32], T.MS0[:, 16:32], ms + "v MK RD")
            ops[-1]["lat"] += EARLY
            ops[-1]["cost"] = 1.0
            send(t, "M", T.MR0[:, 0:16], T.MS0[:, 0:16], ms + "r")

    def prepare(t):
        mr, rk, s = T["MR%d" % t], "recvM%d" % t + " recvN0" * (t == 0), size[t]
        for j in range(QS):
            n = 16 // QS
            cp("%s CO%d %s" % (rk, t, tabs["Q"]), tabs["Q"], puts(16 * n), T.Q[:, 0:8448].indirect(mr[:, n * j:n * j + n]), T.CO[:, 256 * t + 16 * n * j:256 * t + 16 * n * (j + 1)])
        look("S", rk + " " + tabs["Q"], "GQ", 256, T.GQ[:], T.Q[:].indirect(mr[:, 16:32]))
        ts("GQ PF", "BB", 128, T.BB[:], T.GQ[:], 1.5 * s, Op.is_ge, p, Op.mult)
        pick("pC", 0, "BO", "BB", T.BB[:], "BUL", ["NM"])
        cp("BUL", "BL", 16, T.BL[:], T.BUL[:, 15::16])
        act("GQ", "AB", 256, T.AB[:], T.GQ[:], AF.Abs, bias=-s)
        ts("AB", "T1", 128, wide("T1"), T.AB[:], s, Op.is_equal, 2.0 ** 80, Op.mult)
        for j, k in enumerate(("TC", "UW")):
            mm("ID T1", "pD1", 256, T.pD1[:, 256 * j:256 * j + 256], mat("ID"), wide("T1"), True, False)
            mm("ID " + k, "pD1", 256, T.pD1[:, 256 * j:256 * j + 256], mat("ID"), wide(k), False, True)
        act("pD1", "TH", 512, part("TH", 0, 512), T.pD1[:], AF.Copy)
        for j in range(2):
            op("P", "ID GQ", "pT0", PFIX + 128 * PCYC, lambda e, j=j: e.transpose(T.pT0[:, 128 * j:128 * j + 128], T.GQ[:, 128 * j:128 * j + 128], mat("ID")))
        ts("AB", "LU", 128, wide("LU"), T.AB[:], s, Op.not_equal)
        ts("pT0", "L2", 128, wide("L2"), T.pT0[:, 0:256], 1.5 * s, Op.is_ge)
        cp(rk, "L3", 16, lst("L3"), mr[:, 16:32])
        tt("L3 DM", "VD", 32, lst("VD"), lst("L3"), lst("DM"), Op.subtract)

    def widen(t):
        bm, dv = "BM", "DV"
        ts("S8", "S9", 16, lst("S9"), lst("S8"), W - 1, Op.bitwise_and)
        cp("S9", bm, 16, lst(bm), lst("S9"))
        for q in range(4):
            mm("UF%d %s" % (q, bm), "pC", 256, T.pC[:, 128 + q:192:4], T.UF[:, 128 * q:128 * q + 128], lst(bm), True, True)
        act("pC KOF", "BK4", 64, quad("BK4"), T.pC[:, 128:192], AF.Identity, bias=kof)
        tt("pC SY", "SB", 64, quad("SB"), T.pC[:, 128:192], T.SY[:], Op.add)
        for r in range(4):
            mm("RF%d BK4" % r, "pC", 256, T.pC[:, 256 + r:512:4], T.RF[:, 128 * r:128 * r + 128], quad("BK4"), True, True)
        ts("pC", dv, 256, T[dv][:], T.pC[:, 256:512], 4.0 * KAPPA[0] ** 2 + 0.25, Op.add)

    def base():
        ts("VC", "S1", 16, lst("S1"), lst("VC"), 4095, Op.bitwise_and)
        tt("S1", "S2", 32, lst("S2"), lst("S1"), lst("S1"), Op.mult)
        ts("S2", "S3", 16, lst("S3"), lst("S2"), 3, Op.arith_shift_right)
        ts("VC", "S4", 16, lst("S4"), lst("VC"), 37.0, Op.mult)
        tt("S3 S4", "S8", 32, lst("S8"), lst("S4"), lst("S3"), Op.add)

    def hits(t, onv):
        mark = 32.0 ** (t + 1 - TS)
        for j in range(HS):
            n = 16 // HS
            cp("OD%d OD%d OW%d " % (n * j * XS // 16, (n * j + n - 1) * XS // 16, t) + tabs["HT"], tabs["HT"], puts(16 * n), T.HT[:].indirect(T.OD[:, n * j:n * j + n]), T.OW[:, 256 * t:256 * t + 16 * n])
        mm("ID NM", "pH", 256, T.pH[:, 0:256], mat("ID"), T.NM[:], True, False)
        for k in range(16):
            hb, b0, q = "HB%d" % k, 256 * k, "V" if k in onv else "S"
            chain[0] = q
            look(q, "%s OM%d" % (tabs["HT"], k // 4), hb, 256, T.HB[:, b0:b0 + 256], T.HT[:, 0:8464].indirect(T.OM[:, 16 * k:16 * k + 16]))
            chain[0] = None
            for m in range(4):
                mm("ID " + hb, "pH", 64, T.pH[:, 64 * (k % 4):64 * (k % 4) + 64], mat("ID"), T.HB[:, b0 + m:b0 + 256:4], False, k == 15 and m == 3)
        scan("D0 pH", "HUL", 256, T.HUL[:], T.D0[:], T.pH[:, 0:256], -8192.0, Op.min, Op.max)
        tt("FR recvD%d" % t, "FS", 32, lst("FS"), T["DR%d" % t][:], T.F6[:, 0:16], Op.add)
        if mark != 1.0:
            act("FS", "FS", 16, lst("FS"), lst("FS"), AF.Copy, scale=mark)
        fr, v = (T.YS[:, 16:32], T.YS[:, 0:16]) if t == TS - 1 else (T.F6[:, 0:16], lst("VC"))
        tt("VC VN", "S5", 32, lst("S5"), lst("VC"), lst("VN"), Op.subtract)
        tt("HUL FS", "FR", 32, fr, T.HUL[:, 15::16], lst("FS"), Op.is_lt)
        tt("S5 FR", "S6", 32, lst("S6"), lst("S5"), fr, Op.mult)
        tt("S6 VN", "VC", 32, v, lst("S6"), lst("VN"), Op.add)

    def keep():
        tt("HUL FS", "F7", 32, T.F6[:, 16:32], T.HUL[:, 15::16], lst("FS"), Op.is_ge)
        for q in range(4):
            mm("U%d FR F7" % q, "pH", 32, T.pH[:, 256 + q:384:4], mat("U%d" % q), T.F6[:], True, True)
        act("pH", "THR", 64, quad("THR"), T.pH[:, 256:320], AF.Identity, bias=9.0)
        act("pH", "FB", 64, T.FB[:], T.pH[:, 256:320], AF.Identity, bias=16384.0, scale=-131072.0)

    sums("B", lambda l: T.SD[:, l], "SD", None, True, True)
    act("pS0 K2K", "SQ", 64, quad("SQ"), T.pS0[:, 0:64], AF.Square, bias=k2k, scale=0.25)
    ts("SQ KOF", "SY", 64, T.SY[:], quad("SQ"), kof, Op.add)
    cp("V0", "VC", 16, lst("VC"), T.V0[:])
    cp("V0", "S8", 16, lst("S8"), T.V0[:])
    widen(0)
    shadows("pC", "RUL")
    advance(True)

    for t in range(TS):
        last = t == TS - 1
        zf = "ZF%d" % t
        announce(t)
        for b in range(4):
            step(t, b)
        base()
        for b in range(4):
            trails(t, b)
        prepare(t)
        halts(t)
        if not last:
            send(t, "Z", T["ZP%d" % t][:], T[zf][:], both(zf + "."))
        firsts(t)
        if last:
            for m in range(4):
                for q in range(4):
                    mm("YM%d%d TR0 TR1 TR2 TR3" % (m, q), "pC", 256, T.pC[:, 64 * m:64 * m + 64], T.YM[:, 512 * m + 128 * q:512 * m + 128 * q + 128], T.TR[:, q:256:4], q == 0, q == 3)
            for m in range(4):
                act("pC", "YT%d" % m, 64, T.YT[:, :, m, :], T.pC[:, 64 * m:64 * m + 64], AF.Copy)
            dma("Y", "dy", 32, T.yt[:], T.YT[:], "YT0 YT1 YT2 YT3", "yt")
            ops[-1]["lat"] = 4.0
        else:
            widen(t + 1)
            shadows("pC", "RUL")
        j0 = 0
        for k, (q, n) in enumerate(CLAIM):
            pt, a0 = "pT%d" % (k % NT), 128 * (j0 % 16)
            look(q, "%s OM%d" % (tabs["Q"], j0 // 8), "GB%d" % k, 128 * n, T.GB[:, 128 * j0:128 * (j0 + n)], T.Q[:].indirect(T.OM[:, 8 * j0:8 * (j0 + n)]))
            for j in range(n):
                src = T.GB[:, 128 * j0 + j:128 * (j0 + 4):4] if n == 4 else T.GB[:, 128 * (j0 + j):128 * (j0 + j + 1)]
                op("P", "ID GB%d" % k, pt, PFIX + 128 * PCYC, lambda e, j=j, src=src, pt=pt: e.transpose(T[pt][:, 128 * j:128 * j + 128], src, mat("ID")))
            la = " ".join("LA%d" % ((j0 + j) % 16) for j in range(n))
            if n == 4:
                h = j0 % 8 // 4
                ts(pt + " WH", la, 256, T.LA[:, a0:a0 + 512], T[pt][:, 0:512], T.RE[:, 4 + h:5 + h], Op.mult, size[t] ** -2, Op.mult)
            else:
                ts(pt, la, 64 * n, T.LA[:, a0:a0 + 128 * n], T[pt][:, 0:128 * n], 2.0 ** (11 * (3 - j0 % 8 // 2)) * size[t] ** -2, Op.mult)
            lb = " ".join("LB%d" % ((j0 + j) % 16) for j in range(n))
            if k in LB_S:
                act(pt, lb, 128 * n, T.LB[:, a0:a0 + 128 * n], T[pt][:, 0:128 * n], AF.Relu, bias=-size[t])
            else:
                ts(pt, lb, 64 * n, T.LB[:, a0:a0 + 128 * n], T[pt][:, 0:128 * n], -size[t], Op.add, 0.0, Op.max)
            for j in range(j0, j0 + n):
                a1 = 128 * (j % 16)
                mm("LA%d LB%d" % (j % 16, j % 16), "pD1", 128, T.pD1[:, 128:256], T.LA[:, a1:a1 + 128], T.LB[:, a1:a1 + 128], j == 0, j == 31)
            j0 += n
        do = "DO%d" % t
        tt("pD1 SL", "CW", 128, T.CW[:], T.pD1[:, 128:256], T.SL[:], Op.mult)
        n = 16 // XS
        for j in range(XS):
            c, l, bank, sum_ = slice(n * j, n * j + n), slice(16 * n * j, 16 * n * (j + 1)), ("pD0", "pH")[j], T.MUL[:, 16 * n * j + 15:16 * n * (j + 1):16]
            tt("CW BL TH", "BD%d" % j, looks(16 * n), T.BD[:, l], T.CW[:].indirect(T.BL[:, c]), part("TH", l.start, l.stop), Op.is_ge)
            mm("ID NH", bank, 16 * n, T[bank][:, l], mat("ID"), T.NH[:, l], True, False)
            mm("BE D20 D21", bank, 16 * n, T[bank][:, l], mat("BE"), part("D2", l.start, l.stop), False, False)
            mm("BE BD%d" % j, bank, 16 * n, T[bank][:, l], mat("BE"), T.BD[:, l], False, True)
            scan("D0 " + bank, "MUL%d" % j, 16 * n, T.MUL[:, l], T.D0[:, l], T[bank][:, l], -8192.0, Op.min, Op.max)
            tt("IW MUL%d" % j, "%s.%d" % (do, j), 32, T[do][:, c], sum_, part("IW", c.start, c.stop), Op.is_lt)
            mm("ON %s.%d" % (do, j), "pS0", 16, T.pS0[:, 0:n], mat("ON"), T[do][:, c], j == 0, j == XS - 1)
            tt("LF MUL%d" % j, "E1%d" % j, 32, part("E1", c.start, c.stop), sum_, part("LF", c.start, c.stop), Op.max)
            cp("E1%d" % j, "OD%d" % j, 16, T.OD[:, c], part("E1", c.start, c.stop))
            if not last:
                cp("OD%d recvZ%d" % (j, t), XK, puts(16 * n), T.X[:].indirect(T.OD[:, c]), T["ZP%d" % t][:, l])
        send(t, "D", T["DR%d" % t][:], T[do][:], " ".join("%s.%d" % (do, j) for j in range(XS)))
        op("V", "pS0", "AA", vc(16), lambda e, n=n: e.tensor_reduce(T.AA[:], T.pS0[:, 0:n], AxisListType.X, Op.add))
        advance(not last)
        hits(t, LAST_V if last else HITS_V)
        if not last:
            keep()
    dma("Y", "dy", 32, T.ys[:], T.YS[:], "FR VC", "ys")

    N = len(ops)
    preds = [dict() for _ in ops]
    last_w, readers, banks, group = {}, {}, {}, {}
    ends = {}
    for i, o in enumerate(ops):
        def after(j, wake):
            if j != i:
                if wake and ops[j]["q"] == o["q"] and ops[j]["kind"] == "c":
                    wake = OWN
                preds[i][j] = max(preds[i].get(j, 0.0), wake)
        if o["chain"]:
            if o["chain"] in ends:
                after(ends[o["chain"]], 0.0)
            ends[o["chain"]] = i
        for k in o["r"] + o["w"]:
            if k[0] == "p":
                before, now = banks.get(k, ([], []))
                if now and ops[now[-1]]["q"] != o["q"]:
                    before, now = now, []
                for j in before:
                    after(j, WAKE)
                if o["q"] == "P":
                    first, final = o.get("ends", (True, True))
                    for j in (group.get(k, []) if first or final else group[k][:1]):
                        after(j, 0.0)
                    group[k] = [i] if first else group[k] + [i]
                banks[k] = (before, now + [i])
        for k in o["r"]:
            if k[0] != "p" and k in last_w:
                after(last_w[k], WAKE)
        for k in o["w"]:
            if k[0] != "p":
                if k in last_w:
                    after(last_w[k], WAKE)
                for j in readers.get(k, []):
                    after(j, WAKE)
        for k in o["r"]:
            if k[0] != "p":
                readers.setdefault(k, []).append(i)
        for k in o["w"]:
            if k[0] != "p":
                last_w[k] = i
                readers[k] = []
    succs = [[] for _ in ops]
    for i in range(N):
        for j, wake in preds[i].items():
            succs[j].append((i, wake))
    prio = [0.0] * N
    for i in range(N - 1, -1, -1):
        best = 0.0
        for j, wake in succs[i]:
            gap = GAP[ops[i]["chain"]] if ops[i]["chain"] and ops[i]["chain"] == ops[j]["chain"] else 0.0
            best = max(best, wake + ops[i]["lat"] + gap + prio[j])
        prio[i] = best + ops[i]["cost"] + ops[i]["first"]

    costs, queues = [o["cost"] for o in ops], [o["q"] for o in ops]

    def place(turn, behind):
        end = [0.0] * N
        taken = {q: ([], []) for q in eng}
        for i in turn:
            t0 = 0.0
            for j, gap in behind[i]:
                if end[j] + gap > t0:
                    t0 = end[j] + gap
            cost = costs[i]
            a, z = taken[queues[i]]
            lo = n = len(z)
            while lo and z[lo - 1] > t0:
                lo -= 1
            while lo < n and a[lo] < t0 + cost:
                t0 = z[lo]
                lo += 1
            a.insert(lo, t0)
            z.insert(lo, t0 + cost)
            end[i] = t0 + cost
        return end

    if not ORDER:
        ahead = [[(j, wake + ops[j]["lat"]) for j, wake in preds[i].items()] for i in range(N)]
        back = [[(j, wake + ops[i]["lat"]) for j, wake in succs[i]] for i in range(N)]
        turn, best = sorted(range(N), key=lambda i: (-prio[i], i)), None

        def span(end):
            return max(end[i] + ops[i]["lat"] for i in range(N))

        def started(end):
            return sorted(range(N), key=lambda i: (end[i] - ops[i]["cost"], i))
        def polish(turn, rounds):
            best = None
            for n in range(rounds):
                end = place(turn, ahead)
                if best is None or span(end) < best[0]:
                    best = (span(end), end)
                if n < rounds - 1:
                    end = place(sorted(range(N), key=lambda i: (-end[i], -i)), back)
                    turn = sorted(range(N), key=lambda i: (-end[i], i))
            return best
        seed, pool = 1, [polish(turn, ROUNDS)]
        for _ in range(POOL):
            key = list(prio)
            for i in range(N - 1, -1, -1):
                seed = (seed * 1103515245 + 12345) % 2147483648
                key[i] = max([key[i] + URGE * (seed >> 12 & 255) / 255 * (seed >> 8 & 7 == 0)] + [key[j] + 1e-4 for j, _g in back[i]])
            pool.append(polish(sorted(range(N), key=lambda i: (-key[i], i)), ROUNDS))
        for _ in range(MIXES):
            seed = (seed * 1103515245 + 12345) % 2147483648
            pool.sort(key=lambda x: x[0])
            one, other = pool[(seed >> 8) % len(pool)], pool[(seed >> 16) % len(pool)]
            seed = (seed * 1103515245 + 12345) % 2147483648
            cut = one[0] * (seed >> 8 & 1023) / 1024
            head = [i for i in started(one[1]) if one[1][i] - ops[i]["cost"] < cut]
            seen = set(head)
            child = polish(head + [i for i in started(other[1]) if i not in seen], 1 + (seed >> 20 & 1))
            if child[0] < pool[-1][0] and all(abs(child[0] - x[0]) > 1e-6 for x in pool):
                pool[-1] = child
        best = min(pool, key=lambda x: x[0])
        for _ in range(MOVES):
            end = best[1]
            turn = started(end)
            before, last = {}, {}
            for i in turn:
                before[i], last[ops[i]["q"]] = last.get(ops[i]["q"]), i
            i, held = max(range(N), key=lambda i: end[i] + ops[i]["lat"]), []
            while i is not None:
                ready, j = max([(end[j] + gap, j) for j, gap in ahead[i]] + [(0.0, None)])
                if end[i] - ops[i]["cost"] > ready + 1e-6:
                    held.append((i, ready))
                    j = before[i]
                i = j
            if not held:
                break
            seed = (seed * 1103515245 + 12345) % 2147483648
            i, ready = held[(seed >> 8) % len(held)]
            key = {k: float(n) for n, k in enumerate(turn)}
            j = before[i]
            if seed >> 5 & 1:
                n = int(key[i])
                for k in turn[max(0, n - 20 - (seed >> 10 & 127)):n + 10]:
                    seed = (seed * 1103515245 + 12345) % 2147483648
                    key[k] += STIR * ((seed >> 8 & 255) / 255 - 0.5) * (seed >> 16 & 3 == 0)
                for k in range(N):
                    key[k] = max([key[k]] + [key[m] + 1e-4 for m, _g in ahead[k]])
            elif seed >> 6 & 1:
                key[j], todo = key[i] + 0.5, [j]
                while todo:
                    k = todo.pop()
                    for m, _g in back[k]:
                        if key[m] <= key[k]:
                            key[m] = key[k] + 1e-4
                            todo.append(m)
            else:
                while seed >> 7 & 1 and before[j] is not None and end[before[j]] > ready:
                    j = before[j]
                key[i], todo = key[j] - 0.5, [i]
                while todo:
                    k = todo.pop()
                    for m, _g in ahead[k]:
                        if key[m] >= key[k]:
                            key[m] = key[k] - 1e-4
                            todo.append(m)
            end = place(sorted(range(N), key=lambda k: (key[k], k)), ahead)
            if span(end) <= best[0]:
                best = (span(end), end)
        ORDER.extend(started(best[1]))
    order = ORDER

    count = {q: 0 for q in eng}
    clock = {q: {} for q in eng}
    wr, rd, bank = {}, {}, {}

    def need(q, tok):
        s, n, known = tok
        if clock[q].get(s, 0) < n:
            eng[q].wait_ge(T.sem[s], n)
            clock[q][s] = n
            for k, m in known.items():
                clock[q][k] = max(clock[q].get(k, 0), m)

    for i in order:
        o = ops[i]
        q, keys = o["q"], o["r"] + o["w"]
        toks = []
        for k in keys:
            if k[0] == "p":
                toks += [tok for q2, tok in bank.get(k, {}).items() if q2 != q]
            elif k in wr:
                toks.append(wr[k])
        for k in o["w"]:
            if k[0] != "p":
                toks += rd.get(k, {}).values()
        best = {}
        for tok in toks:
            if tok[0] not in best or best[tok[0]][1] < tok[1]:
                best[tok[0]] = tok
        for s in sorted(best, key=lambda s: -len(best[s][2])):
            need(q, best[s])
        ins = o["f"](eng[q])
        if o["kind"] == "c":
            ins.then_inc(T.sem["c" + q], 1)
            count[q] += 1
            tok = ("c" + q, count[q], dict(clock[q]))
        elif o["kind"] == "d":
            tok = (o["sem"], o["n"], dict(clock[q]))
        else:
            tok = (o["sem"], o["n"], {})
        for k in keys:
            if k[0] == "p":
                bank.setdefault(k, {})[q] = tok
        for k in o["r"]:
            if k[0] != "p" and o["kind"] != "r":
                rd.setdefault(k, {})[q] = tok
        for k in o["w"]:
            if k[0] != "p":
                wr[k] = tok
                rd[k] = {}
    g.sync.wait_ge(T.sem.dy, 32)
    g.wait_ge(T.sem.loc, sent[0])
    for q in "VSPG":
        g.wait_ge(T.sem["c" + q], count[q])
